import numpy as np
import ml_dtypes


def mxq(x, axis, fmt="e4m3"):
    dtype, down = {"e4m3": (ml_dtypes.float8_e4m3fn, 7), "e5m2": (ml_dtypes.float8_e5m2, 14)}[fmt]
    v = np.moveaxis(np.asarray(x, np.float32).astype(ml_dtypes.bfloat16).astype(np.float64), axis, -1)
    blocks = v.reshape(v.shape[:-1] + (-1, 32))
    amax = np.abs(blocks).max(-1, keepdims=True)
    byte = np.maximum(np.where(amax > 0, np.frexp(amax)[1] - 1 + 127, 0) - down, 1)
    scale = np.exp2(byte - 127.0)
    codes = (blocks / scale).astype(np.float32).astype(dtype).astype(np.float64)
    return np.moveaxis((codes * scale).reshape(v.shape), -1, axis)


WIDE = False


def mx_kscale(k):
    if not WIDE:
        return np.ones(k)
    levels = np.array([10, -10, 5, -5, 0])
    if k % 512:
        return np.exp2(np.random.permutation(np.resize(levels, k // 32))).repeat(32)
    a = np.empty((k // 512, 16))
    for p in range(k // 512):
        a[p, :8] = np.random.permutation(np.resize(levels, 8))
        for g in range(8):
            far = levels[np.abs(levels - a[p, g]) >= 10]
            a[p, g + 8] = far[np.random.randint(len(far))]
    return np.exp2(a.ravel()).repeat(32)


def f64(x):
    return np.asarray(x).astype(np.float64)


def striped(idx):
    return np.tile(idx.reshape(-1, 16).T, (8, 1)).astype(np.uint16)


def unstriped(offs):
    return offs[:16].T.reshape(-1).astype(np.int64)


E2M1 = np.array([0.0, 0.5, 1.0, 1.5, 2.0, 3.0, 4.0, 6.0, -0.0, -0.5, -1.0, -1.5, -2.0, -3.0, -4.0, -6.0])


def pack_weight(w, fmt):
    k, n = w.shape
    w = f64(np.asarray(w, np.float32).astype(ml_dtypes.bfloat16)).reshape(k // 32, 32, n)
    amax = np.abs(w).max(1)
    if fmt == "e4m3":
        byte = np.frexp(amax)[1] - 1 + 127 - 7
    else:
        mant, ex = np.frexp(amax / 6.0)
        byte = np.where(mant > 0.5, ex, ex - 1) + 127
    byte = np.clip(np.where(amax > 0, byte, 1), 1, 254)
    scaled = (w * np.exp2(127.0 - byte)[:, None, :]).reshape(k, n).astype(np.float32)
    by_word = np.ascontiguousarray(scaled.reshape(k // 512, 128, 4, n).transpose(0, 1, 3, 2))
    if fmt == "e4m3":
        words = by_word.astype(ml_dtypes.float8_e4m3fn).view(np.uint8)
    else:
        c = by_word.astype(ml_dtypes.float4_e2m1fn).view(np.uint8) & 0xF
        words = (c[..., 0::2] | (c[..., 1::2] << 4)).reshape(k // 512, 128, 2 * n)
    return np.ascontiguousarray(words), np.ascontiguousarray(byte.astype(np.uint8).reshape(k // 512, 16, n))


def unpack_weight(words, scales, fmt):
    g, _, n = scales.shape
    words = np.ascontiguousarray(words).reshape(g, 128, n, -1)
    if fmt == "e4m3":
        vals = words.view(ml_dtypes.float8_e4m3fn).astype(np.float64)
    else:
        nib = np.empty((g, 128, n, 4), np.uint8)
        nib[..., 0::2] = words & 0xF
        nib[..., 1::2] = words >> 4
        vals = E2M1[nib]
    vals = vals * np.repeat(np.exp2(scales.astype(np.float64) - 127.0), 8, axis=1)[..., None]
    return vals.transpose(0, 1, 3, 2).reshape(g * 512, n)


def gelu(v):
    return 0.5 * v * (1.0 + np.tanh(np.sqrt(2.0 / np.pi) * (v + 0.044715 * v**3)))


K, T, S, P, H, N = 1024, 2048, 1024, 512, 1024, 512

def setup_inputs():
    n = np.random.standard_normal
    s = mx_kscale(K)[:, None]
    u = mx_kscale(H)[:, None]
    tab_words, tab_scales = pack_weight(n((K, T)) * s, "e4m3")
    w1 = (n((K, H)) / np.sqrt(K) / s).astype(np.float32)
    gain = (np.exp(0.3 * n(H)) * u[:, 0]).astype(np.float32)
    w2_words, w2_scales = pack_weight(n((H, N)) / np.sqrt(H) / u, "e2m1")
    w3_words, w3_scales = pack_weight(n((H, N)) / np.sqrt(H) / u, "e4m3")
    w4 = (n((H, N)) / np.sqrt(H) / u).astype(np.float32)
    offs = striped(np.random.permutation(T)[:S])
    sites = np.random.permutation(S)
    pos1 = striped(sites[:P])
    pos2 = striped(sites[P:])
    return {"tab_words": tab_words, "tab_scales": tab_scales, "offs": offs, "w1": w1, "gain": gain,
            "pos1": pos1, "pos2": pos2, "w2_words": w2_words, "w2_scales": w2_scales,
            "w3_words": w3_words, "w3_scales": w3_scales, "w4": w4}

def reference(tab_words, tab_scales, offs, w1, gain, pos1, pos2, w2_words, w2_scales, w3_words, w3_scales, w4):
    v = unpack_weight(tab_words, tab_scales, "e4m3")[:, unstriped(offs)]
    w1q = mxq(f64(w1), 0, "e4m3")
    h = np.tanh(w1q.T @ v)
    a = h[:, unstriped(pos1)]
    b = h[:, unstriped(pos2)]
    z = f64(gain)[:, None] * (a - b)
    zq = mxq(z, 0, "e4m3")
    w2 = unpack_weight(w2_words, w2_scales, "e2m1")
    w3 = unpack_weight(w3_words, w3_scales, "e4m3")
    w4q = mxq(f64(w4), 0, "e4m3")
    y2 = w2.T @ zq
    y3 = w3.T @ zq
    y4 = w4q.T @ zq
    return y2 * y3 + y4

@@ -1,0 +1,287 @@
+from contextlib import ExitStack
+
+import concourse.mybir as mybir
+
+K, T, S, PAIRS, H, N = 1024, 2048, 1024, 512, 1024, 512
+FLOPS = 2 * K * H * S + 3 * 2 * H * N * PAIRS
+
+F32 = mybir.dt.float32
+BF16 = mybir.dt.bfloat16
+I32 = mybir.dt.int32
+U32 = mybir.dt.uint32
+U16 = mybir.dt.uint16
+U8 = mybir.dt.uint8
+FP8X4 = mybir.dt.float8_e4m3fn_x4
+FP4X4 = mybir.dt.float4_e2m1fn_x4
+MULT = mybir.AluOpType.mult
+ADD = mybir.AluOpType.add
+SUB = mybir.AluOpType.subtract
+TANH = mybir.ActivationFunctionType.Tanh
+
+P = 128
+PACK = 4
+KP = P * PACK
+BANK = 512
+CH = 128
+
+
+def tile_list_site_pair_couplings_kernel(
+    tc, tab_words, tab_scales, offs, w1, gain, pos1, pos2, w2_words, w2_scales, w3_words, w3_scales, w4, out
+):
+    nc = tc.nc
+    with ExitStack() as ctx:
+        keep = ctx.enter_context(tc.tile_pool(name="keep", bufs=1))
+        psum = ctx.enter_context(tc.psum_pool(name="psum", bufs=8))
+
+        def sb(name, shape, dtype):
+            return keep.tile(shape, dtype, name=name, align_bytes=64)
+
+        offs_sb = sb("offs_sb", [P, S // 16], U16)
+        pos_sb = [sb("pos1_sb", [P, PAIRS // 16], U16), sb("pos2_sb", [P, PAIRS // 16], U16)]
+        tab = [sb("tab%d" % a, [P, T], I32) for a in range(2)]
+        tab_sc = sb("tab_sc", [P, T], U8)
+        v = [sb("v%d" % a, [P, S], U32) for a in range(2)]
+        v_sc = sb("v_sc", [P, S], U8)
+        gain_sb = sb("gain_sb", [P, 2, PACK], F32)
+        gain_w = [512, 256]
+        gain_pl = [sb("gain_pl%d" % b, [P, PACK, gain_w[b]], F32) for b in range(2)]
+        warm = sb("warm", [P, 8], F32)
+        w23_sc = sb("w23_sc", [P, 2, N], U8)
+        w2_sb = sb("w2_sb", [P, 2, 2 * N], U8)
+        w3_sb = sb("w3_sb", [P, 2, N], I32)
+
+        nc.vector.memset(tab_sc[:].bitcast(I32), 0)
+        nc.vector.memset(w23_sc[:].bitcast(I32), 0)
+        nc.vector.memset(warm[:], 0.0)
+        nc.scalar.activation(out=warm[:, 0:1], in_=warm[:, 1:2], func=TANH)
+
+        def load_tab(a):
+            nc.sync.dma_start(out=tab[a][:], in_=tab_words[a].rearrange("p t i -> p (t i)").bitcast(I32))
+
+        w1_raw, w1_bf, w1_q, w1_sc = {}, {}, {}, {}
+        for a in range(2):
+            for b in range(2):
+                w1_bf[a, b] = sb("w1_bf%d%d" % (a, b), [P, PACK, P, PACK], BF16)
+                w1_q[a, b] = sb("w1_q%d%d" % (a, b), [P, KP], U32)
+                w1_sc[a, b] = sb("w1_sc%d%d" % (a, b), [P, KP], U8)
+
+        def load_w1(a, b, half, halves):
+            width = KP // halves
+            raw = sb("w1_raw%d%d%d" % (a, b, half), [P, PACK, width], F32)
+            w1_raw[a, b, half] = raw
+            c0 = KP * b + width * half
+            nc.sync.dma_start(
+                out=raw[:], in_=w1[KP * a : KP * (a + 1), c0 : c0 + width].rearrange("(p j) c -> p j c", j=PACK)
+            )
+
+        def round_w1(a, b, half, halves, copy):
+            m = P // halves
+            dst = w1_bf[a, b][:, :, m * half : m * (half + 1), :].rearrange("p t m j -> p m j t")
+            copy(out=dst, in_=w1_raw[a, b, half][:].rearrange("p j (m t) -> p m j t", t=PACK))
+
+        def quant_w1(a, b, t0, t1):
+            cols = slice(P * t0, P * t1)
+            nc.vector.quantize_mx(
+                out=w1_q[a, b][:, cols].bitcast(FP8X4),
+                scales=w1_sc[a, b][:, cols],
+                in_=w1_bf[a, b][:, t0:t1].rearrange("p t m j -> p (t m j)"),
+            )
+
+        load_tab(0)
+        nc.sync.dma_start(offs_sb[:], offs)
+        for q in range(4):
+            nc.sync.dma_start(
+                out=tab_sc[32 * q : 32 * q + 8, :].bitcast(I32), in_=tab_scales[:, 4 * q : 4 * q + 4, :].bitcast(I32)
+            )
+        nc.sync.dma_start(out=gain_sb[:], in_=gain.rearrange("(b p t) -> p b t", b=2, t=PACK))
+        load_w1(0, 0, 0, 1)
+        load_tab(1)
+        load_w1(1, 0, 0, 2)
+        load_w1(1, 0, 1, 2)
+        nc.sync.dma_start(pos_sb[0][:], pos1)
+        nc.sync.dma_start(pos_sb[1][:], pos2)
+        load_w1(0, 1, 0, 1)
+        load_w1(1, 1, 0, 1)
+        w4_raw = [sb("w4_raw%d" % b, [P, PACK, N], F32) for b in range(2)]
+        for b in range(2):
+            nc.sync.dma_start(out=w4_raw[b][:], in_=w4[KP * b : KP * (b + 1), :].rearrange("(p j) c -> p j c", j=PACK))
+        for q in range(4):
+            for row, scales in ((0, w2_scales), (4, w3_scales)):
+                nc.sync.dma_start(
+                    out=w23_sc[32 * q + row : 32 * q + row + 4].bitcast(I32),
+                    in_=scales[:, 4 * q : 4 * q + 4, :].rearrange("b r n -> r b n").bitcast(I32),
+                )
+        nc.sync.dma_start(out=w2_sb[:].bitcast(I32), in_=w2_words.rearrange("b p n -> p b n").bitcast(I32))
+        nc.sync.dma_start(out=w3_sb[:], in_=w3_words.rearrange("b p n i -> p b (n i)").bitcast(I32))
+
+        def gather_words(a):
+            nc.vector.tensor_copy(v[a][:], tab[a][:].bitcast(U32).indirect(offs_sb[:]))
+
+        for b in range(2):
+            nc.scalar.copy(
+                out=gain_pl[b][:], in_=gain_sb[:, b, :].unsqueeze(2).to_broadcast([P, PACK, gain_w[b]])
+            )
+        gather_words(0)
+        nc.vector.tensor_copy(v_sc[:], tab_sc[:].indirect(offs_sb[:]))
+        round_w1(0, 0, 0, 1, nc.scalar.copy)
+        gather_words(1)
+        quant_w1(0, 0, 0, 4)
+        round_w1(1, 0, 0, 2, nc.scalar.copy)
+        round_w1(1, 0, 1, 2, nc.vector.tensor_copy)
+        quant_w1(1, 0, 0, 1)
+        quant_w1(1, 0, 1, 2)
+        quant_w1(1, 0, 2, 4)
+
+        h = {}
+
+        def embed(b, t):
+            h[b, t] = sb("h%d%d" % (b, t), [P, S], F32)
+            cols = slice(P * t, P * (t + 1))
+            for half in range(2):
+                js = slice(BANK * half, BANK * (half + 1))
+                acc = psum.tile([P, BANK], F32, name="acc")
+                for a in range(2):
+                    nc.tensor.matmul_mx(
+                        out=acc[:],
+                        lhsT=w1_q[a, b][:, cols].bitcast(FP8X4),
+                        lhsT_scale=w1_sc[a, b][:, cols],
+                        rhs=v[a][:, js].bitcast(FP8X4),
+                        rhs_scale=v_sc[4 * a :, js],
+                        start=(a == 0),
+                        stop=(a == 1),
+                    )
+                nc.scalar.activation(out=h[b, t][:, js], in_=acc[:], func=TANH)
+
+        z_q = [sb("z_q%d" % b, [P, PAIRS], U32) for b in range(2)]
+        z_sc = [sb("z_sc%d" % b, [P, PAIRS], U8) for b in range(2)]
+        picked, z_bf = {}, {}
+
+        def pick(b, t, c0, c1):
+            if (b, c0) not in picked:
+                picked[b, c0] = [sb("pick%d_%d_%d" % (b, c0, s), [P, PACK, c1 - c0], F32) for s in range(2)]
+            for s in range(2):
+                nc.vector.tensor_tensor(
+                    picked[b, c0][s][:, t, :],
+                    h[b, t][:].indirect(pos_sb[s][:, c0 // 16 : c1 // 16]),
+                    gain_pl[b][:, t, 0 : c1 - c0],
+                    MULT,
+                )
+
+        def diff(b, c0, c1):
+            z_bf[b, c0] = sb("z_bf%d_%d" % (b, c0), [P, c1 - c0, PACK], BF16)
+            first, second = [x[:].rearrange("p t (c i) -> p c t i", i=4) for x in picked[b, c0]]
+            nc.vector.tensor_tensor(z_bf[b, c0][:].rearrange("p (c i) t -> p c t i", i=4), first, second, SUB)
+
+        def quant_z(b, c0, c1):
+            nc.vector.quantize_mx(
+                out=z_q[b][:, c0:c1].bitcast(FP8X4),
+                scales=z_sc[b][:, c0:c1],
+                in_=z_bf[b, c0][:].rearrange("p c t -> p (c t)"),
+            )
+
+        w4_bf = [sb("w4_bf%d" % b, [P, N, PACK], BF16) for b in range(2)]
+        w4_q = [sb("w4_q%d" % b, [P, N], U32) for b in range(2)]
+        w4_sc = [sb("w4_sc%d" % b, [P, N], U8) for b in range(2)]
+
+        def round_w4(b):
+            nc.scalar.copy(
+                out=w4_bf[b][:].rearrange("p (c i) j -> p c j i", i=4),
+                in_=w4_raw[b][:].rearrange("p j (c i) -> p c j i", i=4),
+            )
+
+        def quant_w4(b):
+            nc.vector.quantize_mx(
+                out=w4_q[b][:].bitcast(FP8X4), scales=w4_sc[b][:], in_=w4_bf[b][:].rearrange("p c j -> p (c j)")
+            )
+
+        def weights(which, b, nt):
+            cols = slice(P * nt, P * (nt + 1))
+            if which == 2:
+                return w2_sb[:, b, 2 * P * nt : 2 * P * (nt + 1)].bitcast(FP4X4), w23_sc[:, b, cols]
+            if which == 3:
+                return w3_sb[:, b, cols].bitcast(FP8X4), w23_sc[4:, b, cols]
+            return w4_q[b][:, cols].bitcast(FP8X4), w4_sc[b][:, cols]
+
+        y, y2_sb, prod = {}, {}, {}
+
+        def products(c):
+            cols = slice(CH * c, CH * (c + 1))
+            for which in (2, 3, 4):
+                acc = psum.tile([P, BANK], F32, name="acc")
+                y[c, which] = acc
+                for nt in range(4):
+                    for b in range(2):
+                        codes, scales = weights(which, b, nt)
+                        nc.tensor.matmul_mx(
+                            out=acc[:, CH * nt : CH * (nt + 1)],
+                            lhsT=codes,
+                            lhsT_scale=scales,
+                            rhs=z_q[b][:, cols].bitcast(FP8X4),
+                            rhs_scale=z_sc[b][:, cols],
+                            start=(b == 0),
+                            stop=(b == 1),
+                        )
+                if which == 2:
+                    y2_sb[c] = sb("y2_sb%d" % c, [P, BANK], F32)
+                    nc.scalar.copy(out=y2_sb[c][:], in_=acc[:])
+
+        def multiply(c):
+            prod[c] = sb("prod%d" % c, [P, BANK], F32)
+            nc.vector.tensor_tensor(prod[c][:], y[c, 3][:], y2_sb[c][:], MULT)
+
+        def finish(c):
+            res = sb("res%d" % c, [P, BANK], F32)
+            nc.vector.tensor_tensor(res[:], y[c, 4][:], prod[c][:], ADD)
+            nc.sync.dma_start(
+                out=out[:, CH * c : CH * (c + 1)].rearrange("(nt p) c -> p nt c", p=P),
+                in_=res[:].rearrange("p (nt c) -> p nt c", c=CH),
+            )
+
+        embed(0, 0)
+        embed(0, 1)
+        round_w1(0, 1, 0, 1, nc.scalar.copy)
+        pick(0, 0, 0, 512)
+        embed(0, 2)
+        round_w1(1, 1, 0, 1, nc.scalar.copy)
+        pick(0, 1, 0, 512)
+        quant_w1(0, 1, 0, 4)
+        embed(0, 3)
+        pick(0, 2, 0, 512)
+        quant_w1(1, 1, 0, 4)
+        for t in range(4):
+            embed(1, t)
+        pick(0, 3, 0, 512)
+        round_w4(0)
+        round_w4(1)
+        diff(0, 0, 512)
+        pick(1, 0, 0, 256)
+        quant_z(0, 0, 512)
+        for t in range(1, 4):
+            pick(1, t, 0, 256)
+        quant_w4(0)
+        diff(1, 0, 256)
+        quant_w4(1)
+        pick(1, 0, 256, 384)
+        quant_z(1, 0, 256)
+        products(0)
+        products(1)
+        for t in range(1, 4):
+            pick(1, t, 256, 384)
+        diff(1, 256, 384)
+        pick(1, 0, 384, 512)
+        quant_z(1, 256, 384)
+        multiply(0)
+        pick(1, 1, 384, 512)
+        finish(0)
+        products(2)
+        pick(1, 2, 384, 512)
+        pick(1, 3, 384, 512)
+        diff(1, 384, 512)
+        multiply(1)
+        quant_z(1, 384, 512)
+        finish(1)
+        products(3)
+        multiply(2)
+        finish(2)
+        multiply(3)
+        finish(3)

@@ -33,8 +33,8 @@ def tile_list_site_pair_couplings_kernel(
         keep = ctx.enter_context(tc.tile_pool(name="keep", bufs=1))
         psum = ctx.enter_context(tc.psum_pool(name="psum", bufs=8))
 
-        def sb(name, shape, dtype):
-            return keep.tile(shape, dtype, name=name, align_bytes=64)
+        def sb(name, shape, dtype, tag=""):
+            return keep.tile(shape, dtype, name=name, tag=tag or name, align_bytes=64)
 
         offs_sb = sb("offs_sb", [P, S // 16], U16)
         pos_sb = [sb("pos1_sb", [P, PAIRS // 16], U16), sb("pos2_sb", [P, PAIRS // 16], U16)]
@@ -87,14 +87,15 @@ def tile_list_site_pair_couplings_kernel(
                 in_=w1_bf[a, b][:, t0:t1].rearrange("p t m j -> p (t m j)"),
             )
 
-        load_tab(0)
         nc.sync.dma_start(offs_sb[:], offs)
         for q in range(4):
             nc.sync.dma_start(
                 out=tab_sc[32 * q : 32 * q + 8, :].bitcast(I32), in_=tab_scales[:, 4 * q : 4 * q + 4, :].bitcast(I32)
             )
         nc.sync.dma_start(out=gain_sb[:], in_=gain.rearrange("(b p t) -> p b t", b=2, t=PACK))
-        load_w1(0, 0, 0, 1)
+        load_tab(0)
+        load_w1(0, 0, 0, 2)
+        load_w1(0, 0, 1, 2)
         load_tab(1)
         load_w1(1, 0, 0, 2)
         load_w1(1, 0, 1, 2)
@@ -121,11 +122,12 @@ def tile_list_site_pair_couplings_kernel(
             nc.scalar.copy(
                 out=gain_pl[b][:], in_=gain_sb[:, b, :].unsqueeze(2).to_broadcast([P, PACK, gain_w[b]])
             )
-        gather_words(0)
         nc.vector.tensor_copy(v_sc[:], tab_sc[:].indirect(offs_sb[:]))
-        round_w1(0, 0, 0, 1, nc.scalar.copy)
-        gather_words(1)
+        gather_words(0)
+        round_w1(0, 0, 0, 2, nc.scalar.copy)
+        round_w1(0, 0, 1, 2, nc.vector.tensor_copy)
         quant_w1(0, 0, 0, 4)
+        gather_words(1)
         round_w1(1, 0, 0, 2, nc.scalar.copy)
         round_w1(1, 0, 1, 2, nc.vector.tensor_copy)
         quant_w1(1, 0, 0, 1)
@@ -158,7 +160,10 @@ def tile_list_site_pair_couplings_kernel(
 
         def pick(b, t, c0, c1):
             if (b, c0) not in picked:
-                picked[b, c0] = [sb("pick%d_%d_%d" % (b, c0, s), [P, PACK, c1 - c0], F32) for s in range(2)]
+                picked[b, c0] = [
+                    sb("pick%d_%d_%d" % (b, c0, s), [P, PACK, c1 - c0], F32, "y2_sb0" if (c0, s) == (384, 0) else "")
+                    for s in range(2)
+                ]
             for s in range(2):
                 nc.vector.tensor_tensor(
                     picked[b, c0][s][:, t, :],
@@ -168,7 +173,7 @@ def tile_list_site_pair_couplings_kernel(
                 )
 
         def diff(b, c0, c1):
-            z_bf[b, c0] = sb("z_bf%d_%d" % (b, c0), [P, c1 - c0, PACK], BF16)
+            z_bf[b, c0] = sb("z_bf%d_%d" % (b, c0), [P, c1 - c0, PACK], BF16, "w1_bf11" if b == 0 else "")
             first, second = [x[:].rearrange("p t (c i) -> p c t i", i=4) for x in picked[b, c0]]
             nc.vector.tensor_tensor(z_bf[b, c0][:].rearrange("p (c i) t -> p c t i", i=4), first, second, SUB)
 
@@ -204,9 +209,9 @@ def tile_list_site_pair_couplings_kernel(
 
         y, y2_sb, prod = {}, {}, {}
 
-        def products(c):
+        def products(c, whiches):
             cols = slice(CH * c, CH * (c + 1))
-            for which in (2, 3, 4):
+            for which in whiches:
                 acc = psum.tile([P, BANK], F32, name="acc")
                 y[c, which] = acc
                 for nt in range(4):
@@ -237,20 +242,17 @@ def tile_list_site_pair_couplings_kernel(
                 in_=res[:].rearrange("p (nt c) -> p nt c", c=CH),
             )
 
-        embed(0, 0)
-        embed(0, 1)
+        for t in range(4):
+            embed(0, t)
         round_w1(0, 1, 0, 1, nc.scalar.copy)
-        pick(0, 0, 0, 512)
-        embed(0, 2)
         round_w1(1, 1, 0, 1, nc.scalar.copy)
-        pick(0, 1, 0, 512)
+        for t in range(3):
+            pick(0, t, 0, 512)
         quant_w1(0, 1, 0, 4)
-        embed(0, 3)
-        pick(0, 2, 0, 512)
+        pick(0, 3, 0, 512)
         quant_w1(1, 1, 0, 4)
         for t in range(4):
             embed(1, t)
-        pick(0, 3, 0, 512)
         round_w4(0)
         round_w4(1)
         diff(0, 0, 512)
@@ -258,29 +260,31 @@ def tile_list_site_pair_couplings_kernel(
         quant_z(0, 0, 512)
         for t in range(1, 4):
             pick(1, t, 0, 256)
-        quant_w4(0)
         diff(1, 0, 256)
-        quant_w4(1)
         pick(1, 0, 256, 384)
         quant_z(1, 0, 256)
-        products(0)
-        products(1)
+        products(0, (2, 3))
+        products(1, (2, 3))
         for t in range(1, 4):
             pick(1, t, 256, 384)
+        quant_w4(0)
         diff(1, 256, 384)
-        pick(1, 0, 384, 512)
+        quant_w4(1)
         quant_z(1, 256, 384)
+        products(0, (4,))
+        products(1, (4,))
+        products(2, (2, 3, 4))
         multiply(0)
+        pick(1, 0, 384, 512)
         pick(1, 1, 384, 512)
         finish(0)
-        products(2)
         pick(1, 2, 384, 512)
         pick(1, 3, 384, 512)
         diff(1, 384, 512)
         multiply(1)
         quant_z(1, 384, 512)
+        products(3, (2, 3, 4))
         finish(1)
-        products(3)
         multiply(2)
         finish(2)
         multiply(3)

@@ -74,10 +74,13 @@ def tile_list_site_pair_couplings_kernel(
                 out=raw[:], in_=w1[KP * a : KP * (a + 1), c0 : c0 + width].rearrange("(p j) c -> p j c", j=PACK)
             )
 
-        def round_w1(a, b, half, halves, copy):
+        def round_w1(a, b, half, halves, copy, part=0, parts=1):
             m = P // halves
-            dst = w1_bf[a, b][:, :, m * half : m * (half + 1), :].rearrange("p t m j -> p m j t")
-            copy(out=dst, in_=w1_raw[a, b, half][:].rearrange("p j (m t) -> p m j t", t=PACK))
+            n = m // parts
+            m0 = m * half + n * part
+            dst = w1_bf[a, b][:, :, m0 : m0 + n, :].rearrange("p t m j -> p m j t")
+            src = w1_raw[a, b, half][:, :, PACK * n * part : PACK * n * (part + 1)]
+            copy(out=dst, in_=src.rearrange("p j (m t) -> p m j t", t=PACK))
 
         def quant_w1(a, b, t0, t1):
             cols = slice(P * t0, P * t1)
@@ -87,13 +90,13 @@ def tile_list_site_pair_couplings_kernel(
                 in_=w1_bf[a, b][:, t0:t1].rearrange("p t m j -> p (t m j)"),
             )
 
+        load_tab(0)
         nc.sync.dma_start(offs_sb[:], offs)
         for q in range(4):
             nc.sync.dma_start(
                 out=tab_sc[32 * q : 32 * q + 8, :].bitcast(I32), in_=tab_scales[:, 4 * q : 4 * q + 4, :].bitcast(I32)
             )
         nc.sync.dma_start(out=gain_sb[:], in_=gain.rearrange("(b p t) -> p b t", b=2, t=PACK))
-        load_tab(0)
         load_w1(0, 0, 0, 2)
         load_w1(0, 0, 1, 2)
         load_tab(1)
@@ -101,7 +104,8 @@ def tile_list_site_pair_couplings_kernel(
         load_w1(1, 0, 1, 2)
         nc.sync.dma_start(pos_sb[0][:], pos1)
         nc.sync.dma_start(pos_sb[1][:], pos2)
-        load_w1(0, 1, 0, 1)
+        load_w1(0, 1, 0, 2)
+        load_w1(0, 1, 1, 2)
         load_w1(1, 1, 0, 1)
         w4_raw = [sb("w4_raw%d" % b, [P, PACK, N], F32) for b in range(2)]
         for b in range(2):
@@ -122,14 +126,15 @@ def tile_list_site_pair_couplings_kernel(
             nc.scalar.copy(
                 out=gain_pl[b][:], in_=gain_sb[:, b, :].unsqueeze(2).to_broadcast([P, PACK, gain_w[b]])
             )
-        nc.vector.tensor_copy(v_sc[:], tab_sc[:].indirect(offs_sb[:]))
         gather_words(0)
+        nc.vector.tensor_copy(v_sc[:], tab_sc[:].indirect(offs_sb[:]))
         round_w1(0, 0, 0, 2, nc.scalar.copy)
-        round_w1(0, 0, 1, 2, nc.vector.tensor_copy)
+        round_w1(0, 0, 1, 2, nc.scalar.copy)
         quant_w1(0, 0, 0, 4)
         gather_words(1)
         round_w1(1, 0, 0, 2, nc.scalar.copy)
-        round_w1(1, 0, 1, 2, nc.vector.tensor_copy)
+        round_w1(1, 0, 1, 2, nc.scalar.copy, 0, 2)
+        round_w1(1, 0, 1, 2, nc.vector.tensor_copy, 1, 2)
         quant_w1(1, 0, 0, 1)
         quant_w1(1, 0, 1, 2)
         quant_w1(1, 0, 2, 4)
@@ -137,7 +142,7 @@ def tile_list_site_pair_couplings_kernel(
         h = {}
 
         def embed(b, t):
-            h[b, t] = sb("h%d%d" % (b, t), [P, S], F32)
+            h[b, t] = sb("h%d%d" % (b, t), [P, S], F32, "w1_raw110" if (b, t) == (0, 2) else "")
             cols = slice(P * t, P * (t + 1))
             for half in range(2):
                 js = slice(BANK * half, BANK * (half + 1))
@@ -158,10 +163,12 @@ def tile_list_site_pair_couplings_kernel(
         z_sc = [sb("z_sc%d" % b, [P, PAIRS], U8) for b in range(2)]
         picked, z_bf = {}, {}
 
+        reuse = {(0, 0, 0): "w1_raw010", (1, 384, 0): "y2_sb0"}
+
         def pick(b, t, c0, c1):
             if (b, c0) not in picked:
                 picked[b, c0] = [
-                    sb("pick%d_%d_%d" % (b, c0, s), [P, PACK, c1 - c0], F32, "y2_sb0" if (c0, s) == (384, 0) else "")
+                    sb("pick%d_%d_%d" % (b, c0, s), [P, PACK, c1 - c0], F32, reuse.get((b, c0, s), ""))
                     for s in range(2)
                 ]
             for s in range(2):
@@ -174,8 +181,8 @@ def tile_list_site_pair_couplings_kernel(
 
         def diff(b, c0, c1):
             z_bf[b, c0] = sb("z_bf%d_%d" % (b, c0), [P, c1 - c0, PACK], BF16, "w1_bf11" if b == 0 else "")
-            first, second = [x[:].rearrange("p t (c i) -> p c t i", i=4) for x in picked[b, c0]]
-            nc.vector.tensor_tensor(z_bf[b, c0][:].rearrange("p (c i) t -> p c t i", i=4), first, second, SUB)
+            first, second = [x[:].rearrange("p t (c i) -> p c t i", i=2) for x in picked[b, c0]]
+            nc.vector.tensor_tensor(z_bf[b, c0][:].rearrange("p (c i) t -> p c t i", i=2), first, second, SUB)
 
         def quant_z(b, c0, c1):
             nc.vector.quantize_mx(
@@ -242,31 +249,35 @@ def tile_list_site_pair_couplings_kernel(
                 in_=res[:].rearrange("p (nt c) -> p nt c", c=CH),
             )
 
-        for t in range(4):
-            embed(0, t)
-        round_w1(0, 1, 0, 1, nc.scalar.copy)
+        round_w1(0, 1, 0, 2, nc.vector.tensor_copy)
+        embed(0, 0)
+        embed(0, 1)
+        round_w1(0, 1, 1, 2, nc.scalar.copy)
         round_w1(1, 1, 0, 1, nc.scalar.copy)
-        for t in range(3):
+        embed(0, 2)
+        embed(0, 3)
+        for t in range(4):
             pick(0, t, 0, 512)
-        quant_w1(0, 1, 0, 4)
-        pick(0, 3, 0, 512)
-        quant_w1(1, 1, 0, 4)
+            if t < 2:
+                quant_w1(t, 1, 0, 4)
         for t in range(4):
             embed(1, t)
         round_w4(0)
         round_w4(1)
-        diff(0, 0, 512)
         pick(1, 0, 0, 256)
+        diff(0, 0, 512)
+        pick(1, 1, 0, 256)
         quant_z(0, 0, 512)
-        for t in range(1, 4):
-            pick(1, t, 0, 256)
-        diff(1, 0, 256)
+        pick(1, 2, 0, 256)
+        pick(1, 3, 0, 256)
         pick(1, 0, 256, 384)
+        diff(1, 0, 256)
+        pick(1, 1, 256, 384)
         quant_z(1, 0, 256)
         products(0, (2, 3))
         products(1, (2, 3))
-        for t in range(1, 4):
-            pick(1, t, 256, 384)
+        pick(1, 2, 256, 384)
+        pick(1, 3, 256, 384)
         quant_w4(0)
         diff(1, 256, 384)
         quant_w4(1)
@@ -275,17 +286,14 @@ def tile_list_site_pair_couplings_kernel(
         products(1, (4,))
         products(2, (2, 3, 4))
         multiply(0)
-        pick(1, 0, 384, 512)
-        pick(1, 1, 384, 512)
-        finish(0)
-        pick(1, 2, 384, 512)
-        pick(1, 3, 384, 512)
-        diff(1, 384, 512)
+        for t in range(4):
+            pick(1, t, 384, 512)
         multiply(1)
+        diff(1, 384, 512)
+        multiply(2)
         quant_z(1, 384, 512)
         products(3, (2, 3, 4))
-        finish(1)
-        multiply(2)
-        finish(2)
+        for c in range(3):
+            finish(c)
         multiply(3)
         finish(3)

@@ -20,9 +20,19 @@ TANH = mybir.ActivationFunctionType.Tanh
 
 P = 128
 PACK = 4
-KP = P * PACK
+PASS = P * PACK
+PASSES = 2
 BANK = 512
-CH = 128
+BANKS = 8
+GROUP = 16
+QUADRANT = 32
+SCALE_ROWS = 4
+CHUNK = 128
+ROW_TILES = N // P
+
+ALL = (0, PAIRS)
+FIRST, SECOND, LAST = (0, 256), (256, 384), (384, PAIRS)
+WIDEST_RUN = (PAIRS, 256)
 
 
 def tile_list_site_pair_couplings_kernel(
@@ -31,58 +41,53 @@ def tile_list_site_pair_couplings_kernel(
     nc = tc.nc
     with ExitStack() as ctx:
         keep = ctx.enter_context(tc.tile_pool(name="keep", bufs=1))
-        psum = ctx.enter_context(tc.psum_pool(name="psum", bufs=8))
+        psum = ctx.enter_context(tc.psum_pool(name="psum", bufs=BANKS))
 
         def sb(name, shape, dtype, tag=""):
             return keep.tile(shape, dtype, name=name, tag=tag or name, align_bytes=64)
 
-        offs_sb = sb("offs_sb", [P, S // 16], U16)
-        pos_sb = [sb("pos1_sb", [P, PAIRS // 16], U16), sb("pos2_sb", [P, PAIRS // 16], U16)]
-        tab = [sb("tab%d" % a, [P, T], I32) for a in range(2)]
+        offs_sb = sb("offs_sb", [P, S // GROUP], U16)
+        pos_sb = [sb("pos1_sb", [P, PAIRS // GROUP], U16), sb("pos2_sb", [P, PAIRS // GROUP], U16)]
+        tab = [sb("tab%d" % a, [P, T], I32) for a in range(PASSES)]
         tab_sc = sb("tab_sc", [P, T], U8)
-        v = [sb("v%d" % a, [P, S], U32) for a in range(2)]
+        v = [sb("v%d" % a, [P, S], U32) for a in range(PASSES)]
         v_sc = sb("v_sc", [P, S], U8)
-        gain_sb = sb("gain_sb", [P, 2, PACK], F32)
-        gain_w = [512, 256]
-        gain_pl = [sb("gain_pl%d" % b, [P, PACK, gain_w[b]], F32) for b in range(2)]
-        warm = sb("warm", [P, 8], F32)
-        w23_sc = sb("w23_sc", [P, 2, N], U8)
-        w2_sb = sb("w2_sb", [P, 2, 2 * N], U8)
-        w3_sb = sb("w3_sb", [P, 2, N], I32)
+        gain_sb = sb("gain_sb", [P, PASSES, PACK], F32)
+        gain_rows = [sb("gain_rows%d" % b, [P, PACK, WIDEST_RUN[b]], F32) for b in range(PASSES)]
+        w23_sc = sb("w23_sc", [P, PASSES, N], U8)
+        w2_sb = sb("w2_sb", [P, PASSES, 2 * N], U8)
+        w3_sb = sb("w3_sb", [P, PASSES, N], I32)
 
         nc.vector.memset(tab_sc[:].bitcast(I32), 0)
         nc.vector.memset(w23_sc[:].bitcast(I32), 0)
-        nc.vector.memset(warm[:], 0.0)
-        nc.scalar.activation(out=warm[:, 0:1], in_=warm[:, 1:2], func=TANH)
 
-        def load_tab(a):
-            nc.sync.dma_start(out=tab[a][:], in_=tab_words[a].rearrange("p t i -> p (t i)").bitcast(I32))
-
+        pieces = {(0, 0): 2, (1, 0): 2, (0, 1): 2, (1, 1): 1}
         w1_raw, w1_bf, w1_q, w1_sc = {}, {}, {}, {}
-        for a in range(2):
-            for b in range(2):
+        for a in range(PASSES):
+            for b in range(PASSES):
                 w1_bf[a, b] = sb("w1_bf%d%d" % (a, b), [P, PACK, P, PACK], BF16)
-                w1_q[a, b] = sb("w1_q%d%d" % (a, b), [P, KP], U32)
-                w1_sc[a, b] = sb("w1_sc%d%d" % (a, b), [P, KP], U8)
+                w1_q[a, b] = sb("w1_q%d%d" % (a, b), [P, PASS], U32)
+                w1_sc[a, b] = sb("w1_sc%d%d" % (a, b), [P, PASS], U8)
 
-        def load_w1(a, b, half, halves):
-            width = KP // halves
-            raw = sb("w1_raw%d%d%d" % (a, b, half), [P, PACK, width], F32)
-            w1_raw[a, b, half] = raw
-            c0 = KP * b + width * half
-            nc.sync.dma_start(
-                out=raw[:], in_=w1[KP * a : KP * (a + 1), c0 : c0 + width].rearrange("(p j) c -> p j c", j=PACK)
+        def load_table_words(a):
+            nc.sync.dma_start(out=tab[a][:], in_=tab_words[a].rearrange("p c i -> p (c i)").bitcast(I32))
+
+        def load_w1(a, b):
+            width = PASS // pieces[a, b]
+            for piece in range(pieces[a, b]):
+                w1_raw[a, b, piece] = sb("w1_raw%d%d%d" % (a, b, piece), [P, PACK, width], F32)
+                channel = PASS * b + width * piece
+                rows = w1[PASS * a : PASS * (a + 1), channel : channel + width]
+                nc.sync.dma_start(out=w1_raw[a, b, piece][:], in_=rows.rearrange("(p j) c -> p j c", j=PACK))
+
+        def round_w1(a, b, piece, copy):
+            count = P // pieces[a, b]
+            copy(
+                out=w1_bf[a, b][:, :, count * piece : count * (piece + 1), :].rearrange("p t m j -> p m j t"),
+                in_=w1_raw[a, b, piece][:].rearrange("p j (m t) -> p m j t", t=PACK),
             )
 
-        def round_w1(a, b, half, halves, copy, part=0, parts=1):
-            m = P // halves
-            n = m // parts
-            m0 = m * half + n * part
-            dst = w1_bf[a, b][:, :, m0 : m0 + n, :].rearrange("p t m j -> p m j t")
-            src = w1_raw[a, b, half][:, :, PACK * n * part : PACK * n * (part + 1)]
-            copy(out=dst, in_=src.rearrange("p j (m t) -> p m j t", t=PACK))
-
-        def quant_w1(a, b, t0, t1):
+        def quantize_w1(a, b, t0, t1):
             cols = slice(P * t0, P * t1)
             nc.vector.quantize_mx(
                 out=w1_q[a, b][:, cols].bitcast(FP8X4),
@@ -90,110 +95,92 @@ def tile_list_site_pair_couplings_kernel(
                 in_=w1_bf[a, b][:, t0:t1].rearrange("p t m j -> p (t m j)"),
             )
 
-        load_tab(0)
+        nc.sync.dma_start(out=gain_sb[:], in_=gain.rearrange("(b p t) -> p b t", b=PASSES, t=PACK))
+        load_table_words(0)
         nc.sync.dma_start(offs_sb[:], offs)
-        for q in range(4):
+        for q in range(P // QUADRANT):
             nc.sync.dma_start(
-                out=tab_sc[32 * q : 32 * q + 8, :].bitcast(I32), in_=tab_scales[:, 4 * q : 4 * q + 4, :].bitcast(I32)
+                out=tab_sc[QUADRANT * q : QUADRANT * q + PASSES * SCALE_ROWS, :].bitcast(I32),
+                in_=tab_scales[:, SCALE_ROWS * q : SCALE_ROWS * (q + 1), :].bitcast(I32),
             )
-        nc.sync.dma_start(out=gain_sb[:], in_=gain.rearrange("(b p t) -> p b t", b=2, t=PACK))
-        load_w1(0, 0, 0, 2)
-        load_w1(0, 0, 1, 2)
-        load_tab(1)
-        load_w1(1, 0, 0, 2)
-        load_w1(1, 0, 1, 2)
+        load_w1(0, 0)
+        load_table_words(1)
+        load_w1(1, 0)
         nc.sync.dma_start(pos_sb[0][:], pos1)
         nc.sync.dma_start(pos_sb[1][:], pos2)
-        load_w1(0, 1, 0, 2)
-        load_w1(0, 1, 1, 2)
-        load_w1(1, 1, 0, 1)
-        w4_raw = [sb("w4_raw%d" % b, [P, PACK, N], F32) for b in range(2)]
-        for b in range(2):
-            nc.sync.dma_start(out=w4_raw[b][:], in_=w4[KP * b : KP * (b + 1), :].rearrange("(p j) c -> p j c", j=PACK))
-        for q in range(4):
-            for row, scales in ((0, w2_scales), (4, w3_scales)):
+        load_w1(0, 1)
+        load_w1(1, 1)
+        w4_raw = [sb("w4_raw%d" % b, [P, PACK, N], F32) for b in range(PASSES)]
+        for b in range(PASSES):
+            rows = w4[PASS * b : PASS * (b + 1), :]
+            nc.sync.dma_start(out=w4_raw[b][:], in_=rows.rearrange("(p j) c -> p j c", j=PACK))
+        for q in range(P // QUADRANT):
+            for first_row, scales in ((0, w2_scales), (SCALE_ROWS, w3_scales)):
+                row = QUADRANT * q + first_row
                 nc.sync.dma_start(
-                    out=w23_sc[32 * q + row : 32 * q + row + 4].bitcast(I32),
-                    in_=scales[:, 4 * q : 4 * q + 4, :].rearrange("b r n -> r b n").bitcast(I32),
+                    out=w23_sc[row : row + SCALE_ROWS].bitcast(I32),
+                    in_=scales[:, SCALE_ROWS * q : SCALE_ROWS * (q + 1), :].rearrange("b r n -> r b n").bitcast(I32),
                 )
         nc.sync.dma_start(out=w2_sb[:].bitcast(I32), in_=w2_words.rearrange("b p n -> p b n").bitcast(I32))
         nc.sync.dma_start(out=w3_sb[:], in_=w3_words.rearrange("b p n i -> p b (n i)").bitcast(I32))
 
-        def gather_words(a):
-            nc.vector.tensor_copy(v[a][:], tab[a][:].bitcast(U32).indirect(offs_sb[:]))
-
-        for b in range(2):
-            nc.scalar.copy(
-                out=gain_pl[b][:], in_=gain_sb[:, b, :].unsqueeze(2).to_broadcast([P, PACK, gain_w[b]])
-            )
-        gather_words(0)
-        nc.vector.tensor_copy(v_sc[:], tab_sc[:].indirect(offs_sb[:]))
-        round_w1(0, 0, 0, 2, nc.scalar.copy)
-        round_w1(0, 0, 1, 2, nc.scalar.copy)
-        quant_w1(0, 0, 0, 4)
-        gather_words(1)
-        round_w1(1, 0, 0, 2, nc.scalar.copy)
-        round_w1(1, 0, 1, 2, nc.scalar.copy, 0, 2)
-        round_w1(1, 0, 1, 2, nc.vector.tensor_copy, 1, 2)
-        quant_w1(1, 0, 0, 1)
-        quant_w1(1, 0, 1, 2)
-        quant_w1(1, 0, 2, 4)
-
         h = {}
 
-        def embed(b, t):
-            h[b, t] = sb("h%d%d" % (b, t), [P, S], F32, "w1_raw110" if (b, t) == (0, 2) else "")
+        def gather_table_words(a):
+            nc.vector.tensor_copy(v[a][:], tab[a][:].bitcast(U32).indirect(offs_sb[:]))
+
+        def embed(b, t, tag=""):
+            h[b, t] = sb("h%d%d" % (b, t), [P, S], F32, tag)
             cols = slice(P * t, P * (t + 1))
-            for half in range(2):
-                js = slice(BANK * half, BANK * (half + 1))
+            for site in range(0, S, BANK):
+                sites = slice(site, site + BANK)
                 acc = psum.tile([P, BANK], F32, name="acc")
-                for a in range(2):
+                for a in range(PASSES):
                     nc.tensor.matmul_mx(
                         out=acc[:],
                         lhsT=w1_q[a, b][:, cols].bitcast(FP8X4),
                         lhsT_scale=w1_sc[a, b][:, cols],
-                        rhs=v[a][:, js].bitcast(FP8X4),
-                        rhs_scale=v_sc[4 * a :, js],
+                        rhs=v[a][:, sites].bitcast(FP8X4),
+                        rhs_scale=v_sc[SCALE_ROWS * a :, sites],
                         start=(a == 0),
-                        stop=(a == 1),
+                        stop=(a == PASSES - 1),
                     )
-                nc.scalar.activation(out=h[b, t][:, js], in_=acc[:], func=TANH)
+                nc.scalar.activation(out=h[b, t][:, sites], in_=acc[:], func=TANH)
 
-        z_q = [sb("z_q%d" % b, [P, PAIRS], U32) for b in range(2)]
-        z_sc = [sb("z_sc%d" % b, [P, PAIRS], U8) for b in range(2)]
+        z_q = [sb("z_q%d" % b, [P, PAIRS], U32) for b in range(PASSES)]
+        z_sc = [sb("z_sc%d" % b, [P, PAIRS], U8) for b in range(PASSES)]
         picked, z_bf = {}, {}
 
-        reuse = {(0, 0, 0): "w1_raw010", (1, 384, 0): "y2_sb0"}
+        def new_run(b, run, tag=""):
+            shape = [P, PACK, run[1] - run[0]]
+            picked[b, run] = [sb("pick%d_%d_0" % (b, run[0]), shape, F32, tag), sb("pick%d_%d_1" % (b, run[0]), shape, F32)]
 
-        def pick(b, t, c0, c1):
-            if (b, c0) not in picked:
-                picked[b, c0] = [
-                    sb("pick%d_%d_%d" % (b, c0, s), [P, PACK, c1 - c0], F32, reuse.get((b, c0, s), ""))
-                    for s in range(2)
-                ]
-            for s in range(2):
+        def pick(b, t, run):
+            c0, c1 = run
+            for side in range(2):
                 nc.vector.tensor_tensor(
-                    picked[b, c0][s][:, t, :],
-                    h[b, t][:].indirect(pos_sb[s][:, c0 // 16 : c1 // 16]),
-                    gain_pl[b][:, t, 0 : c1 - c0],
+                    picked[b, run][side][:, t, :],
+                    h[b, t][:].indirect(pos_sb[side][:, c0 // GROUP : c1 // GROUP]),
+                    gain_rows[b][:, t, 0 : c1 - c0],
                     MULT,
                 )
 
-        def diff(b, c0, c1):
-            z_bf[b, c0] = sb("z_bf%d_%d" % (b, c0), [P, c1 - c0, PACK], BF16, "w1_bf11" if b == 0 else "")
-            first, second = [x[:].rearrange("p t (c i) -> p c t i", i=2) for x in picked[b, c0]]
-            nc.vector.tensor_tensor(z_bf[b, c0][:].rearrange("p (c i) t -> p c t i", i=2), first, second, SUB)
+        def subtract(b, run, tag=""):
+            z_bf[b, run] = sb("z_bf%d_%d" % (b, run[0]), [P, run[1] - run[0], PACK], BF16, tag)
+            first, second = [x[:].rearrange("p t (c i) -> p c t i", i=2) for x in picked[b, run]]
+            nc.vector.tensor_tensor(z_bf[b, run][:].rearrange("p (c i) t -> p c t i", i=2), first, second, SUB)
 
-        def quant_z(b, c0, c1):
+        def quantize_z(b, run):
+            cols = slice(run[0], run[1])
             nc.vector.quantize_mx(
-                out=z_q[b][:, c0:c1].bitcast(FP8X4),
-                scales=z_sc[b][:, c0:c1],
-                in_=z_bf[b, c0][:].rearrange("p c t -> p (c t)"),
+                out=z_q[b][:, cols].bitcast(FP8X4),
+                scales=z_sc[b][:, cols],
+                in_=z_bf[b, run][:].rearrange("p c t -> p (c t)"),
             )
 
-        w4_bf = [sb("w4_bf%d" % b, [P, N, PACK], BF16) for b in range(2)]
-        w4_q = [sb("w4_q%d" % b, [P, N], U32) for b in range(2)]
-        w4_sc = [sb("w4_sc%d" % b, [P, N], U8) for b in range(2)]
+        w4_bf = [sb("w4_bf%d" % b, [P, N, PACK], BF16) for b in range(PASSES)]
+        w4_q = [sb("w4_q%d" % b, [P, N], U32) for b in range(PASSES)]
+        w4_sc = [sb("w4_sc%d" % b, [P, N], U8) for b in range(PASSES)]
 
         def round_w4(b):
             nc.scalar.copy(
@@ -201,99 +188,121 @@ def tile_list_site_pair_couplings_kernel(
                 in_=w4_raw[b][:].rearrange("p j (c i) -> p c j i", i=4),
             )
 
-        def quant_w4(b):
+        def quantize_w4(b):
             nc.vector.quantize_mx(
                 out=w4_q[b][:].bitcast(FP8X4), scales=w4_sc[b][:], in_=w4_bf[b][:].rearrange("p c j -> p (c j)")
             )
 
-        def weights(which, b, nt):
-            cols = slice(P * nt, P * (nt + 1))
+        def weights(which, b, tile):
+            cols = slice(P * tile, P * (tile + 1))
             if which == 2:
-                return w2_sb[:, b, 2 * P * nt : 2 * P * (nt + 1)].bitcast(FP4X4), w23_sc[:, b, cols]
+                return w2_sb[:, b, 2 * P * tile : 2 * P * (tile + 1)].bitcast(FP4X4), w23_sc[:, b, cols]
             if which == 3:
-                return w3_sb[:, b, cols].bitcast(FP8X4), w23_sc[4:, b, cols]
+                return w3_sb[:, b, cols].bitcast(FP8X4), w23_sc[SCALE_ROWS:, b, cols]
             return w4_q[b][:, cols].bitcast(FP8X4), w4_sc[b][:, cols]
 
-        y, y2_sb, prod = {}, {}, {}
+        y, y2_sb, y23 = {}, {}, {}
 
-        def products(c, whiches):
-            cols = slice(CH * c, CH * (c + 1))
-            for which in whiches:
-                acc = psum.tile([P, BANK], F32, name="acc")
-                y[c, which] = acc
-                for nt in range(4):
-                    for b in range(2):
-                        codes, scales = weights(which, b, nt)
-                        nc.tensor.matmul_mx(
-                            out=acc[:, CH * nt : CH * (nt + 1)],
-                            lhsT=codes,
-                            lhsT_scale=scales,
-                            rhs=z_q[b][:, cols].bitcast(FP8X4),
-                            rhs_scale=z_sc[b][:, cols],
-                            start=(b == 0),
-                            stop=(b == 1),
-                        )
-                if which == 2:
-                    y2_sb[c] = sb("y2_sb%d" % c, [P, BANK], F32)
-                    nc.scalar.copy(out=y2_sb[c][:], in_=acc[:])
+        def product(chunk, which):
+            cols = slice(CHUNK * chunk, CHUNK * (chunk + 1))
+            acc = psum.tile([P, BANK], F32, name="acc")
+            y[chunk, which] = acc
+            for tile in range(ROW_TILES):
+                for b in range(PASSES):
+                    codes, scales = weights(which, b, tile)
+                    nc.tensor.matmul_mx(
+                        out=acc[:, CHUNK * tile : CHUNK * (tile + 1)],
+                        lhsT=codes,
+                        lhsT_scale=scales,
+                        rhs=z_q[b][:, cols].bitcast(FP8X4),
+                        rhs_scale=z_sc[b][:, cols],
+                        start=(b == 0),
+                        stop=(b == PASSES - 1),
+                    )
+            if which == 2:
+                y2_sb[chunk] = sb("y2_sb%d" % chunk, [P, BANK], F32)
+                nc.scalar.copy(out=y2_sb[chunk][:], in_=acc[:])
 
-        def multiply(c):
-            prod[c] = sb("prod%d" % c, [P, BANK], F32)
-            nc.vector.tensor_tensor(prod[c][:], y[c, 3][:], y2_sb[c][:], MULT)
+        def multiply(chunk):
+            y23[chunk] = sb("y23_%d" % chunk, [P, BANK], F32)
+            nc.vector.tensor_tensor(y23[chunk][:], y[chunk, 3][:], y2_sb[chunk][:], MULT)
 
-        def finish(c):
-            res = sb("res%d" % c, [P, BANK], F32)
-            nc.vector.tensor_tensor(res[:], y[c, 4][:], prod[c][:], ADD)
+        def add_and_store(chunk):
+            result = sb("result%d" % chunk, [P, BANK], F32)
+            nc.vector.tensor_tensor(result[:], y[chunk, 4][:], y23[chunk][:], ADD)
             nc.sync.dma_start(
-                out=out[:, CH * c : CH * (c + 1)].rearrange("(nt p) c -> p nt c", p=P),
-                in_=res[:].rearrange("p (nt c) -> p nt c", c=CH),
+                out=out[:, CHUNK * chunk : CHUNK * (chunk + 1)].rearrange("(tile p) c -> p tile c", p=P),
+                in_=result[:].rearrange("p (tile c) -> p tile c", c=CHUNK),
             )
 
-        round_w1(0, 1, 0, 2, nc.vector.tensor_copy)
+        for b in range(PASSES):
+            spread = gain_sb[:, b, :].unsqueeze(2).to_broadcast([P, PACK, WIDEST_RUN[b]])
+            nc.scalar.copy(out=gain_rows[b][:], in_=spread)
+        gather_table_words(0)
+        nc.vector.tensor_copy(v_sc[:], tab_sc[:].indirect(offs_sb[:]))
+        round_w1(0, 0, 0, nc.scalar.copy)
+        round_w1(0, 0, 1, nc.scalar.copy)
+        quantize_w1(0, 0, 0, PACK)
+        gather_table_words(1)
+        round_w1(1, 0, 0, nc.scalar.copy)
+        round_w1(1, 0, 1, nc.vector.tensor_copy)
+        quantize_w1(1, 0, 0, 1)
+        quantize_w1(1, 0, 1, 2)
+        quantize_w1(1, 0, 2, PACK)
+
+        round_w1(0, 1, 0, nc.vector.tensor_copy)
         embed(0, 0)
         embed(0, 1)
-        round_w1(0, 1, 1, 2, nc.scalar.copy)
-        round_w1(1, 1, 0, 1, nc.scalar.copy)
-        embed(0, 2)
+        round_w1(0, 1, 1, nc.scalar.copy)
+        round_w1(1, 1, 0, nc.scalar.copy)
+        embed(0, 2, "w1_raw110")
         embed(0, 3)
-        for t in range(4):
-            pick(0, t, 0, 512)
-            if t < 2:
-                quant_w1(t, 1, 0, 4)
-        for t in range(4):
+        new_run(0, ALL, "w1_raw010")
+        for t in range(PACK):
+            pick(0, t, ALL)
+            if t < PASSES:
+                quantize_w1(t, 1, 0, PACK)
+        for t in range(PACK):
             embed(1, t)
-        round_w4(0)
-        round_w4(1)
-        pick(1, 0, 0, 256)
-        diff(0, 0, 512)
-        pick(1, 1, 0, 256)
-        quant_z(0, 0, 512)
-        pick(1, 2, 0, 256)
-        pick(1, 3, 0, 256)
-        pick(1, 0, 256, 384)
-        diff(1, 0, 256)
-        pick(1, 1, 256, 384)
-        quant_z(1, 0, 256)
-        products(0, (2, 3))
-        products(1, (2, 3))
-        pick(1, 2, 256, 384)
-        pick(1, 3, 256, 384)
-        quant_w4(0)
-        diff(1, 256, 384)
-        quant_w4(1)
-        quant_z(1, 256, 384)
-        products(0, (4,))
-        products(1, (4,))
-        products(2, (2, 3, 4))
+        for b in range(PASSES):
+            round_w4(b)
+
+        new_run(1, FIRST)
+        pick(1, 0, FIRST)
+        subtract(0, ALL, "w1_bf11")
+        pick(1, 1, FIRST)
+        quantize_z(0, ALL)
+        pick(1, 2, FIRST)
+        pick(1, 3, FIRST)
+        new_run(1, SECOND)
+        pick(1, 0, SECOND)
+        subtract(1, FIRST)
+        pick(1, 1, SECOND)
+        quantize_z(1, FIRST)
+        for chunk in (0, 1):
+            product(chunk, 2)
+            product(chunk, 3)
+        pick(1, 2, SECOND)
+        pick(1, 3, SECOND)
+        quantize_w4(0)
+        subtract(1, SECOND)
+        quantize_w4(1)
+        quantize_z(1, SECOND)
+        product(0, 4)
+        product(1, 4)
+        for which in (2, 3, 4):
+            product(2, which)
         multiply(0)
-        for t in range(4):
-            pick(1, t, 384, 512)
+        new_run(1, LAST, "y2_sb0")
+        for t in range(PACK):
+            pick(1, t, LAST)
         multiply(1)
-        diff(1, 384, 512)
+        subtract(1, LAST)
         multiply(2)
-        quant_z(1, 384, 512)
-        products(3, (2, 3, 4))
-        for c in range(3):
-            finish(c)
+        quantize_z(1, LAST)
+        for which in (2, 3, 4):
+            product(3, which)
+        for chunk in range(3):
+            add_and_store(chunk)
         multiply(3)
-        finish(3)
+        add_and_store(3)

@@ -17,6 +17,7 @@ MULT = mybir.AluOpType.mult
 ADD = mybir.AluOpType.add
 SUB = mybir.AluOpType.subtract
 TANH = mybir.ActivationFunctionType.Tanh
+COPY = mybir.ActivationFunctionType.Copy
 
 P = 128
 PACK = 4
@@ -30,9 +31,9 @@ SCALE_ROWS = 4
 CHUNK = 128
 ROW_TILES = N // P
 
+HALF = PAIRS // 2
 ALL = (0, PAIRS)
-FIRST, SECOND, LAST = (0, 256), (256, 384), (384, PAIRS)
-WIDEST_RUN = (PAIRS, 256)
+FIRST, LAST = (0, HALF), (HALF, PAIRS)
 
 
 def tile_list_site_pair_couplings_kernel(
@@ -41,7 +42,7 @@ def tile_list_site_pair_couplings_kernel(
     nc = tc.nc
     with ExitStack() as ctx:
         keep = ctx.enter_context(tc.tile_pool(name="keep", bufs=1))
-        psum = ctx.enter_context(tc.psum_pool(name="psum", bufs=BANKS))
+        psum = ctx.enter_context(tc.psum_pool(name="psum", bufs=1))
 
         def sb(name, shape, dtype, tag=""):
             return keep.tile(shape, dtype, name=name, tag=tag or name, align_bytes=64)
@@ -50,23 +51,20 @@ def tile_list_site_pair_couplings_kernel(
         pos_sb = [sb("pos1_sb", [P, PAIRS // GROUP], U16), sb("pos2_sb", [P, PAIRS // GROUP], U16)]
         tab = [sb("tab%d" % a, [P, T], I32) for a in range(PASSES)]
         tab_sc = sb("tab_sc", [P, T], U8)
-        v = [sb("v%d" % a, [P, S], U32) for a in range(PASSES)]
+        v = {}
         v_sc = sb("v_sc", [P, S], U8)
         gain_sb = sb("gain_sb", [P, PASSES, PACK], F32)
-        gain_rows = [sb("gain_rows%d" % b, [P, PACK, WIDEST_RUN[b]], F32) for b in range(PASSES)]
         w23_sc = sb("w23_sc", [P, PASSES, N], U8)
         w2_sb = sb("w2_sb", [P, PASSES, 2 * N], U8)
         w3_sb = sb("w3_sb", [P, PASSES, N], I32)
 
         nc.vector.memset(tab_sc[:].bitcast(I32), 0)
-        nc.vector.memset(w23_sc[:].bitcast(I32), 0)
+        nc.gpsimd.memset(w23_sc[:].bitcast(I32), 0)
 
-        pieces = {(0, 0): 2, (1, 0): 2, (0, 1): 2, (1, 1): 1}
+        pieces = {(0, 0): 2, (1, 0): 2, (0, 1): 2, (1, 1): 2}
         w1_raw, w1_bf, w1_q, w1_sc = {}, {}, {}, {}
         for a in range(PASSES):
             for b in range(PASSES):
-                w1_bf[a, b] = sb("w1_bf%d%d" % (a, b), [P, PACK, P, PACK], BF16)
-                w1_q[a, b] = sb("w1_q%d%d" % (a, b), [P, PASS], U32)
                 w1_sc[a, b] = sb("w1_sc%d%d" % (a, b), [P, PASS], U8)
 
         def load_table_words(a):
@@ -80,14 +78,18 @@ def tile_list_site_pair_couplings_kernel(
                 rows = w1[PASS * a : PASS * (a + 1), channel : channel + width]
                 nc.sync.dma_start(out=w1_raw[a, b, piece][:], in_=rows.rearrange("(p j) c -> p j c", j=PACK))
 
-        def round_w1(a, b, piece, copy):
+        def round_w1(a, b, piece, copy, tag=""):
+            if piece == 0:
+                w1_bf[a, b] = sb("w1_bf%d%d" % (a, b), [P, PACK, P, PACK], BF16, tag)
             count = P // pieces[a, b]
             copy(
                 out=w1_bf[a, b][:, :, count * piece : count * (piece + 1), :].rearrange("p t m j -> p m j t"),
                 in_=w1_raw[a, b, piece][:].rearrange("p j (m t) -> p m j t", t=PACK),
             )
 
-        def quantize_w1(a, b, t0, t1):
+        def quantize_w1(a, b, t0, t1, tag=""):
+            if t0 == 0:
+                w1_q[a, b] = sb("w1_q%d%d" % (a, b), [P, PASS], U32, tag)
             cols = slice(P * t0, P * t1)
             nc.vector.quantize_mx(
                 out=w1_q[a, b][:, cols].bitcast(FP8X4),
@@ -126,7 +128,8 @@ def tile_list_site_pair_couplings_kernel(
 
         h = {}
 
-        def gather_table_words(a):
+        def gather_table_words(a, tag=""):
+            v[a] = sb("v%d" % a, [P, S], U32, tag)
             nc.vector.tensor_copy(v[a][:], tab[a][:].bitcast(U32).indirect(offs_sb[:]))
 
         def embed(b, t, tag=""):
@@ -134,7 +137,8 @@ def tile_list_site_pair_couplings_kernel(
             cols = slice(P * t, P * (t + 1))
             for site in range(0, S, BANK):
                 sites = slice(site, site + BANK)
-                acc = psum.tile([P, BANK], F32, name="acc")
+                bank = 4 + 2 * (t % 2) + site // BANK
+                acc = psum.tile([P, BANK], F32, name="acc%d%d%d" % (b, t, site), tag="bank%d" % bank)
                 for a in range(PASSES):
                     nc.tensor.matmul_mx(
                         out=acc[:],
@@ -149,26 +153,50 @@ def tile_list_site_pair_couplings_kernel(
 
         z_q = [sb("z_q%d" % b, [P, PAIRS], U32) for b in range(PASSES)]
         z_sc = [sb("z_sc%d" % b, [P, PAIRS], U8) for b in range(PASSES)]
-        picked, z_bf = {}, {}
+        diff0 = [sb("diff0%d" % t, [P, PAIRS], F32) for t in range(PACK)]
+        diff1 = sb("diff1", [P, PACK, PAIRS], F32)
+        z_bf = {}
 
-        def new_run(b, run, tag=""):
-            shape = [P, PACK, run[1] - run[0]]
-            picked[b, run] = [sb("pick%d_%d_0" % (b, run[0]), shape, F32, tag), sb("pick%d_%d_1" % (b, run[0]), shape, F32)]
 
-        def pick(b, t, run):
-            c0, c1 = run
-            for side in range(2):
+        def differences(b, parts, stage):
+            for i, (t, (c0, c1)) in enumerate(parts):
+                nc.vector.tensor_copy(
+                    stage[i][:, :], h[b, t][:].indirect(pos_sb[1][:, c0 // GROUP : c1 // GROUP])
+                )
+            for i, (t, (c0, c1)) in enumerate(parts):
                 nc.vector.tensor_tensor(
-                    picked[b, run][side][:, t, :],
-                    h[b, t][:].indirect(pos_sb[side][:, c0 // GROUP : c1 // GROUP]),
-                    gain_rows[b][:, t, 0 : c1 - c0],
-                    MULT,
+                    diff0[t][:, c0:c1] if b == 0 else diff1[:, t, c0:c1],
+                    h[b, t][:].indirect(pos_sb[0][:, c0 // GROUP : c1 // GROUP]),
+                    stage[i][:, :],
+                    SUB,
                 )
 
-        def subtract(b, run, tag=""):
-            z_bf[b, run] = sb("z_bf%d_%d" % (b, run[0]), [P, run[1] - run[0], PACK], BF16, tag)
-            first, second = [x[:].rearrange("p t (c i) -> p c t i", i=2) for x in picked[b, run]]
-            nc.vector.tensor_tensor(z_bf[b, run][:].rearrange("p (c i) t -> p c t i", i=2), first, second, SUB)
+        def halves(t, run):
+            middle = (run[0] + run[1]) // 2
+            return [(t, (run[0], middle)), (t, (middle, run[1]))]
+
+        def scale_on_vector(b, run, tag):
+            c0, c1 = run
+            z_bf[b, run] = sb("z_bf%d_%d" % (b, c0), [P, c1 - c0, PACK], BF16, tag)
+            nc.vector.tensor_tensor(
+                z_bf[b, run][:].rearrange("p (c i) t -> p c t i", i=2),
+                diff1[:, :, c0:c1].rearrange("p t (c i) -> p c t i", i=2),
+                gain_sb[:, b, :].unsqueeze(1).unsqueeze(3).to_broadcast([P, (c1 - c0) // 2, PACK, 2]),
+                MULT,
+            )
+
+        z_rows = {(b, run): sb("z_rows%d" % b, [P, PACK, run[1]], BF16) for b, run in ((0, ALL), (1, FIRST))}
+
+        def scale_on_scalar(b, run, t):
+            source = diff0[t][:] if b == 0 else diff1[:, t, run[0] : run[1]]
+            nc.scalar.activation(out=z_rows[b, run][:, t, :], in_=source, func=COPY, scale=gain_sb[:, b, t : t + 1])
+
+        def interleave_on_scalar(b, held, run):
+            z_bf[b, run] = sb("z_bf%d_%d" % (b, run[0]), [P, run[1] - run[0], PACK], BF16)
+            nc.scalar.copy(
+                out=z_bf[b, run][:].rearrange("p (c i) t -> p c t i", i=4),
+                in_=z_rows[b, held][:, :, run[0] : run[1]].rearrange("p t (c i) -> p c t i", i=4),
+            )
 
         def quantize_z(b, run):
             cols = slice(run[0], run[1])
@@ -178,11 +206,12 @@ def tile_list_site_pair_couplings_kernel(
                 in_=z_bf[b, run][:].rearrange("p c t -> p (c t)"),
             )
 
-        w4_bf = [sb("w4_bf%d" % b, [P, N, PACK], BF16) for b in range(PASSES)]
+        w4_bf = {}
         w4_q = [sb("w4_q%d" % b, [P, N], U32) for b in range(PASSES)]
         w4_sc = [sb("w4_sc%d" % b, [P, N], U8) for b in range(PASSES)]
 
-        def round_w4(b):
+        def round_w4(b, tag):
+            w4_bf[b] = sb("w4_bf%d" % b, [P, N, PACK], BF16, tag)
             nc.scalar.copy(
                 out=w4_bf[b][:].rearrange("p (c i) j -> p c j i", i=4),
                 in_=w4_raw[b][:].rearrange("p j (c i) -> p c j i", i=4),
@@ -203,106 +232,116 @@ def tile_list_site_pair_couplings_kernel(
 
         y, y2_sb, y23 = {}, {}, {}
 
-        def product(chunk, which):
-            cols = slice(CHUNK * chunk, CHUNK * (chunk + 1))
-            acc = psum.tile([P, BANK], F32, name="acc")
-            y[chunk, which] = acc
-            for tile in range(ROW_TILES):
-                for b in range(PASSES):
-                    codes, scales = weights(which, b, tile)
-                    nc.tensor.matmul_mx(
-                        out=acc[:, CHUNK * tile : CHUNK * (tile + 1)],
-                        lhsT=codes,
-                        lhsT_scale=scales,
-                        rhs=z_q[b][:, cols].bitcast(FP8X4),
-                        rhs_scale=z_sc[b][:, cols],
-                        start=(b == 0),
-                        stop=(b == PASSES - 1),
-                    )
-            if which == 2:
-                y2_sb[chunk] = sb("y2_sb%d" % chunk, [P, BANK], F32)
-                nc.scalar.copy(out=y2_sb[chunk][:], in_=acc[:])
+        def product(block, which, b, bank=None):
+            half, u = block
+            if b == 0:
+                y[block, which] = psum.tile([P, BANK], F32, name="y%d%d%d" % (half, u, which), tag="bank%d" % bank)
+            acc = y[block, which]
+            width = CHUNK if which == 2 else HALF
+            for at in range(0, BANK, width):
+                codes, scales = weights(which, b, 2 * u + at // HALF)
+                cols = slice(HALF * half + at % HALF, HALF * half + at % HALF + width)
+                nc.tensor.matmul_mx(
+                    out=acc[:, at : at + width],
+                    lhsT=codes,
+                    lhsT_scale=scales,
+                    rhs=z_q[b][:, cols].bitcast(FP8X4),
+                    rhs_scale=z_sc[b][:, cols],
+                    start=(b == 0 and at == 0),
+                    stop=(b == PASSES - 1 and at + width == BANK),
+                )
+            if which == 2 and b == PASSES - 1:
+                y2_sb[block] = sb("y2_sb%d%d" % block, [P, BANK], F32)
+                nc.scalar.copy(out=y2_sb[block][:], in_=acc[:])
 
-        def multiply(chunk):
-            y23[chunk] = sb("y23_%d" % chunk, [P, BANK], F32)
-            nc.vector.tensor_tensor(y23[chunk][:], y[chunk, 3][:], y2_sb[chunk][:], MULT)
+        def multiply(block):
+            y23[block] = sb("y23_%d%d" % block, [P, BANK], F32)
+            nc.vector.tensor_tensor(y23[block][:], y[block, 3][:], y2_sb[block][:], MULT)
 
-        def add_and_store(chunk):
-            result = sb("result%d" % chunk, [P, BANK], F32)
-            nc.vector.tensor_tensor(result[:], y[chunk, 4][:], y23[chunk][:], ADD)
+        def add_and_store(block):
+            half, u = block
+            result = sb("result%d%d" % block, [P, BANK], F32)
+            nc.vector.tensor_tensor(result[:], y[block, 4][:], y23[block][:], ADD)
             nc.sync.dma_start(
-                out=out[:, CHUNK * chunk : CHUNK * (chunk + 1)].rearrange("(tile p) c -> p tile c", p=P),
-                in_=result[:].rearrange("p (tile c) -> p tile c", c=CHUNK),
+                out=out[HALF * u : HALF * (u + 1), HALF * half : HALF * (half + 1)].rearrange("(i p) c -> p i c", p=P),
+                in_=result[:].rearrange("p (i c) -> p i c", c=HALF),
             )
 
-        for b in range(PASSES):
-            spread = gain_sb[:, b, :].unsqueeze(2).to_broadcast([P, PACK, WIDEST_RUN[b]])
-            nc.scalar.copy(out=gain_rows[b][:], in_=spread)
         gather_table_words(0)
         nc.vector.tensor_copy(v_sc[:], tab_sc[:].indirect(offs_sb[:]))
         round_w1(0, 0, 0, nc.scalar.copy)
         round_w1(0, 0, 1, nc.scalar.copy)
         quantize_w1(0, 0, 0, PACK)
-        gather_table_words(1)
+        gather_table_words(1, "w1_bf00")
         round_w1(1, 0, 0, nc.scalar.copy)
-        round_w1(1, 0, 1, nc.vector.tensor_copy)
+        round_w1(1, 0, 1, nc.scalar.copy)
         quantize_w1(1, 0, 0, 1)
         quantize_w1(1, 0, 1, 2)
         quantize_w1(1, 0, 2, PACK)
 
-        round_w1(0, 1, 0, nc.vector.tensor_copy)
-        embed(0, 0)
-        embed(0, 1)
-        round_w1(0, 1, 1, nc.scalar.copy)
-        round_w1(1, 1, 0, nc.scalar.copy)
-        embed(0, 2, "w1_raw110")
-        embed(0, 3)
-        new_run(0, ALL, "w1_raw010")
-        for t in range(PACK):
-            pick(0, t, ALL)
-            if t < PASSES:
-                quantize_w1(t, 1, 0, PACK)
-        for t in range(PACK):
-            embed(1, t)
-        for b in range(PASSES):
-            round_w4(b)
+        round_w1(0, 1, 0, nc.vector.tensor_copy, "w1_bf10")
+        round_w1(0, 1, 1, nc.vector.tensor_copy)
+        def stage(name, width, tag=""):
+            both = sb(name, [P, 2, width], F32, tag)
+            return [both[:, i, :] for i in range(2)]
 
-        new_run(1, FIRST)
-        pick(1, 0, FIRST)
-        subtract(0, ALL, "w1_bf11")
-        pick(1, 1, FIRST)
-        quantize_z(0, ALL)
-        pick(1, 2, FIRST)
-        pick(1, 3, FIRST)
-        new_run(1, SECOND)
-        pick(1, 0, SECOND)
-        subtract(1, FIRST)
-        pick(1, 1, SECOND)
-        quantize_z(1, FIRST)
-        for chunk in (0, 1):
-            product(chunk, 2)
-            product(chunk, 3)
-        pick(1, 2, SECOND)
-        pick(1, 3, SECOND)
+        for t in range(PACK - 1):
+            embed(0, t)
+        differences(0, halves(0, ALL), [sb("stage0_%d" % i, [P, HALF], F32) for i in range(2)])
+        quantize_w1(0, 1, 0, PACK, "stage0_0")
+        differences(0, halves(1, ALL), stage("stage1", HALF))
+        round_w1(1, 1, 0, nc.scalar.copy, "stage0_1")
+        round_w1(1, 1, 1, nc.scalar.copy)
+        embed(0, 3, "w1_raw111")
+        quantize_w1(1, 1, 0, PACK)
+        differences(0, [(2, ALL), (3, ALL)], stage("stage_a", PAIRS, "stage0_1"))
+        scale_on_scalar(0, ALL, 0)
+        embed(1, 0)
+        embed(1, 1)
+        scale_on_scalar(0, ALL, 1)
+        embed(1, 2)
+        embed(1, 3)
+        scale_on_scalar(0, ALL, 2)
+        scale_on_scalar(0, ALL, 3)
+        round_w4(0, "stage0_1")
+        interleave_on_scalar(0, ALL, ALL)
+        round_w4(1, "z_rows0")
+
+        differences(1, [(0, ALL), (1, ALL)], stage("stage_b", PAIRS, "diff01"))
         quantize_w4(0)
-        subtract(1, SECOND)
-        quantize_w4(1)
-        quantize_z(1, SECOND)
-        product(0, 4)
-        product(1, 4)
-        for which in (2, 3, 4):
-            product(2, which)
-        multiply(0)
-        new_run(1, LAST, "y2_sb0")
+        differences(1, [(2, FIRST), (3, FIRST)], stage("stage_c", HALF, "diff02"))
         for t in range(PACK):
-            pick(1, t, LAST)
-        multiply(1)
-        subtract(1, LAST)
-        multiply(2)
+            scale_on_scalar(1, FIRST, t)
+        for quarter in ((0, CHUNK), (CHUNK, HALF)):
+            interleave_on_scalar(1, FIRST, quarter)
+        quantize_z(0, ALL)
+        blocks = [(half, u) for half in range(2) for u in range(2)]
+        for bank in range(BANKS):
+            product(blocks[bank // 3], 2 + bank % 3, 0, bank)
+        quantize_w4(1)
+        differences(1, [(2, LAST), (3, LAST)], stage("stage_d", HALF, "z_bf0_0"))
+        for quarter in ((0, CHUNK), (CHUNK, HALF)):
+            quantize_z(1, quarter)
+        for which in (2, 3):
+            product(blocks[0], which, 1)
+        for which in (2, 3):
+            product(blocks[1], which, 1)
+        product(blocks[0], 4, 1)
+        product(blocks[1], 4, 1)
+        scale_on_vector(1, LAST, "z_bf1_0")
+        multiply(blocks[0])
         quantize_z(1, LAST)
-        for which in (2, 3, 4):
-            product(3, which)
-        for chunk in range(3):
-            add_and_store(chunk)
-        multiply(3)
-        add_and_store(3)
+        product(blocks[2], 2, 1)
+        product(blocks[2], 3, 1)
+        for block, which, bank in ((blocks[2], 4, 0), (blocks[3], 2, 1), (blocks[3], 3, 3)):
+            product(block, which, 0, bank)
+            product(block, which, 1)
+        multiply(blocks[1])
+        product(blocks[3], 4, 0, 4)
+        product(blocks[3], 4, 1)
+        add_and_store(blocks[0])
+        multiply(blocks[2])
+        add_and_store(blocks[1])
+        multiply(blocks[3])
+        add_and_store(blocks[2])
+        add_and_store(blocks[3])

@@ -58,10 +58,10 @@ def tile_list_site_pair_couplings_kernel(
         w2_sb = sb("w2_sb", [P, PASSES, 2 * N], U8)
         w3_sb = sb("w3_sb", [P, PASSES, N], I32)
 
-        nc.vector.memset(tab_sc[:].bitcast(I32), 0)
-        nc.gpsimd.memset(w23_sc[:].bitcast(I32), 0)
+        nc.gpsimd.memset(tab_sc[:].bitcast(I32), 0)
+        nc.vector.memset(w23_sc[:].bitcast(I32), 0)
 
-        pieces = {(0, 0): 2, (1, 0): 2, (0, 1): 2, (1, 1): 2}
+        pieces = {(0, 0): 1, (1, 0): 1, (0, 1): 2, (1, 1): 1}
         w1_raw, w1_bf, w1_q, w1_sc = {}, {}, {}, {}
         for a in range(PASSES):
             for b in range(PASSES):
@@ -78,13 +78,14 @@ def tile_list_site_pair_couplings_kernel(
                 rows = w1[PASS * a : PASS * (a + 1), channel : channel + width]
                 nc.sync.dma_start(out=w1_raw[a, b, piece][:], in_=rows.rearrange("(p j) c -> p j c", j=PACK))
 
-        def round_w1(a, b, piece, copy, tag=""):
-            if piece == 0:
+        def round_w1(a, b, m0, m1, copy, tag=""):
+            if m0 == 0:
                 w1_bf[a, b] = sb("w1_bf%d%d" % (a, b), [P, PACK, P, PACK], BF16, tag)
             count = P // pieces[a, b]
+            raw = w1_raw[a, b, m0 // count][:].rearrange("p j (m t) -> p m j t", t=PACK)
             copy(
-                out=w1_bf[a, b][:, :, count * piece : count * (piece + 1), :].rearrange("p t m j -> p m j t"),
-                in_=w1_raw[a, b, piece][:].rearrange("p j (m t) -> p m j t", t=PACK),
+                out=w1_bf[a, b][:, :, m0:m1, :].rearrange("p t m j -> p m j t"),
+                in_=raw[:, m0 % count : m0 % count + m1 - m0],
             )
 
         def quantize_w1(a, b, t0, t1, tag=""):
@@ -97,11 +98,10 @@ def tile_list_site_pair_couplings_kernel(
                 in_=w1_bf[a, b][:, t0:t1].rearrange("p t m j -> p (t m j)"),
             )
 
-        nc.sync.dma_start(out=gain_sb[:], in_=gain.rearrange("(b p t) -> p b t", b=PASSES, t=PACK))
-        load_table_words(0)
         nc.sync.dma_start(offs_sb[:], offs)
+        load_table_words(0)
         for q in range(P // QUADRANT):
-            nc.sync.dma_start(
+            nc.gpsimd.dma_start(
                 out=tab_sc[QUADRANT * q : QUADRANT * q + PASSES * SCALE_ROWS, :].bitcast(I32),
                 in_=tab_scales[:, SCALE_ROWS * q : SCALE_ROWS * (q + 1), :].bitcast(I32),
             )
@@ -112,6 +112,7 @@ def tile_list_site_pair_couplings_kernel(
         nc.sync.dma_start(pos_sb[1][:], pos2)
         load_w1(0, 1)
         load_w1(1, 1)
+        nc.sync.dma_start(out=gain_sb[:], in_=gain.rearrange("(b p t) -> p b t", b=PASSES, t=PACK))
         w4_raw = [sb("w4_raw%d" % b, [P, PACK, N], F32) for b in range(PASSES)]
         for b in range(PASSES):
             rows = w4[PASS * b : PASS * (b + 1), :]
@@ -269,18 +270,17 @@ def tile_list_site_pair_couplings_kernel(
 
         gather_table_words(0)
         nc.vector.tensor_copy(v_sc[:], tab_sc[:].indirect(offs_sb[:]))
-        round_w1(0, 0, 0, nc.scalar.copy)
-        round_w1(0, 0, 1, nc.scalar.copy)
+        round_w1(0, 0, 0, P, nc.scalar.copy)
         quantize_w1(0, 0, 0, PACK)
         gather_table_words(1, "w1_bf00")
-        round_w1(1, 0, 0, nc.scalar.copy)
-        round_w1(1, 0, 1, nc.scalar.copy)
+        round_w1(1, 0, 0, 48, nc.scalar.copy)
+        round_w1(1, 0, 48, P, nc.vector.tensor_copy)
         quantize_w1(1, 0, 0, 1)
         quantize_w1(1, 0, 1, 2)
         quantize_w1(1, 0, 2, PACK)
 
-        round_w1(0, 1, 0, nc.vector.tensor_copy, "w1_bf10")
-        round_w1(0, 1, 1, nc.vector.tensor_copy)
+        round_w1(0, 1, 0, P // 2, nc.vector.tensor_copy, "w1_bf10")
+        round_w1(0, 1, P // 2, P, nc.vector.tensor_copy)
         def stage(name, width, tag=""):
             both = sb(name, [P, 2, width], F32, tag)
             return [both[:, i, :] for i in range(2)]
@@ -290,9 +290,8 @@ def tile_list_site_pair_couplings_kernel(
         differences(0, halves(0, ALL), [sb("stage0_%d" % i, [P, HALF], F32) for i in range(2)])
         quantize_w1(0, 1, 0, PACK, "stage0_0")
         differences(0, halves(1, ALL), stage("stage1", HALF))
-        round_w1(1, 1, 0, nc.scalar.copy, "stage0_1")
-        round_w1(1, 1, 1, nc.scalar.copy)
-        embed(0, 3, "w1_raw111")
+        round_w1(1, 1, 0, P, nc.scalar.copy, "stage0_1")
+        embed(0, 3, "w1_raw110")
         quantize_w1(1, 1, 0, PACK)
         differences(0, [(2, ALL), (3, ALL)], stage("stage_a", PAIRS, "stage0_1"))
         scale_on_scalar(0, ALL, 0)

@@ -58,10 +58,10 @@ def tile_list_site_pair_couplings_kernel(
         w2_sb = sb("w2_sb", [P, PASSES, 2 * N], U8)
         w3_sb = sb("w3_sb", [P, PASSES, N], I32)
 
-        nc.gpsimd.memset(tab_sc[:].bitcast(I32), 0)
-        nc.vector.memset(w23_sc[:].bitcast(I32), 0)
+        nc.vector.memset(tab_sc[:].bitcast(I32), 0)
+        nc.gpsimd.memset(w23_sc[:].bitcast(I32), 0)
 
-        pieces = {(0, 0): 1, (1, 0): 1, (0, 1): 2, (1, 1): 1}
+        pieces = {(0, 0): 1, (1, 0): 2, (0, 1): 2, (1, 1): 1}
         w1_raw, w1_bf, w1_q, w1_sc = {}, {}, {}, {}
         for a in range(PASSES):
             for b in range(PASSES):
@@ -98,17 +98,17 @@ def tile_list_site_pair_couplings_kernel(
                 in_=w1_bf[a, b][:, t0:t1].rearrange("p t m j -> p (t m j)"),
             )
 
-        nc.sync.dma_start(offs_sb[:], offs)
+        nc.sync.dma_start(pos_sb[0][:], pos1)
         load_table_words(0)
+        nc.sync.dma_start(offs_sb[:], offs)
         for q in range(P // QUADRANT):
-            nc.gpsimd.dma_start(
+            nc.sync.dma_start(
                 out=tab_sc[QUADRANT * q : QUADRANT * q + PASSES * SCALE_ROWS, :].bitcast(I32),
                 in_=tab_scales[:, SCALE_ROWS * q : SCALE_ROWS * (q + 1), :].bitcast(I32),
             )
         load_w1(0, 0)
         load_table_words(1)
         load_w1(1, 0)
-        nc.sync.dma_start(pos_sb[0][:], pos1)
         nc.sync.dma_start(pos_sb[1][:], pos2)
         load_w1(0, 1)
         load_w1(1, 1)
@@ -273,8 +273,8 @@ def tile_list_site_pair_couplings_kernel(
         round_w1(0, 0, 0, P, nc.scalar.copy)
         quantize_w1(0, 0, 0, PACK)
         gather_table_words(1, "w1_bf00")
-        round_w1(1, 0, 0, 48, nc.scalar.copy)
-        round_w1(1, 0, 48, P, nc.vector.tensor_copy)
+        round_w1(1, 0, 0, P // 2, nc.scalar.copy)
+        round_w1(1, 0, P // 2, P, nc.scalar.copy)
         quantize_w1(1, 0, 0, 1)
         quantize_w1(1, 0, 1, 2)
         quantize_w1(1, 0, 2, PACK)

@@ -67,20 +67,24 @@ def tile_list_site_pair_couplings_kernel(
             for b in range(PASSES):
                 w1_sc[a, b] = sb("w1_sc%d%d" % (a, b), [P, PASS], U8)
 
+        shared = sb("w1_bf_shared", [P, 2 * PACK * PASS - PASS // 2], BF16)
+        w1_bf[1, 0] = shared[:, 0 : PACK * PASS].rearrange("p (t m j) -> p t m j", t=PACK, j=PACK)
+        w1_bf[0, 1] = shared[:, PACK * PASS - PASS // 2 :].rearrange("p (t m j) -> p t m j", t=PACK, j=PACK)
+
         def load_table_words(a):
             nc.sync.dma_start(out=tab[a][:], in_=tab_words[a].rearrange("p c i -> p (c i)").bitcast(I32))
 
         def load_w1(a, b):
             width = PASS // pieces[a, b]
-            for piece in range(pieces[a, b]):
+            for piece in (1, 0) if (a, b) == (0, 1) else range(pieces[a, b]):
                 w1_raw[a, b, piece] = sb("w1_raw%d%d%d" % (a, b, piece), [P, PACK, width], F32)
                 channel = PASS * b + width * piece
                 rows = w1[PASS * a : PASS * (a + 1), channel : channel + width]
                 nc.sync.dma_start(out=w1_raw[a, b, piece][:], in_=rows.rearrange("(p j) c -> p j c", j=PACK))
 
         def round_w1(a, b, m0, m1, copy, tag=""):
-            if m0 == 0:
-                w1_bf[a, b] = sb("w1_bf%d%d" % (a, b), [P, PACK, P, PACK], BF16, tag)
+            if (a, b) not in w1_bf:
+                w1_bf[a, b] = sb("w1_bf%d%d" % (a, b), [P, PACK, P, PACK], BF16, tag)[:]
             count = P // pieces[a, b]
             raw = w1_raw[a, b, m0 // count][:].rearrange("p j (m t) -> p m j t", t=PACK)
             copy(
@@ -208,7 +212,7 @@ def tile_list_site_pair_couplings_kernel(
             )
 
         w4_bf = {}
-        w4_q = [sb("w4_q%d" % b, [P, N], U32) for b in range(PASSES)]
+        w4_q = {}
         w4_sc = [sb("w4_sc%d" % b, [P, N], U8) for b in range(PASSES)]
 
         def round_w4(b, tag):
@@ -218,7 +222,8 @@ def tile_list_site_pair_couplings_kernel(
                 in_=w4_raw[b][:].rearrange("p j (c i) -> p c j i", i=4),
             )
 
-        def quantize_w4(b):
+        def quantize_w4(b, tag=""):
+            w4_q[b] = sb("w4_q%d" % b, [P, N], U32, tag)
             nc.vector.quantize_mx(
                 out=w4_q[b][:].bitcast(FP8X4), scales=w4_sc[b][:], in_=w4_bf[b][:].rearrange("p c j -> p (c j)")
             )
@@ -259,12 +264,19 @@ def tile_list_site_pair_couplings_kernel(
             y23[block] = sb("y23_%d%d" % block, [P, BANK], F32)
             nc.vector.tensor_tensor(y23[block][:], y[block, 3][:], y2_sb[block][:], MULT)
 
-        def add_and_store(block):
+        def add_and_store(block, parts=1):
             half, u = block
-            result = sb("result%d%d" % block, [P, BANK], F32)
-            nc.vector.tensor_tensor(result[:], y[block, 4][:], y23[block][:], ADD)
+            width = BANK // parts
+            for at in range(0, BANK, width):
+                result = sb("result%d%d_%d" % (half, u, at), [P, width], F32)
+                nc.vector.tensor_tensor(result[:], y[block, 4][:, at : at + width], y23[block][:, at : at + width], ADD)
+                store(block, result, at, width)
+
+        def store(block, result, at, width):
+            half, u = block
+            row = HALF * u + at // HALF * P
             nc.sync.dma_start(
-                out=out[HALF * u : HALF * (u + 1), HALF * half : HALF * (half + 1)].rearrange("(i p) c -> p i c", p=P),
+                out=out[row : row + width // HALF * P, HALF * half : HALF * (half + 1)].rearrange("(i p) c -> p i c", p=P),
                 in_=result[:].rearrange("p (i c) -> p i c", c=HALF),
             )
 
@@ -279,8 +291,9 @@ def tile_list_site_pair_couplings_kernel(
         quantize_w1(1, 0, 1, 2)
         quantize_w1(1, 0, 2, PACK)
 
-        round_w1(0, 1, 0, P // 2, nc.vector.tensor_copy, "w1_bf10")
-        round_w1(0, 1, P // 2, P, nc.vector.tensor_copy)
+        round_w1(0, 1, P // 2, P, nc.scalar.copy)
+        round_w1(0, 1, 0, P // 2, nc.vector.tensor_copy)
+        quantize_w1(0, 1, 0, PACK)
         def stage(name, width, tag=""):
             both = sb(name, [P, 2, width], F32, tag)
             return [both[:, i, :] for i in range(2)]
@@ -288,13 +301,12 @@ def tile_list_site_pair_couplings_kernel(
         for t in range(PACK - 1):
             embed(0, t)
         differences(0, halves(0, ALL), [sb("stage0_%d" % i, [P, HALF], F32) for i in range(2)])
-        quantize_w1(0, 1, 0, PACK, "stage0_0")
         differences(0, halves(1, ALL), stage("stage1", HALF))
-        round_w1(1, 1, 0, P, nc.scalar.copy, "stage0_1")
-        embed(0, 3, "w1_raw110")
+        round_w1(1, 1, 0, P, nc.scalar.copy, "stage0_0")
+        embed(0, 3)
         quantize_w1(1, 1, 0, PACK)
-        differences(0, [(2, ALL), (3, ALL)], stage("stage_a", PAIRS, "stage0_1"))
         scale_on_scalar(0, ALL, 0)
+        differences(0, [(2, ALL), (3, ALL)], stage("stage_a", PAIRS, "diff00"))
         embed(1, 0)
         embed(1, 1)
         scale_on_scalar(0, ALL, 1)
@@ -302,7 +314,7 @@ def tile_list_site_pair_couplings_kernel(
         embed(1, 3)
         scale_on_scalar(0, ALL, 2)
         scale_on_scalar(0, ALL, 3)
-        round_w4(0, "stage0_1")
+        round_w4(0, "diff00")
         interleave_on_scalar(0, ALL, ALL)
         round_w4(1, "z_rows0")
 
@@ -317,30 +329,27 @@ def tile_list_site_pair_couplings_kernel(
         blocks = [(half, u) for half in range(2) for u in range(2)]
         for bank in range(BANKS):
             product(blocks[bank // 3], 2 + bank % 3, 0, bank)
-        quantize_w4(1)
         differences(1, [(2, LAST), (3, LAST)], stage("stage_d", HALF, "z_bf0_0"))
         for quarter in ((0, CHUNK), (CHUNK, HALF)):
             quantize_z(1, quarter)
-        for which in (2, 3):
-            product(blocks[0], which, 1)
-        for which in (2, 3):
-            product(blocks[1], which, 1)
-        product(blocks[0], 4, 1)
-        product(blocks[1], 4, 1)
+        for block in blocks[:2]:
+            for which in (2, 3):
+                product(block, which, 1)
         scale_on_vector(1, LAST, "z_bf1_0")
-        multiply(blocks[0])
+        quantize_w4(1, "z_bf1_128")
+        for block in blocks[:2]:
+            product(block, 4, 1)
         quantize_z(1, LAST)
         product(blocks[2], 2, 1)
         product(blocks[2], 3, 1)
-        for block, which, bank in ((blocks[2], 4, 0), (blocks[3], 2, 1), (blocks[3], 3, 3)):
+        multiply(blocks[0])
+        multiply(blocks[1])
+        for block, which, bank in ((blocks[3], 2, 0), (blocks[3], 3, 3), (blocks[2], 4, 1), (blocks[3], 4, 4)):
             product(block, which, 0, bank)
             product(block, which, 1)
-        multiply(blocks[1])
-        product(blocks[3], 4, 0, 4)
-        product(blocks[3], 4, 1)
         add_and_store(blocks[0])
-        multiply(blocks[2])
         add_and_store(blocks[1])
+        multiply(blocks[2])
         multiply(blocks[3])
         add_and_store(blocks[2])
-        add_and_store(blocks[3])
+        add_and_store(blocks[3], 2)

@@ -163,6 +163,17 @@ def tile_list_site_pair_couplings_kernel(
         z_bf = {}
 
 
+        late = {}
+
+        def diff_row(b, t, run):
+            if b == 0:
+                return diff0[t][:, run[0] : run[1]]
+            if t >= 2 and run == FIRST:
+                if not late:
+                    late[0] = sb("diff1_first", [P, 2, HALF], F32, "z_bf0_0")
+                return late[0][:, t - 2, :]
+            return diff1[:, t, run[0] : run[1]]
+
         def differences(b, parts, stage):
             for i, (t, (c0, c1)) in enumerate(parts):
                 nc.vector.tensor_copy(
@@ -170,7 +181,7 @@ def tile_list_site_pair_couplings_kernel(
                 )
             for i, (t, (c0, c1)) in enumerate(parts):
                 nc.vector.tensor_tensor(
-                    diff0[t][:, c0:c1] if b == 0 else diff1[:, t, c0:c1],
+                    diff_row(b, t, (c0, c1)),
                     h[b, t][:].indirect(pos_sb[0][:, c0 // GROUP : c1 // GROUP]),
                     stage[i][:, :],
                     SUB,
@@ -193,7 +204,7 @@ def tile_list_site_pair_couplings_kernel(
         z_rows = {(b, run): sb("z_rows%d" % b, [P, PACK, run[1]], BF16) for b, run in ((0, ALL), (1, FIRST))}
 
         def scale_on_scalar(b, run, t):
-            source = diff0[t][:] if b == 0 else diff1[:, t, run[0] : run[1]]
+            source = diff_row(b, t, run)
             nc.scalar.activation(out=z_rows[b, run][:, t, :], in_=source, func=COPY, scale=gain_sb[:, b, t : t + 1])
 
         def interleave_on_scalar(b, held, run):
@@ -215,11 +226,12 @@ def tile_list_site_pair_couplings_kernel(
         w4_q = {}
         w4_sc = [sb("w4_sc%d" % b, [P, N], U8) for b in range(PASSES)]
 
-        def round_w4(b, tag):
-            w4_bf[b] = sb("w4_bf%d" % b, [P, N, PACK], BF16, tag)
+        def round_w4(b, n0, n1, tag=""):
+            if n0 == 0:
+                w4_bf[b] = sb("w4_bf%d" % b, [P, N, PACK], BF16, tag)
             nc.scalar.copy(
-                out=w4_bf[b][:].rearrange("p (c i) j -> p c j i", i=4),
-                in_=w4_raw[b][:].rearrange("p j (c i) -> p c j i", i=4),
+                out=w4_bf[b][:, n0:n1, :].rearrange("p (c i) j -> p c j i", i=4),
+                in_=w4_raw[b][:, :, n0:n1].rearrange("p j (c i) -> p c j i", i=4),
             )
 
         def quantize_w4(b, tag=""):
@@ -272,6 +284,11 @@ def tile_list_site_pair_couplings_kernel(
                 nc.vector.tensor_tensor(result[:], y[block, 4][:, at : at + width], y23[block][:, at : at + width], ADD)
                 store(block, result, at, width)
 
+        def add_on_gpsimd_and_store(block):
+            result = sb("result%d%d" % block, [P, BANK], F32)
+            nc.gpsimd.tensor_tensor(result[:], y4_sb[:], y23[block][:], ADD)
+            store(block, result, 0, BANK)
+
         def store(block, result, at, width):
             half, u = block
             row = HALF * u + at // HALF * P
@@ -307,6 +324,8 @@ def tile_list_site_pair_couplings_kernel(
         quantize_w1(1, 1, 0, PACK)
         scale_on_scalar(0, ALL, 0)
         differences(0, [(2, ALL), (3, ALL)], stage("stage_a", PAIRS, "diff00"))
+        round_w4(0, 0, N, "stage1")
+        quantize_w4(0)
         embed(1, 0)
         embed(1, 1)
         scale_on_scalar(0, ALL, 1)
@@ -314,41 +333,46 @@ def tile_list_site_pair_couplings_kernel(
         embed(1, 3)
         scale_on_scalar(0, ALL, 2)
         scale_on_scalar(0, ALL, 3)
-        round_w4(0, "diff00")
+        round_w4(1, 0, N // 4)
         interleave_on_scalar(0, ALL, ALL)
-        round_w4(1, "z_rows0")
+        round_w4(1, N // 4, N)
 
         differences(1, [(0, ALL), (1, ALL)], stage("stage_b", PAIRS, "diff01"))
-        quantize_w4(0)
-        differences(1, [(2, FIRST), (3, FIRST)], stage("stage_c", HALF, "diff02"))
-        for t in range(PACK):
-            scale_on_scalar(1, FIRST, t)
-        for quarter in ((0, CHUNK), (CHUNK, HALF)):
-            interleave_on_scalar(1, FIRST, quarter)
         quantize_z(0, ALL)
         blocks = [(half, u) for half in range(2) for u in range(2)]
         for bank in range(BANKS):
             product(blocks[bank // 3], 2 + bank % 3, 0, bank)
-        differences(1, [(2, LAST), (3, LAST)], stage("stage_d", HALF, "z_bf0_0"))
+        for run in (FIRST, LAST):
+            tiles = [sb("stage_%d_%d" % (run[0], t), [P, HALF], F32, "diff0%d" % t) for t in (2, 3)]
+            differences(1, [(2, run), (3, run)], tiles)
+        for t in range(PACK):
+            scale_on_scalar(1, FIRST, t)
+        for quarter in ((0, CHUNK), (CHUNK, HALF)):
+            interleave_on_scalar(1, FIRST, quarter)
         for quarter in ((0, CHUNK), (CHUNK, HALF)):
             quantize_z(1, quarter)
+        quantize_w4(1, "z_bf1_0")
         for block in blocks[:2]:
             for which in (2, 3):
                 product(block, which, 1)
-        scale_on_vector(1, LAST, "z_bf1_0")
-        quantize_w4(1, "z_bf1_128")
         for block in blocks[:2]:
             product(block, 4, 1)
-        quantize_z(1, LAST)
-        product(blocks[2], 2, 1)
-        product(blocks[2], 3, 1)
+        y4_sb = sb("y4_sb", [P, BANK], F32)
+        nc.scalar.copy(out=y4_sb[:], in_=y[blocks[1], 4][:])
+        scale_on_vector(1, LAST, "z_bf1_128")
         multiply(blocks[0])
+        product(blocks[3], 2, 0, 0)
+        product(blocks[3], 3, 0, 3)
+        quantize_z(1, LAST)
+        for which in (2, 3):
+            for block in blocks[2:]:
+                product(block, which, 1)
+        for block, bank in ((blocks[2], 1), (blocks[3], 5)):
+            product(block, 4, 0, bank)
+            product(block, 4, 1)
         multiply(blocks[1])
-        for block, which, bank in ((blocks[3], 2, 0), (blocks[3], 3, 3), (blocks[2], 4, 1), (blocks[3], 4, 4)):
-            product(block, which, 0, bank)
-            product(block, which, 1)
         add_and_store(blocks[0])
-        add_and_store(blocks[1])
+        add_on_gpsimd_and_store(blocks[1])
         multiply(blocks[2])
         multiply(blocks[3])
         add_and_store(blocks[2])

@@ -102,9 +102,8 @@ def tile_list_site_pair_couplings_kernel(
                 in_=w1_bf[a, b][:, t0:t1].rearrange("p t m j -> p (t m j)"),
             )
 
-        nc.sync.dma_start(pos_sb[0][:], pos1)
-        load_table_words(0)
         nc.sync.dma_start(offs_sb[:], offs)
+        load_table_words(0)
         for q in range(P // QUADRANT):
             nc.sync.dma_start(
                 out=tab_sc[QUADRANT * q : QUADRANT * q + PASSES * SCALE_ROWS, :].bitcast(I32),
@@ -113,8 +112,9 @@ def tile_list_site_pair_couplings_kernel(
         load_w1(0, 0)
         load_table_words(1)
         load_w1(1, 0)
-        nc.sync.dma_start(pos_sb[1][:], pos2)
         load_w1(0, 1)
+        nc.sync.dma_start(pos_sb[1][:], pos2)
+        nc.sync.dma_start(pos_sb[0][:], pos1)
         load_w1(1, 1)
         nc.sync.dma_start(out=gain_sb[:], in_=gain.rearrange("(b p t) -> p b t", b=PASSES, t=PACK))
         w4_raw = [sb("w4_raw%d" % b, [P, PACK, N], F32) for b in range(PASSES)]
@@ -158,7 +158,7 @@ def tile_list_site_pair_couplings_kernel(
 
         z_q = [sb("z_q%d" % b, [P, PAIRS], U32) for b in range(PASSES)]
         z_sc = [sb("z_sc%d" % b, [P, PAIRS], U8) for b in range(PASSES)]
-        diff0 = [sb("diff0%d" % t, [P, PAIRS], F32) for t in range(PACK)]
+        diff0 = {t: sb("diff0%d" % t, [P, PAIRS], F32) for t in (2, 3)}
         diff1 = sb("diff1", [P, PACK, PAIRS], F32)
         z_bf = {}
 
@@ -186,10 +186,6 @@ def tile_list_site_pair_couplings_kernel(
                     stage[i][:, :],
                     SUB,
                 )
-
-        def halves(t, run):
-            middle = (run[0] + run[1]) // 2
-            return [(t, (run[0], middle)), (t, (middle, run[1]))]
 
         def scale_on_vector(b, run, tag):
             c0, c1 = run
@@ -317,13 +313,14 @@ def tile_list_site_pair_couplings_kernel(
 
         for t in range(PACK - 1):
             embed(0, t)
-        differences(0, halves(0, ALL), [sb("stage0_%d" % i, [P, HALF], F32) for i in range(2)])
-        differences(0, halves(1, ALL), stage("stage1", HALF))
-        round_w1(1, 1, 0, P, nc.scalar.copy, "stage0_0")
+        round_w1(1, 1, 0, P, nc.scalar.copy, "w1_raw011")
         embed(0, 3)
+        diff0[0] = sb("diff00", [P, PAIRS], F32, "w1_q00")
+        diff0[1] = sb("diff01", [P, PAIRS], F32, "w1_sc00")
+        differences(0, [(0, ALL), (1, ALL)], stage("stage1", PAIRS))
         quantize_w1(1, 1, 0, PACK)
         scale_on_scalar(0, ALL, 0)
-        differences(0, [(2, ALL), (3, ALL)], stage("stage_a", PAIRS, "diff00"))
+        differences(0, [(2, ALL), (3, ALL)], stage("stage_a", PAIRS, "w1_q00"))
         round_w4(0, 0, N, "stage1")
         quantize_w4(0)
         embed(1, 0)
@@ -337,7 +334,7 @@ def tile_list_site_pair_couplings_kernel(
         interleave_on_scalar(0, ALL, ALL)
         round_w4(1, N // 4, N)
 
-        differences(1, [(0, ALL), (1, ALL)], stage("stage_b", PAIRS, "diff01"))
+        differences(1, [(0, ALL), (1, ALL)], stage("stage_b", PAIRS, "w1_sc00"))
         quantize_z(0, ALL)
         blocks = [(half, u) for half in range(2) for u in range(2)]
         for bank in range(BANKS):

@@ -280,11 +280,6 @@ def tile_list_site_pair_couplings_kernel(
                 nc.vector.tensor_tensor(result[:], y[block, 4][:, at : at + width], y23[block][:, at : at + width], ADD)
                 store(block, result, at, width)
 
-        def add_on_gpsimd_and_store(block):
-            result = sb("result%d%d" % block, [P, BANK], F32)
-            nc.gpsimd.tensor_tensor(result[:], y4_sb[:], y23[block][:], ADD)
-            store(block, result, 0, BANK)
-
         def store(block, result, at, width):
             half, u = block
             row = HALF * u + at // HALF * P
@@ -354,8 +349,6 @@ def tile_list_site_pair_couplings_kernel(
                 product(block, which, 1)
         for block in blocks[:2]:
             product(block, 4, 1)
-        y4_sb = sb("y4_sb", [P, BANK], F32)
-        nc.scalar.copy(out=y4_sb[:], in_=y[blocks[1], 4][:])
         scale_on_vector(1, LAST, "z_bf1_128")
         multiply(blocks[0])
         product(blocks[3], 2, 0, 0)
@@ -364,12 +357,12 @@ def tile_list_site_pair_couplings_kernel(
         for which in (2, 3):
             for block in blocks[2:]:
                 product(block, which, 1)
-        for block, bank in ((blocks[2], 1), (blocks[3], 5)):
+        for block, bank in ((blocks[2], 1), (blocks[3], 4)):
             product(block, 4, 0, bank)
             product(block, 4, 1)
         multiply(blocks[1])
         add_and_store(blocks[0])
-        add_on_gpsimd_and_store(blocks[1])
+        add_and_store(blocks[1])
         multiply(blocks[2])
         multiply(blocks[3])
         add_and_store(blocks[2])

@@ -28,9 +28,22 @@ BANKS = 8
 GROUP = 16
 QUADRANT = 32
 SCALE_ROWS = 4
+SECOND = 8
 CHUNK = 128
 ROW_TILES = N // P
 
+KIB = 1024
+LATER = {
+    "tab_sc": 0,
+    "w1_raw100": 0, "w1_bf001": 0, "w1_bf101": 2 * KIB, "stage1": 0,
+    "w1_raw001": 4 * KIB, "w1_raw101": 8 * KIB, "w1_raw010": 12 * KIB, "h02": 12 * KIB,
+    "w1_raw110": 22 * KIB, "z_tile0": 22 * KIB, "z_tile1": 23 * KIB,
+    "w4_raw0": 30 * KIB, "stage_last2": 30 * KIB, "stage_last3": 31 * KIB,
+    "w4_raw1": 38 * KIB, "w3_sb": 46 * KIB, "w2_sb": 50 * KIB, "gain_a": 52 * KIB, "gain_b": 52 * KIB + 64,
+    "diff1_first": 54 * KIB, "z_rows0": 55 * KIB, "z_rows1": 56 * KIB, "w4_bf0": 58 * KIB, "w4_bf1": 57 * KIB, "z_bf1_256": 55 * KIB,
+    "w1_q1100": 64 * KIB, "z_tile2": 64 * KIB - 512, "z_tile3": 64 * KIB + 512,
+}
+LATER_BYTES = 53 * KIB
 HALF = PAIRS // 2
 ALL = (0, PAIRS)
 FIRST, LAST = (0, HALF), (HALF, PAIRS)
@@ -42,94 +55,98 @@ def tile_list_site_pair_couplings_kernel(
     nc = tc.nc
     with ExitStack() as ctx:
         keep = ctx.enter_context(tc.tile_pool(name="keep", bufs=1))
+        later = ctx.enter_context(tc.tile_pool(name="later", bufs=1))
         psum = ctx.enter_context(tc.psum_pool(name="psum", bufs=1))
 
         def sb(name, shape, dtype, tag=""):
+            if (tag or name) in LATER:
+                return later.tile(shape, dtype, name=name, tag=tag or name, align_bytes=64, offset=LATER[tag or name])
             return keep.tile(shape, dtype, name=name, tag=tag or name, align_bytes=64)
 
         offs_sb = sb("offs_sb", [P, S // GROUP], U16)
         pos_sb = [sb("pos1_sb", [P, PAIRS // GROUP], U16), sb("pos2_sb", [P, PAIRS // GROUP], U16)]
         tab = [sb("tab%d" % a, [P, T], I32) for a in range(PASSES)]
-        tab_sc = sb("tab_sc", [P, T], U8)
+        tab_sc = sb("tab_sc", [P, LATER_BYTES], U8)[:, 0:T]
+        picked_sc = sb("picked_sc", [P, S], U8)
         v = {}
         v_sc = sb("v_sc", [P, S], U8)
-        gain_sb = sb("gain_sb", [P, PASSES, PACK], F32)
-        w23_sc = sb("w23_sc", [P, PASSES, N], U8)
+        gain_a = sb("gain_a", [P, 2, PACK], F32)
+        gain_b = sb("gain_b", [P, PACK], F32)
         w2_sb = sb("w2_sb", [P, PASSES, 2 * N], U8)
         w3_sb = sb("w3_sb", [P, PASSES, N], I32)
 
-        nc.vector.memset(tab_sc[:].bitcast(I32), 0)
-        nc.gpsimd.memset(w23_sc[:].bitcast(I32), 0)
+        nc.vector.memset(tab_sc[QUADRANT : 2 * QUADRANT].bitcast(I32), 0)
+        nc.vector.memset(tab_sc[2 * QUADRANT :].bitcast(I32), 0)
+        nc.gpsimd.memset(v_sc[:].bitcast(I32), 0)
 
-        pieces = {(0, 0): 1, (1, 0): 2, (0, 1): 2, (1, 1): 1}
+        pieces = (2, 1)
         w1_raw, w1_bf, w1_q, w1_sc = {}, {}, {}, {}
         for a in range(PASSES):
             for b in range(PASSES):
                 w1_sc[a, b] = sb("w1_sc%d%d" % (a, b), [P, PASS], U8)
 
-        shared = sb("w1_bf_shared", [P, 2 * PACK * PASS - PASS // 2], BF16)
-        w1_bf[1, 0] = shared[:, 0 : PACK * PASS].rearrange("p (t m j) -> p t m j", t=PACK, j=PACK)
-        w1_bf[0, 1] = shared[:, PACK * PASS - PASS // 2 :].rearrange("p (t m j) -> p t m j", t=PACK, j=PACK)
-
         def load_table_words(a):
             nc.sync.dma_start(out=tab[a][:], in_=tab_words[a].rearrange("p c i -> p (c i)").bitcast(I32))
 
-        def load_w1(a, b):
-            width = PASS // pieces[a, b]
-            for piece in (1, 0) if (a, b) == (0, 1) else range(pieces[a, b]):
-                w1_raw[a, b, piece] = sb("w1_raw%d%d%d" % (a, b, piece), [P, PACK, width], F32)
-                channel = PASS * b + width * piece
-                rows = w1[PASS * a : PASS * (a + 1), channel : channel + width]
-                nc.sync.dma_start(out=w1_raw[a, b, piece][:], in_=rows.rearrange("(p j) c -> p j c", j=PACK))
+        def load_w1(a, b, u=0):
+            width = PASS // pieces[b]
+            w1_raw[a, b, u] = sb("w1_raw%d%d%d" % (a, b, u), [P, PACK, width], F32)
+            channel = PASS * b + width * u
+            rows = w1[PASS * a : PASS * (a + 1), channel : channel + width]
+            nc.sync.dma_start(out=w1_raw[a, b, u][:], in_=rows.rearrange("(p j) c -> p j c", j=PACK))
 
-        def round_w1(a, b, m0, m1, copy, tag=""):
-            if (a, b) not in w1_bf:
-                w1_bf[a, b] = sb("w1_bf%d%d" % (a, b), [P, PACK, P, PACK], BF16, tag)[:]
-            count = P // pieces[a, b]
-            raw = w1_raw[a, b, m0 // count][:].rearrange("p j (m t) -> p m j t", t=PACK)
+        def round_w1(a, b, u, copy, tag=""):
+            w1_bf[a, b, u] = sb("w1_bf%d%d%d" % (a, b, u), [P, PACK, P // pieces[b], PACK], BF16, tag)
             copy(
-                out=w1_bf[a, b][:, :, m0:m1, :].rearrange("p t m j -> p m j t"),
-                in_=raw[:, m0 % count : m0 % count + m1 - m0],
+                out=w1_bf[a, b, u][:].rearrange("p t m j -> p m j t"),
+                in_=w1_raw[a, b, u][:].rearrange("p j (m t) -> p m j t", t=PACK),
             )
 
-        def quantize_w1(a, b, t0, t1, tag=""):
-            if t0 == 0:
-                w1_q[a, b] = sb("w1_q%d%d" % (a, b), [P, PASS], U32, tag)
-            cols = slice(P * t0, P * t1)
+        def quantize_w1(a, b, u, i0, i1):
+            codes = sb("w1_q%d%d%d%d" % (a, b, u, i0), [P, P * (i1 - i0)], U32)
+            first = 2 * u
+            for i in range(i0, i1):
+                w1_q[a, b, first + i] = codes[:, P * (i - i0) : P * (i - i0 + 1)]
             nc.vector.quantize_mx(
-                out=w1_q[a, b][:, cols].bitcast(FP8X4),
-                scales=w1_sc[a, b][:, cols],
-                in_=w1_bf[a, b][:, t0:t1].rearrange("p t m j -> p (t m j)"),
+                out=codes[:].bitcast(FP8X4),
+                scales=w1_sc[a, b][:, P * (first + i0) : P * (first + i1)],
+                in_=w1_bf[a, b, u][:].rearrange("p t m j -> p (t m j)")[:, PASS * i0 : PASS * i1],
             )
 
         nc.sync.dma_start(offs_sb[:], offs)
+        for half in range(2):
+            for a in range(PASSES):
+                row = GROUP * half + SECOND * a
+                queue = nc.sync if half == 1 else nc.scalar
+                queue.dma_start(
+                    out=tab_sc[row : row + SECOND, :].bitcast(I32),
+                    in_=tab_scales[a, SECOND * half : SECOND * (half + 1), :].bitcast(I32),
+                )
         load_table_words(0)
-        for q in range(P // QUADRANT):
-            nc.sync.dma_start(
-                out=tab_sc[QUADRANT * q : QUADRANT * q + PASSES * SCALE_ROWS, :].bitcast(I32),
-                in_=tab_scales[:, SCALE_ROWS * q : SCALE_ROWS * (q + 1), :].bitcast(I32),
-            )
-        load_w1(0, 0)
-        load_table_words(1)
-        load_w1(1, 0)
-        load_w1(0, 1)
         nc.sync.dma_start(pos_sb[1][:], pos2)
         nc.sync.dma_start(pos_sb[0][:], pos1)
+        load_w1(0, 0)
+        load_table_words(1)
+        nc.vector.tensor_copy(picked_sc[:], tab_sc.indirect(offs_sb[:]))
+        for q in range(P // QUADRANT):
+            source = GROUP * (q // 2) + SCALE_ROWS * (q % 2)
+            nc.sync.dma_start(
+                out=v_sc[QUADRANT * q : QUADRANT * q + GROUP, :].bitcast(I32),
+                in_=picked_sc[source : source + GROUP, :].bitcast(I32),
+            )
+        load_w1(1, 0, 0)
+        load_w1(0, 0, 1)
+        load_w1(1, 0, 1)
+        load_w1(0, 1)
         load_w1(1, 1)
-        nc.sync.dma_start(out=gain_sb[:], in_=gain.rearrange("(b p t) -> p b t", b=PASSES, t=PACK))
+        by_piece = gain[0:PASS].rearrange("(u m t) -> m u t", u=2, t=PACK)
+        nc.sync.dma_start(out=gain_a[0 : P // 2], in_=by_piece)
+        nc.sync.dma_start(out=gain_a[P // 2 :, :, 0 : PACK - 1], in_=by_piece[:, :, 1:PACK])
+        nc.sync.dma_start(out=gain_b[:], in_=gain[PASS:].rearrange("(p t) -> p t", t=PACK))
         w4_raw = [sb("w4_raw%d" % b, [P, PACK, N], F32) for b in range(PASSES)]
         for b in range(PASSES):
             rows = w4[PASS * b : PASS * (b + 1), :]
             nc.sync.dma_start(out=w4_raw[b][:], in_=rows.rearrange("(p j) c -> p j c", j=PACK))
-        for q in range(P // QUADRANT):
-            for first_row, scales in ((0, w2_scales), (SCALE_ROWS, w3_scales)):
-                row = QUADRANT * q + first_row
-                nc.sync.dma_start(
-                    out=w23_sc[row : row + SCALE_ROWS].bitcast(I32),
-                    in_=scales[:, SCALE_ROWS * q : SCALE_ROWS * (q + 1), :].rearrange("b r n -> r b n").bitcast(I32),
-                )
-        nc.sync.dma_start(out=w2_sb[:].bitcast(I32), in_=w2_words.rearrange("b p n -> p b n").bitcast(I32))
-        nc.sync.dma_start(out=w3_sb[:], in_=w3_words.rearrange("b p n i -> p b (n i)").bitcast(I32))
 
         h = {}
 
@@ -147,19 +164,22 @@ def tile_list_site_pair_couplings_kernel(
                 for a in range(PASSES):
                     nc.tensor.matmul_mx(
                         out=acc[:],
-                        lhsT=w1_q[a, b][:, cols].bitcast(FP8X4),
+                        lhsT=w1_q[a, b, t].bitcast(FP8X4),
                         lhsT_scale=w1_sc[a, b][:, cols],
                         rhs=v[a][:, sites].bitcast(FP8X4),
-                        rhs_scale=v_sc[SCALE_ROWS * a :, sites],
+                        rhs_scale=v_sc[SECOND * a :, sites],
                         start=(a == 0),
                         stop=(a == PASSES - 1),
                     )
                 nc.scalar.activation(out=h[b, t][:, sites], in_=acc[:], func=TANH)
 
-        z_q = [sb("z_q%d" % b, [P, PAIRS], U32) for b in range(PASSES)]
         z_sc = [sb("z_sc%d" % b, [P, PAIRS], U8) for b in range(PASSES)]
-        diff0 = {t: sb("diff0%d" % t, [P, PAIRS], F32) for t in (2, 3)}
-        diff1 = sb("diff1", [P, PACK, PAIRS], F32)
+        whole = sb("z_q0", [P, PAIRS], U32)
+        z_q = {(0, half): whole[:, HALF * half : HALF * (half + 1)] for half in range(2)}
+        for half in range(2):
+            z_q[1, half] = sb("z_q1%d" % half, [P, HALF], U32)[:]
+        diff0 = {}
+        diff1 = sb("diff1", [P, PACK, PAIRS], F32, "w1_sc11")
         z_bf = {}
 
 
@@ -170,15 +190,17 @@ def tile_list_site_pair_couplings_kernel(
                 return diff0[t][:, run[0] : run[1]]
             if t >= 2 and run == FIRST:
                 if not late:
-                    late[0] = sb("diff1_first", [P, 2, HALF], F32, "z_bf0_0")
+                    late[0] = sb("diff1_first", [P, 2, HALF], F32)
                 return late[0][:, t - 2, :]
             return diff1[:, t, run[0] : run[1]]
 
-        def differences(b, parts, stage):
+        def differences(b, parts, stage, between=None):
             for i, (t, (c0, c1)) in enumerate(parts):
                 nc.vector.tensor_copy(
                     stage[i][:, :], h[b, t][:].indirect(pos_sb[1][:, c0 // GROUP : c1 // GROUP])
                 )
+            if between:
+                between()
             for i, (t, (c0, c1)) in enumerate(parts):
                 nc.vector.tensor_tensor(
                     diff_row(b, t, (c0, c1)),
@@ -193,7 +215,7 @@ def tile_list_site_pair_couplings_kernel(
             nc.vector.tensor_tensor(
                 z_bf[b, run][:].rearrange("p (c i) t -> p c t i", i=2),
                 diff1[:, :, c0:c1].rearrange("p t (c i) -> p c t i", i=2),
-                gain_sb[:, b, :].unsqueeze(1).unsqueeze(3).to_broadcast([P, (c1 - c0) // 2, PACK, 2]),
+                gain_b[:].unsqueeze(1).unsqueeze(3).to_broadcast([P, (c1 - c0) // 2, PACK, 2]),
                 MULT,
             )
 
@@ -201,7 +223,17 @@ def tile_list_site_pair_couplings_kernel(
 
         def scale_on_scalar(b, run, t):
             source = diff_row(b, t, run)
-            nc.scalar.activation(out=z_rows[b, run][:, t, :], in_=source, func=COPY, scale=gain_sb[:, b, t : t + 1])
+            nc.scalar.activation(out=z_rows[b, run][:, t, :], in_=source, func=COPY, scale=gain_b[:, t : t + 1])
+
+        def scale_and_move(i):
+            u, s = divmod(i, 2)
+            z_tile = sb("z_tile%d" % i, [P, PAIRS], BF16)
+            nc.scalar.activation(out=z_tile[:], in_=diff0[i][:], func=COPY, scale=gain_a[:, u, 2 * s : 2 * s + 1])
+            for e in range(2):
+                nc.sync.dma_start(
+                    out=z_rows[0, ALL][P // 2 * u : P // 2 * (u + 1), 2 * s + e, :],
+                    in_=z_tile[P // 2 * e : P // 2 * (e + 1), :],
+                )
 
         def interleave_on_scalar(b, held, run):
             z_bf[b, run] = sb("z_bf%d_%d" % (b, run[0]), [P, run[1] - run[0], PACK], BF16)
@@ -213,7 +245,7 @@ def tile_list_site_pair_couplings_kernel(
         def quantize_z(b, run):
             cols = slice(run[0], run[1])
             nc.vector.quantize_mx(
-                out=z_q[b][:, cols].bitcast(FP8X4),
+                out=(whole[:] if b == 0 else z_q[b, run[0] // HALF][:, run[0] % HALF : run[0] % HALF + run[1] - run[0]]).bitcast(FP8X4),
                 scales=z_sc[b][:, cols],
                 in_=z_bf[b, run][:].rearrange("p c t -> p (c t)"),
             )
@@ -230,10 +262,13 @@ def tile_list_site_pair_couplings_kernel(
                 in_=w4_raw[b][:, :, n0:n1].rearrange("p j (c i) -> p c j i", i=4),
             )
 
-        def quantize_w4(b, tag=""):
-            w4_q[b] = sb("w4_q%d" % b, [P, N], U32, tag)
+        def quantize_w4(b, n0=0, n1=N):
+            if n0 == 0:
+                w4_q[b] = sb("w4_q%d" % b, [P, N], U32)
             nc.vector.quantize_mx(
-                out=w4_q[b][:].bitcast(FP8X4), scales=w4_sc[b][:], in_=w4_bf[b][:].rearrange("p c j -> p (c j)")
+                out=w4_q[b][:, n0:n1].bitcast(FP8X4),
+                scales=w4_sc[b][:, n0:n1],
+                in_=w4_bf[b][:, n0:n1, :].rearrange("p c j -> p (c j)"),
             )
 
         def weights(which, b, tile):
@@ -259,14 +294,15 @@ def tile_list_site_pair_couplings_kernel(
                     out=acc[:, at : at + width],
                     lhsT=codes,
                     lhsT_scale=scales,
-                    rhs=z_q[b][:, cols].bitcast(FP8X4),
+                    rhs=z_q[b, half][:, at % HALF : at % HALF + width].bitcast(FP8X4),
                     rhs_scale=z_sc[b][:, cols],
                     start=(b == 0 and at == 0),
                     stop=(b == PASSES - 1 and at + width == BANK),
                 )
-            if which == 2 and b == PASSES - 1:
-                y2_sb[block] = sb("y2_sb%d%d" % block, [P, BANK], F32)
-                nc.scalar.copy(out=y2_sb[block][:], in_=acc[:])
+
+        def copy_y2(block):
+            y2_sb[block] = sb("y2_sb%d%d" % block, [P, BANK], F32)
+            nc.scalar.copy(out=y2_sb[block][:], in_=y[block, 2][:])
 
         def multiply(block):
             y23[block] = sb("y23_%d%d" % block, [P, BANK], F32)
@@ -280,6 +316,11 @@ def tile_list_site_pair_couplings_kernel(
                 nc.vector.tensor_tensor(result[:], y[block, 4][:, at : at + width], y23[block][:, at : at + width], ADD)
                 store(block, result, at, width)
 
+        def add_on_gpsimd(block):
+            result = sb("result%d%d" % block, [P, BANK], F32)
+            nc.gpsimd.tensor_tensor(result[:], y4_sb[:], y23[block][:], ADD)
+            store(block, result, 0, BANK)
+
         def store(block, result, at, width):
             half, u = block
             row = HALF * u + at // HALF * P
@@ -289,81 +330,106 @@ def tile_list_site_pair_couplings_kernel(
             )
 
         gather_table_words(0)
-        nc.vector.tensor_copy(v_sc[:], tab_sc[:].indirect(offs_sb[:]))
-        round_w1(0, 0, 0, P, nc.scalar.copy)
-        quantize_w1(0, 0, 0, PACK)
-        gather_table_words(1, "w1_bf00")
-        round_w1(1, 0, 0, P // 2, nc.scalar.copy)
-        round_w1(1, 0, P // 2, P, nc.scalar.copy)
-        quantize_w1(1, 0, 0, 1)
-        quantize_w1(1, 0, 1, 2)
-        quantize_w1(1, 0, 2, PACK)
+        round_w1(0, 0, 0, nc.scalar.copy)
+        quantize_w1(0, 0, 0, 0, 2)
+        w23_sc = sb("w23_sc", [P, PASSES, N], U8, "w1_raw000")
+        nc.vector.memset(w23_sc[:].bitcast(I32), 0)
+        for q in range(P // QUADRANT):
+            for first_row, scales in ((0, w2_scales), (SCALE_ROWS, w3_scales)):
+                row = QUADRANT * q + first_row
+                nc.sync.dma_start(
+                    out=w23_sc[row : row + SCALE_ROWS].bitcast(I32),
+                    in_=scales[:, SCALE_ROWS * q : SCALE_ROWS * (q + 1), :].rearrange("b r n -> r b n").bitcast(I32),
+                )
+        nc.sync.dma_start(out=w2_sb[:].bitcast(I32), in_=w2_words.rearrange("b p n -> p b n").bitcast(I32))
+        nc.sync.dma_start(out=w3_sb[:], in_=w3_words.rearrange("b p n i -> p b (n i)").bitcast(I32))
 
-        round_w1(0, 1, P // 2, P, nc.scalar.copy)
-        round_w1(0, 1, 0, P // 2, nc.vector.tensor_copy)
-        quantize_w1(0, 1, 0, PACK)
+        gather_table_words(1, "w1_bf000")
+        round_w1(1, 0, 0, nc.scalar.copy)
+        quantize_w1(1, 0, 0, 0, 1)
+        quantize_w1(1, 0, 0, 1, 2)
+        round_w1(0, 0, 1, nc.scalar.copy)
+        round_w1(1, 0, 1, nc.vector.tensor_copy)
+        quantize_w1(0, 0, 1, 0, 2)
+        quantize_w1(1, 0, 1, 0, 2)
+
         def stage(name, width, tag=""):
             both = sb(name, [P, 2, width], F32, tag)
             return [both[:, i, :] for i in range(2)]
 
-        for t in range(PACK - 1):
-            embed(0, t)
-        round_w1(1, 1, 0, P, nc.scalar.copy, "w1_raw011")
+        embed(0, 0)
+        embed(0, 1)
+        round_w1(0, 1, 0, nc.scalar.copy, "w1_q1001")
+        embed(0, 2)
         embed(0, 3)
-        diff0[0] = sb("diff00", [P, PAIRS], F32, "w1_q00")
-        diff0[1] = sb("diff01", [P, PAIRS], F32, "w1_sc00")
+        round_w1(1, 1, 0, nc.scalar.copy)
+        diff0[0] = sb("diff00", [P, PAIRS], F32, "w1_q0010")
+        diff0[1] = sb("diff01", [P, PAIRS], F32, "w1_q1010")
         differences(0, [(0, ALL), (1, ALL)], stage("stage1", PAIRS))
-        quantize_w1(1, 1, 0, PACK)
-        scale_on_scalar(0, ALL, 0)
-        differences(0, [(2, ALL), (3, ALL)], stage("stage_a", PAIRS, "w1_q00"))
-        round_w4(0, 0, N, "stage1")
-        quantize_w4(0)
+        quantize_w1(0, 1, 0, 0, PACK)
+        scale_and_move(0)
+        scale_and_move(1)
+        diff0[2] = sb("diff02", [P, PAIRS], F32, "w1_q0010")
+        diff0[3] = sb("diff03", [P, PAIRS], F32, "w1_q1010")
+
+        def quantize_second_channels():
+            quantize_w1(1, 1, 0, 0, 2)
+            quantize_w1(1, 1, 0, 2, PACK)
+
+        differences(0, [(2, ALL), (3, ALL)], stage("stage_a", PAIRS), quantize_second_channels)
         embed(1, 0)
         embed(1, 1)
-        scale_on_scalar(0, ALL, 1)
+        scale_and_move(2)
+        scale_and_move(3)
         embed(1, 2)
         embed(1, 3)
-        scale_on_scalar(0, ALL, 2)
-        scale_on_scalar(0, ALL, 3)
-        round_w4(1, 0, N // 4)
         interleave_on_scalar(0, ALL, ALL)
-        round_w4(1, N // 4, N)
+        round_w4(0, 0, N)
 
-        differences(1, [(0, ALL), (1, ALL)], stage("stage_b", PAIRS, "w1_sc00"))
-        quantize_z(0, ALL)
+        differences(1, [(0, ALL), (1, ALL)], stage("stage_b", PAIRS))
+        differences(1, [(2, FIRST), (3, FIRST)], stage("stage_first", HALF), lambda: quantize_z(0, ALL))
+        quantize_w4(0)
         blocks = [(half, u) for half in range(2) for u in range(2)]
         for bank in range(BANKS):
             product(blocks[bank // 3], 2 + bank % 3, 0, bank)
-        for run in (FIRST, LAST):
-            tiles = [sb("stage_%d_%d" % (run[0], t), [P, HALF], F32, "diff0%d" % t) for t in (2, 3)]
-            differences(1, [(2, run), (3, run)], tiles)
+        differences(1, [(2, LAST), (3, LAST)], [sb("stage_last%d" % t, [P, HALF], F32) for t in (2, 3)])
         for t in range(PACK):
             scale_on_scalar(1, FIRST, t)
         for quarter in ((0, CHUNK), (CHUNK, HALF)):
             interleave_on_scalar(1, FIRST, quarter)
+        round_w4(1, 0, N // 2)
+        round_w4(1, N // 2, 3 * N // 4)
         for quarter in ((0, CHUNK), (CHUNK, HALF)):
             quantize_z(1, quarter)
-        quantize_w4(1, "z_bf1_0")
         for block in blocks[:2]:
             for which in (2, 3):
                 product(block, which, 1)
-        for block in blocks[:2]:
-            product(block, 4, 1)
-        scale_on_vector(1, LAST, "z_bf1_128")
-        multiply(blocks[0])
+            copy_y2(block)
+        round_w4(1, 3 * N // 4, N)
+        scale_on_vector(1, LAST, "")
+        quantize_w4(1, 0, N // 2)
+        product(blocks[0], 4, 1)
         product(blocks[3], 2, 0, 0)
         product(blocks[3], 3, 0, 3)
         quantize_z(1, LAST)
         for which in (2, 3):
             for block in blocks[2:]:
                 product(block, which, 1)
-        for block, bank in ((blocks[2], 1), (blocks[3], 4)):
-            product(block, 4, 0, bank)
-            product(block, 4, 1)
+        copy_y2(blocks[2])
+        y4_sb = sb("y4_sb", [P, BANK], F32)
+        nc.scalar.copy(out=y4_sb[:], in_=y[blocks[0], 4][:])
+        copy_y2(blocks[3])
+        multiply(blocks[0])
         multiply(blocks[1])
-        add_and_store(blocks[0])
-        add_and_store(blocks[1])
+        quantize_w4(1, N // 2, N)
+        product(blocks[1], 4, 1)
+        product(blocks[2], 4, 0, 1)
+        product(blocks[2], 4, 1)
+        product(blocks[3], 4, 0, 4)
+        product(blocks[3], 4, 1)
         multiply(blocks[2])
+        add_and_store(blocks[1])
+        add_on_gpsimd(blocks[0])
         multiply(blocks[3])
         add_and_store(blocks[2])
         add_and_store(blocks[3], 2)

@@ -28,7 +28,6 @@ BANKS = 8
 GROUP = 16
 QUADRANT = 32
 SCALE_ROWS = 4
-SECOND = 8
 CHUNK = 128
 ROW_TILES = N // P
 
@@ -114,14 +113,11 @@ def tile_list_site_pair_couplings_kernel(
             )
 
         nc.sync.dma_start(offs_sb[:], offs)
-        for half in range(2):
-            for a in range(PASSES):
-                row = GROUP * half + SECOND * a
-                queue = nc.sync if half == 1 else nc.scalar
-                queue.dma_start(
-                    out=tab_sc[row : row + SECOND, :].bitcast(I32),
-                    in_=tab_scales[a, SECOND * half : SECOND * (half + 1), :].bitcast(I32),
-                )
+        for a, queue in enumerate((nc.scalar, nc.sync)):
+            queue.dma_start(
+                out=tab_sc[GROUP * a : GROUP * (a + 1), :].bitcast(I32),
+                in_=tab_scales[a].bitcast(I32).rearrange("(q r) c -> r q c", r=SCALE_ROWS),
+            )
         load_table_words(0)
         nc.sync.dma_start(pos_sb[1][:], pos2)
         nc.sync.dma_start(pos_sb[0][:], pos1)
@@ -129,10 +125,9 @@ def tile_list_site_pair_couplings_kernel(
         load_table_words(1)
         nc.vector.tensor_copy(picked_sc[:], tab_sc.indirect(offs_sb[:]))
         for q in range(P // QUADRANT):
-            source = GROUP * (q // 2) + SCALE_ROWS * (q % 2)
             nc.sync.dma_start(
-                out=v_sc[QUADRANT * q : QUADRANT * q + GROUP, :].bitcast(I32),
-                in_=picked_sc[source : source + GROUP, :].bitcast(I32),
+                out=v_sc[QUADRANT * q : QUADRANT * q + PASSES * SCALE_ROWS, :].bitcast(I32),
+                in_=picked_sc[q:QUADRANT:SCALE_ROWS, :].bitcast(I32),
             )
         load_w1(1, 0, 0)
         load_w1(0, 0, 1)
@@ -167,7 +162,7 @@ def tile_list_site_pair_couplings_kernel(
                         lhsT=w1_q[a, b, t].bitcast(FP8X4),
                         lhsT_scale=w1_sc[a, b][:, cols],
                         rhs=v[a][:, sites].bitcast(FP8X4),
-                        rhs_scale=v_sc[SECOND * a :, sites],
+                        rhs_scale=v_sc[SCALE_ROWS * a :, sites],
                         start=(a == 0),
                         stop=(a == PASSES - 1),
                     )

@@ -68,7 +68,7 @@ def tile_list_site_pair_couplings_kernel(
         tab_sc = sb("tab_sc", [P, LATER_BYTES], U8)[:, 0:T]
         picked_sc = sb("picked_sc", [P, S], U8)
         v = {}
-        v_sc = sb("v_sc", [P, S], U8)
+        v_sc = sb("v_sc", [P, PASSES, S], U8)
         gain_a = sb("gain_a", [P, 2, PACK], F32)
         gain_b = sb("gain_b", [P, PACK], F32)
         w2_sb = sb("w2_sb", [P, PASSES, 2 * N], U8)
@@ -113,11 +113,9 @@ def tile_list_site_pair_couplings_kernel(
             )
 
         nc.sync.dma_start(offs_sb[:], offs)
-        for a, queue in enumerate((nc.scalar, nc.sync)):
-            queue.dma_start(
-                out=tab_sc[GROUP * a : GROUP * (a + 1), :].bitcast(I32),
-                in_=tab_scales[a].bitcast(I32).rearrange("(q r) c -> r q c", r=SCALE_ROWS),
-            )
+        nc.scalar.dma_start(
+            out=tab_sc[0:QUADRANT, :].bitcast(I32), in_=tab_scales.bitcast(I32).rearrange("a row c -> row a c")
+        )
         load_table_words(0)
         nc.sync.dma_start(pos_sb[1][:], pos2)
         nc.sync.dma_start(pos_sb[0][:], pos1)
@@ -126,8 +124,8 @@ def tile_list_site_pair_couplings_kernel(
         nc.vector.tensor_copy(picked_sc[:], tab_sc.indirect(offs_sb[:]))
         for q in range(P // QUADRANT):
             nc.sync.dma_start(
-                out=v_sc[QUADRANT * q : QUADRANT * q + PASSES * SCALE_ROWS, :].bitcast(I32),
-                in_=picked_sc[q:QUADRANT:SCALE_ROWS, :].bitcast(I32),
+                out=v_sc[QUADRANT * q : QUADRANT * q + SCALE_ROWS].bitcast(I32),
+                in_=picked_sc[PASSES * SCALE_ROWS * q : PASSES * SCALE_ROWS * (q + 1), :].bitcast(I32),
             )
         load_w1(1, 0, 0)
         load_w1(0, 0, 1)
@@ -162,7 +160,7 @@ def tile_list_site_pair_couplings_kernel(
                         lhsT=w1_q[a, b, t].bitcast(FP8X4),
                         lhsT_scale=w1_sc[a, b][:, cols],
                         rhs=v[a][:, sites].bitcast(FP8X4),
-                        rhs_scale=v_sc[SCALE_ROWS * a :, sites],
+                        rhs_scale=v_sc[:, a, sites],
                         start=(a == 0),
                         stop=(a == PASSES - 1),
                     )
@@ -281,7 +279,7 @@ def tile_list_site_pair_couplings_kernel(
             if b == 0:
                 y[block, which] = psum.tile([P, BANK], F32, name="y%d%d%d" % (half, u, which), tag="bank%d" % bank)
             acc = y[block, which]
-            width = CHUNK if which == 2 else HALF
+            width = HALF
             for at in range(0, BANK, width):
                 codes, scales = weights(which, b, 2 * u + at // HALF)
                 cols = slice(HALF * half + at % HALF, HALF * half + at % HALF + width)
@@ -328,7 +326,6 @@ def tile_list_site_pair_couplings_kernel(
         round_w1(0, 0, 0, nc.scalar.copy)
         quantize_w1(0, 0, 0, 0, 2)
         w23_sc = sb("w23_sc", [P, PASSES, N], U8, "w1_raw000")
-        nc.vector.memset(w23_sc[:].bitcast(I32), 0)
         for q in range(P // QUADRANT):
             for first_row, scales in ((0, w2_scales), (SCALE_ROWS, w3_scales)):
                 row = QUADRANT * q + first_row

@@ -36,11 +36,10 @@ LATER = {
     "tab_sc": 0,
     "w1_raw100": 0, "w1_bf001": 0, "w1_bf101": 2 * KIB, "stage1": 0,
     "w1_raw001": 4 * KIB, "w1_raw101": 8 * KIB, "w1_raw010": 12 * KIB, "h02": 12 * KIB,
-    "w1_raw110": 22 * KIB, "z_tile0": 22 * KIB, "z_tile1": 23 * KIB,
-    "w4_raw0": 30 * KIB, "stage_last2": 30 * KIB, "stage_last3": 31 * KIB,
+    "w1_raw110": 22 * KIB, "diff02": 22 * KIB, "diff03": 24 * KIB,
+    "w4_raw0": 30 * KIB,
     "w4_raw1": 38 * KIB, "w3_sb": 46 * KIB, "w2_sb": 50 * KIB, "gain_a": 52 * KIB, "gain_b": 52 * KIB + 64,
-    "diff1_first": 54 * KIB, "z_rows0": 55 * KIB, "z_rows1": 56 * KIB, "w4_bf0": 58 * KIB, "w4_bf1": 57 * KIB, "z_bf1_256": 55 * KIB,
-    "w1_q1100": 64 * KIB, "z_tile2": 64 * KIB - 512, "z_tile3": 64 * KIB + 512,
+    "diff1_first": 53 * KIB + 64, "z_rows0": 55 * KIB, "z_rows1": 55 * KIB + 64, "w4_bf0_0": 26 * KIB, "w4_bf1_0": 58 * KIB + 64,
 }
 LATER_BYTES = 53 * KIB
 HALF = PAIRS // 2
@@ -69,7 +68,7 @@ def tile_list_site_pair_couplings_kernel(
         picked_sc = sb("picked_sc", [P, S], U8)
         v = {}
         v_sc = sb("v_sc", [P, PASSES, S], U8)
-        gain_a = sb("gain_a", [P, 2, PACK], F32)
+        gain_a = sb("gain_a", [P, PACK], F32)
         gain_b = sb("gain_b", [P, PACK], F32)
         w2_sb = sb("w2_sb", [P, PASSES, 2 * N], U8)
         w3_sb = sb("w3_sb", [P, PASSES, N], I32)
@@ -95,7 +94,19 @@ def tile_list_site_pair_couplings_kernel(
             nc.sync.dma_start(out=w1_raw[a, b, u][:], in_=rows.rearrange("(p j) c -> p j c", j=PACK))
 
         def round_w1(a, b, u, copy, tag=""):
-            w1_bf[a, b, u] = sb("w1_bf%d%d%d" % (a, b, u), [P, PACK, P // pieces[b], PACK], BF16, tag)
+            if b == 0:
+                w1_bf[a, b, u] = sb("w1_bf%d%d%d" % (a, b, u), [P, HALF, PACK], BF16, tag)
+                if copy is None:
+                    nc.gpsimd.tensor_scalar(
+                        w1_bf[a, b, u][:], w1_raw[a, b, u][:].rearrange("p j c -> p c j"), 1.0, 0.0, MULT, ADD
+                    )
+                    return
+                copy(
+                    out=w1_bf[a, b, u][:].rearrange("p (c i) j -> p c j i", i=4),
+                    in_=w1_raw[a, b, u][:].rearrange("p j (c i) -> p c j i", i=4),
+                )
+                return
+            w1_bf[a, b, u] = sb("w1_bf%d%d%d" % (a, b, u), [P, PACK, P, PACK], BF16, tag)
             copy(
                 out=w1_bf[a, b, u][:].rearrange("p t m j -> p m j t"),
                 in_=w1_raw[a, b, u][:].rearrange("p j (m t) -> p m j t", t=PACK),
@@ -109,7 +120,7 @@ def tile_list_site_pair_couplings_kernel(
             nc.vector.quantize_mx(
                 out=codes[:].bitcast(FP8X4),
                 scales=w1_sc[a, b][:, P * (first + i0) : P * (first + i1)],
-                in_=w1_bf[a, b, u][:].rearrange("p t m j -> p (t m j)")[:, PASS * i0 : PASS * i1],
+                in_=w1_bf[a, b, u][:].rearrange("p c j -> p (c j)" if b == 0 else "p t m j -> p (t m j)")[:, PASS * i0 : PASS * i1],
             )
 
         nc.sync.dma_start(offs_sb[:], offs)
@@ -132,9 +143,8 @@ def tile_list_site_pair_couplings_kernel(
         load_w1(1, 0, 1)
         load_w1(0, 1)
         load_w1(1, 1)
-        by_piece = gain[0:PASS].rearrange("(u m t) -> m u t", u=2, t=PACK)
-        nc.sync.dma_start(out=gain_a[0 : P // 2], in_=by_piece)
-        nc.sync.dma_start(out=gain_a[P // 2 :, :, 0 : PACK - 1], in_=by_piece[:, :, 1:PACK])
+        with nc.allow_non_contiguous_dma(reason="one gain for each partition and tile"):
+            nc.sync.dma_start(out=gain_a[:], in_=gain[0:PASS].rearrange("(i m) -> m i", m=P))
         nc.sync.dma_start(out=gain_b[:], in_=gain[PASS:].rearrange("(p t) -> p t", t=PACK))
         w4_raw = [sb("w4_raw%d" % b, [P, PACK, N], F32) for b in range(PASSES)]
         for b in range(PASSES):
@@ -202,37 +212,34 @@ def tile_list_site_pair_couplings_kernel(
                     SUB,
                 )
 
-        def scale_on_vector(b, run, tag):
-            c0, c1 = run
-            z_bf[b, run] = sb("z_bf%d_%d" % (b, c0), [P, c1 - c0, PACK], BF16, tag)
-            nc.vector.tensor_tensor(
-                z_bf[b, run][:].rearrange("p (c i) t -> p c t i", i=2),
-                diff1[:, :, c0:c1].rearrange("p t (c i) -> p c t i", i=2),
-                gain_b[:].unsqueeze(1).unsqueeze(3).to_broadcast([P, (c1 - c0) // 2, PACK, 2]),
-                MULT,
-            )
-
-        z_rows = {(b, run): sb("z_rows%d" % b, [P, PACK, run[1]], BF16) for b, run in ((0, ALL), (1, FIRST))}
+        shared = sb("z_rows1", [P, PACK + 2, HALF], BF16)
+        z_rows = {(0, ALL): sb("z_rows0", [P, PACK, PAIRS], BF16), (1, FIRST): shared[:, 2:, :], (1, LAST): shared[:, :PACK, :]}
 
         def scale_on_scalar(b, run, t):
             source = diff_row(b, t, run)
             nc.scalar.activation(out=z_rows[b, run][:, t, :], in_=source, func=COPY, scale=gain_b[:, t : t + 1])
 
+        z_pair = {}
+
         def scale_and_move(i):
-            u, s = divmod(i, 2)
-            z_tile = sb("z_tile%d" % i, [P, PAIRS], BF16)
-            nc.scalar.activation(out=z_tile[:], in_=diff0[i][:], func=COPY, scale=gain_a[:, u, 2 * s : 2 * s + 1])
-            for e in range(2):
-                nc.sync.dma_start(
-                    out=z_rows[0, ALL][P // 2 * u : P // 2 * (u + 1), 2 * s + e, :],
-                    in_=z_tile[P // 2 * e : P // 2 * (e + 1), :],
-                )
+            if i % 2 == 0:
+                z_pair[i // 2] = sb("z_pair%d" % i, [P, 2 * PAIRS], BF16, "w1_q1001" if i == 0 else "")
+            z_tile = z_pair[i // 2][:, PAIRS * (i % 2) : PAIRS * (i % 2 + 1)]
+            nc.gpsimd.tensor_scalar(z_tile, diff0[i][:], gain_a[:, i : i + 1], 0.0, MULT, ADD)
+            nc.sync.dma_start(out=z_rows[0, ALL][QUADRANT * i : QUADRANT * (i + 1)], in_=z_tile)
 
         def interleave_on_scalar(b, held, run):
             z_bf[b, run] = sb("z_bf%d_%d" % (b, run[0]), [P, run[1] - run[0], PACK], BF16)
             nc.scalar.copy(
                 out=z_bf[b, run][:].rearrange("p (c i) t -> p c t i", i=4),
                 in_=z_rows[b, held][:, :, run[0] : run[1]].rearrange("p t (c i) -> p c t i", i=4),
+            )
+
+        def interleave_on_vector(b, run):
+            z_bf[b, run] = sb("z_bf%d_%d" % (b, run[0]), [P, run[1] - run[0], PACK], BF16)
+            nc.vector.tensor_copy(
+                out=z_bf[b, run][:].rearrange("p (c i) t -> p c t i", i=4),
+                in_=z_rows[b, run].rearrange("p t (c i) -> p c t i", i=4),
             )
 
         def quantize_z(b, run):
@@ -248,20 +255,19 @@ def tile_list_site_pair_couplings_kernel(
         w4_sc = [sb("w4_sc%d" % b, [P, N], U8) for b in range(PASSES)]
 
         def round_w4(b, n0, n1, tag=""):
-            if n0 == 0:
-                w4_bf[b] = sb("w4_bf%d" % b, [P, N, PACK], BF16, tag)
+            w4_bf[b, n0] = sb("w4_bf%d_%d" % (b, n0), [P, n1 - n0, PACK], BF16, tag)
             nc.scalar.copy(
-                out=w4_bf[b][:, n0:n1, :].rearrange("p (c i) j -> p c j i", i=4),
+                out=w4_bf[b, n0][:].rearrange("p (c i) j -> p c j i", i=4),
                 in_=w4_raw[b][:, :, n0:n1].rearrange("p j (c i) -> p c j i", i=4),
             )
 
         def quantize_w4(b, n0=0, n1=N):
             if n0 == 0:
-                w4_q[b] = sb("w4_q%d" % b, [P, N], U32)
+                w4_q[b] = sb("w4_q%d" % b, [P, N], U32, "z_bf0_0" if b == 1 else "stage_b")
             nc.vector.quantize_mx(
                 out=w4_q[b][:, n0:n1].bitcast(FP8X4),
                 scales=w4_sc[b][:, n0:n1],
-                in_=w4_bf[b][:, n0:n1, :].rearrange("p c j -> p (c j)"),
+                in_=(w4_bf[0, n0][:] if b == 0 else w4_bf[1, 0][:, n0:n1, :]).rearrange("p c j -> p (c j)"),
             )
 
         def weights(which, b, tile):
@@ -355,14 +361,15 @@ def tile_list_site_pair_couplings_kernel(
         embed(0, 2)
         embed(0, 3)
         round_w1(1, 1, 0, nc.scalar.copy)
+        round_w4(0, 0, N // 2)
         diff0[0] = sb("diff00", [P, PAIRS], F32, "w1_q0010")
         diff0[1] = sb("diff01", [P, PAIRS], F32, "w1_q1010")
         differences(0, [(0, ALL), (1, ALL)], stage("stage1", PAIRS))
         quantize_w1(0, 1, 0, 0, PACK)
         scale_and_move(0)
         scale_and_move(1)
-        diff0[2] = sb("diff02", [P, PAIRS], F32, "w1_q0010")
-        diff0[3] = sb("diff03", [P, PAIRS], F32, "w1_q1010")
+        diff0[2] = sb("diff02", [P, PAIRS], F32)
+        diff0[3] = sb("diff03", [P, PAIRS], F32)
 
         def quantize_second_channels():
             quantize_w1(1, 1, 0, 0, 2)
@@ -375,53 +382,54 @@ def tile_list_site_pair_couplings_kernel(
         scale_and_move(3)
         embed(1, 2)
         embed(1, 3)
+        round_w4(0, N // 2, N, "w1_q1102")
         interleave_on_scalar(0, ALL, ALL)
-        round_w4(0, 0, N)
 
         differences(1, [(0, ALL), (1, ALL)], stage("stage_b", PAIRS))
         differences(1, [(2, FIRST), (3, FIRST)], stage("stage_first", HALF), lambda: quantize_z(0, ALL))
-        quantize_w4(0)
+        quantize_w4(0, 0, N // 2)
+        quantize_w4(0, N // 2, N)
         blocks = [(half, u) for half in range(2) for u in range(2)]
         for bank in range(BANKS):
             product(blocks[bank // 3], 2 + bank % 3, 0, bank)
-        differences(1, [(2, LAST), (3, LAST)], [sb("stage_last%d" % t, [P, HALF], F32) for t in (2, 3)])
-        for t in range(PACK):
-            scale_on_scalar(1, FIRST, t)
+        differences(1, [(2, LAST), (3, LAST)], stage("stage_last", HALF, "z_bf0_0"))
+        round_w4(1, 0, N)
+        for run, t in ((FIRST, 0), (FIRST, 1), (LAST, 0), (LAST, 1), (FIRST, 2), (FIRST, 3)):
+            scale_on_scalar(1, run, t)
         for quarter in ((0, CHUNK), (CHUNK, HALF)):
             interleave_on_scalar(1, FIRST, quarter)
-        round_w4(1, 0, N // 2)
-        round_w4(1, N // 2, 3 * N // 4)
+        for t in (2, 3):
+            scale_on_scalar(1, LAST, t)
         for quarter in ((0, CHUNK), (CHUNK, HALF)):
             quantize_z(1, quarter)
         for block in blocks[:2]:
             for which in (2, 3):
                 product(block, which, 1)
             copy_y2(block)
-        round_w4(1, 3 * N // 4, N)
-        scale_on_vector(1, LAST, "")
         quantize_w4(1, 0, N // 2)
         product(blocks[0], 4, 1)
+        interleave_on_vector(1, LAST)
+        quantize_w4(1, N // 2, N)
+        product(blocks[1], 4, 1)
         product(blocks[3], 2, 0, 0)
         product(blocks[3], 3, 0, 3)
         quantize_z(1, LAST)
         for which in (2, 3):
             for block in blocks[2:]:
                 product(block, which, 1)
-        copy_y2(blocks[2])
         y4_sb = sb("y4_sb", [P, BANK], F32)
         nc.scalar.copy(out=y4_sb[:], in_=y[blocks[0], 4][:])
+        copy_y2(blocks[2])
         copy_y2(blocks[3])
         multiply(blocks[0])
         multiply(blocks[1])
-        quantize_w4(1, N // 2, N)
-        product(blocks[1], 4, 1)
         product(blocks[2], 4, 0, 1)
         product(blocks[2], 4, 1)
         product(blocks[3], 4, 0, 4)
         product(blocks[3], 4, 1)
-        multiply(blocks[2])
-        add_and_store(blocks[1])
         add_on_gpsimd(blocks[0])
+        add_and_store(blocks[1])
+        multiply(blocks[2])
         multiply(blocks[3])
         add_and_store(blocks[2])
         add_and_store(blocks[3], 2)

@@ -24,27 +24,28 @@ PACK = 4
 PASS = P * PACK
 PASSES = 2
 BANK = 512
-BANKS = 8
 GROUP = 16
 QUADRANT = 32
 SCALE_ROWS = 4
-CHUNK = 128
-ROW_TILES = N // P
+HALF = PAIRS // 2
+LINE = 4
 
 KIB = 1024
-LATER = {
+STEP = 64
+PLACE = {
     "tab_sc": 0,
-    "w1_raw100": 0, "w1_bf001": 0, "w1_bf101": 2 * KIB, "stage1": 0,
-    "w1_raw001": 4 * KIB, "w1_raw101": 8 * KIB, "w1_raw010": 12 * KIB, "h02": 12 * KIB,
-    "w1_raw110": 22 * KIB, "diff02": 22 * KIB, "diff03": 24 * KIB,
+    "w1_raw10": 0, "w1_bf01": 0, "w1_bf11": 2 * KIB, "second01": 0,
+    "w1_raw01": 4 * KIB, "w1_raw11": 8 * KIB,
+    "w1_raw0b": 12 * KIB, "h2": 12 * KIB,
+    "w1_raw1b": 22 * KIB, "diff2": 22 * KIB, "diff3": 24 * KIB, "w4_bf00": 26 * KIB,
     "w4_raw0": 30 * KIB,
-    "w4_raw1": 38 * KIB, "w3_sb": 46 * KIB, "w2_sb": 50 * KIB, "gain_a": 52 * KIB, "gain_b": 52 * KIB + 64,
-    "diff1_first": 53 * KIB + 64, "z_rows0": 55 * KIB, "z_rows1": 55 * KIB + 64, "w4_bf0_0": 26 * KIB, "w4_bf1_0": 58 * KIB + 64,
+    "w4_raw1": 38 * KIB,
+    "w3_sb": 46 * KIB, "w2_sb": 50 * KIB, "gain_a": 52 * KIB, "gain_b": 52 * KIB + STEP,
+    "y2_sb1": 54 * KIB, "z_pairs1": 55 * KIB, "z_moved": 57 * KIB - STEP, "second7": 57 * KIB, "diff6_0": 59 * KIB,
+    "w4_bf1": 60 * KIB,
+    "w4_q1": 64 * KIB, "z_pairs0": 66 * KIB - STEP, "diff7_1": 66 * KIB,
 }
-LATER_BYTES = 53 * KIB
-HALF = PAIRS // 2
-ALL = (0, PAIRS)
-FIRST, LAST = (0, HALF), (HALF, PAIRS)
+HELD_BYTES = 53 * KIB
 
 
 def tile_list_site_pair_couplings_kernel(
@@ -53,84 +54,46 @@ def tile_list_site_pair_couplings_kernel(
     nc = tc.nc
     with ExitStack() as ctx:
         keep = ctx.enter_context(tc.tile_pool(name="keep", bufs=1))
-        later = ctx.enter_context(tc.tile_pool(name="later", bufs=1))
+        placed = ctx.enter_context(tc.tile_pool(name="placed", bufs=1))
         psum = ctx.enter_context(tc.psum_pool(name="psum", bufs=1))
 
-        def sb(name, shape, dtype, tag=""):
-            if (tag or name) in LATER:
-                return later.tile(shape, dtype, name=name, tag=tag or name, align_bytes=64, offset=LATER[tag or name])
-            return keep.tile(shape, dtype, name=name, tag=tag or name, align_bytes=64)
+        def sb(name, shape, dtype, on=""):
+            if name in PLACE:
+                return placed.tile(shape, dtype, name=name, tag=name, align_bytes=64, offset=PLACE[name])
+            return keep.tile(shape, dtype, name=name, tag=on or name, align_bytes=64)
+
+        def words(pairs):
+            return pairs.rearrange("p h c e -> p h (c e)").bitcast(U32)
 
         offs_sb = sb("offs_sb", [P, S // GROUP], U16)
-        pos_sb = [sb("pos1_sb", [P, PAIRS // GROUP], U16), sb("pos2_sb", [P, PAIRS // GROUP], U16)]
+        pos1_sb = sb("pos1_sb", [P, PAIRS // GROUP], U16)
+        pos2_sb = sb("pos2_sb", [P, PAIRS // GROUP], U16)
         tab = [sb("tab%d" % a, [P, T], I32) for a in range(PASSES)]
-        tab_sc = sb("tab_sc", [P, LATER_BYTES], U8)[:, 0:T]
+        tab_sc = sb("tab_sc", [P, HELD_BYTES], U8)[:, 0:T]
         picked_sc = sb("picked_sc", [P, S], U8)
-        v = {}
         v_sc = sb("v_sc", [P, PASSES, S], U8)
-        gain_a = sb("gain_a", [P, PACK], F32)
-        gain_b = sb("gain_b", [P, PACK], F32)
-        w2_sb = sb("w2_sb", [P, PASSES, 2 * N], U8)
-        w3_sb = sb("w3_sb", [P, PASSES, N], I32)
-
         nc.vector.memset(tab_sc[QUADRANT : 2 * QUADRANT].bitcast(I32), 0)
         nc.vector.memset(tab_sc[2 * QUADRANT :].bitcast(I32), 0)
         nc.gpsimd.memset(v_sc[:].bitcast(I32), 0)
 
-        pieces = (2, 1)
-        w1_raw, w1_bf, w1_q, w1_sc = {}, {}, {}, {}
-        for a in range(PASSES):
-            for b in range(PASSES):
-                w1_sc[a, b] = sb("w1_sc%d%d" % (a, b), [P, PASS], U8)
+        def load_rows(name, source, first_row, first_col, width):
+            raw = sb(name, [P, PACK, width], F32)
+            rows = source[first_row : first_row + PASS, first_col : first_col + width]
+            nc.sync.dma_start(out=raw[:], in_=rows.rearrange("(p j) c -> p j c", j=PACK))
+            return raw
 
         def load_table_words(a):
             nc.sync.dma_start(out=tab[a][:], in_=tab_words[a].rearrange("p c i -> p (c i)").bitcast(I32))
 
-        def load_w1(a, b, u=0):
-            width = PASS // pieces[b]
-            w1_raw[a, b, u] = sb("w1_raw%d%d%d" % (a, b, u), [P, PACK, width], F32)
-            channel = PASS * b + width * u
-            rows = w1[PASS * a : PASS * (a + 1), channel : channel + width]
-            nc.sync.dma_start(out=w1_raw[a, b, u][:], in_=rows.rearrange("(p j) c -> p j c", j=PACK))
-
-        def round_w1(a, b, u, copy, tag=""):
-            if b == 0:
-                w1_bf[a, b, u] = sb("w1_bf%d%d%d" % (a, b, u), [P, HALF, PACK], BF16, tag)
-                if copy is None:
-                    nc.gpsimd.tensor_scalar(
-                        w1_bf[a, b, u][:], w1_raw[a, b, u][:].rearrange("p j c -> p c j"), 1.0, 0.0, MULT, ADD
-                    )
-                    return
-                copy(
-                    out=w1_bf[a, b, u][:].rearrange("p (c i) j -> p c j i", i=4),
-                    in_=w1_raw[a, b, u][:].rearrange("p j (c i) -> p c j i", i=4),
-                )
-                return
-            w1_bf[a, b, u] = sb("w1_bf%d%d%d" % (a, b, u), [P, PACK, P, PACK], BF16, tag)
-            copy(
-                out=w1_bf[a, b, u][:].rearrange("p t m j -> p m j t"),
-                in_=w1_raw[a, b, u][:].rearrange("p j (m t) -> p m j t", t=PACK),
-            )
-
-        def quantize_w1(a, b, u, i0, i1):
-            codes = sb("w1_q%d%d%d%d" % (a, b, u, i0), [P, P * (i1 - i0)], U32)
-            first = 2 * u
-            for i in range(i0, i1):
-                w1_q[a, b, first + i] = codes[:, P * (i - i0) : P * (i - i0 + 1)]
-            nc.vector.quantize_mx(
-                out=codes[:].bitcast(FP8X4),
-                scales=w1_sc[a, b][:, P * (first + i0) : P * (first + i1)],
-                in_=w1_bf[a, b, u][:].rearrange("p c j -> p (c j)" if b == 0 else "p t m j -> p (t m j)")[:, PASS * i0 : PASS * i1],
-            )
-
+        w1_raw = {}
         nc.sync.dma_start(offs_sb[:], offs)
         nc.scalar.dma_start(
             out=tab_sc[0:QUADRANT, :].bitcast(I32), in_=tab_scales.bitcast(I32).rearrange("a row c -> row a c")
         )
         load_table_words(0)
-        nc.sync.dma_start(pos_sb[1][:], pos2)
-        nc.sync.dma_start(pos_sb[0][:], pos1)
-        load_w1(0, 0)
+        nc.sync.dma_start(pos2_sb[:], pos2)
+        nc.sync.dma_start(pos1_sb[:], pos1)
+        w1_raw[0, 0] = load_rows("w1_raw00", w1, 0, 0, HALF)
         load_table_words(1)
         nc.vector.tensor_copy(picked_sc[:], tab_sc.indirect(offs_sb[:]))
         for q in range(P // QUADRANT):
@@ -138,137 +101,145 @@ def tile_list_site_pair_couplings_kernel(
                 out=v_sc[QUADRANT * q : QUADRANT * q + SCALE_ROWS].bitcast(I32),
                 in_=picked_sc[PASSES * SCALE_ROWS * q : PASSES * SCALE_ROWS * (q + 1), :].bitcast(I32),
             )
-        load_w1(1, 0, 0)
-        load_w1(0, 0, 1)
-        load_w1(1, 0, 1)
-        load_w1(0, 1)
-        load_w1(1, 1)
-        with nc.allow_non_contiguous_dma(reason="one gain for each partition and tile"):
-            nc.sync.dma_start(out=gain_a[:], in_=gain[0:PASS].rearrange("(i m) -> m i", m=P))
+        w1_raw[1, 0] = load_rows("w1_raw10", w1, PASS, 0, HALF)
+        for a in range(PASSES):
+            w1_raw[a, 1] = load_rows("w1_raw%d1" % a, w1, PASS * a, HALF, HALF)
+        for a in range(PASSES):
+            w1_raw[a, "b"] = load_rows("w1_raw%db" % a, w1, PASS * a, PASS, PASS)
+        gain_a = sb("gain_a", [P, 2, 2], F32)
+        gain_b = sb("gain_b", [P, PACK], F32)
+        with nc.allow_non_contiguous_dma(reason="two neighbouring gains for each partition and piece"):
+            nc.sync.dma_start(out=gain_a[:], in_=gain[0:PASS].rearrange("(u q e) -> q u e", u=2, e=2))
         nc.sync.dma_start(out=gain_b[:], in_=gain[PASS:].rearrange("(p t) -> p t", t=PACK))
-        w4_raw = [sb("w4_raw%d" % b, [P, PACK, N], F32) for b in range(PASSES)]
-        for b in range(PASSES):
-            rows = w4[PASS * b : PASS * (b + 1), :]
-            nc.sync.dma_start(out=w4_raw[b][:], in_=rows.rearrange("(p j) c -> p j c", j=PACK))
+        w4_raw = [load_rows("w4_raw%d" % b, w4, PASS * b, 0, N) for b in range(PASSES)]
 
-        h = {}
+        w1_bf, w1_q = {}, {}
+        w1_sc = [sb("w1_sc%d" % a, [P, H], U8) for a in range(PASSES)]
+        w1_sc_last = sb("w1_sc_last", [P, PASS], U8)
 
-        def gather_table_words(a, tag=""):
-            v[a] = sb("v%d" % a, [P, S], U32, tag)
+        def w1_scales(a, first, end):
+            if a == 1 and first >= PACK:
+                return w1_sc_last[:, P * (first - PACK) : P * (end - PACK)]
+            return w1_sc[a][:, P * first : P * end]
+
+        def round_piece(a, u, copy):
+            w1_bf[a, u] = sb("w1_bf%d%d" % (a, u), [P, 2, P, PACK], BF16)
+            copy(
+                out=w1_bf[a, u][:].rearrange("p e (m s) j -> p m j s e", s=2),
+                in_=w1_raw[a, u][:].rearrange("p j (m s e) -> p m j s e", s=2, e=2),
+            )
+
+        def round_second(a, on=""):
+            w1_bf[a, "b"] = sb("w1_bf%db" % a, [P, PACK, P, PACK], BF16, on)
+            nc.scalar.copy(
+                out=w1_bf[a, "b"][:].rearrange("p t m j -> p m j t"),
+                in_=w1_raw[a, "b"][:].rearrange("p j (m t) -> p m j t", t=PACK),
+            )
+
+        def quantize_w1(a, first, end):
+            piece, base = (first // 2, 2 * (first // 2)) if first < PACK else ("b", PACK)
+            codes = sb("w1_q%d%d" % (a, first), [P, P * (end - first)], U32)
+            for i in range(first, end):
+                w1_q[a, i] = codes[:, P * (i - first) : P * (i - first + 1)]
+            values = w1_bf[a, piece][:].rearrange("p t m j -> p (t m j)")
+            nc.vector.quantize_mx(
+                out=codes[:].bitcast(FP8X4),
+                scales=w1_scales(a, first, end),
+                in_=values[:, PASS * (first - base) : PASS * (end - base)],
+            )
+
+        v, h = {}, {}
+
+        def gather_words(a, on=""):
+            v[a] = sb("v%d" % a, [P, S], U32, on)
             nc.vector.tensor_copy(v[a][:], tab[a][:].bitcast(U32).indirect(offs_sb[:]))
 
-        def embed(b, t, tag=""):
-            h[b, t] = sb("h%d%d" % (b, t), [P, S], F32, tag)
-            cols = slice(P * t, P * (t + 1))
+        def embed(i):
+            h[i] = sb("h%d" % i, [P, S], F32)
             for site in range(0, S, BANK):
                 sites = slice(site, site + BANK)
-                bank = 4 + 2 * (t % 2) + site // BANK
-                acc = psum.tile([P, BANK], F32, name="acc%d%d%d" % (b, t, site), tag="bank%d" % bank)
+                acc = psum.tile([P, BANK], F32, name="acc%d_%d" % (i, site), tag="bank%d" % (4 + 2 * (i % 2) + site // BANK))
                 for a in range(PASSES):
                     nc.tensor.matmul_mx(
                         out=acc[:],
-                        lhsT=w1_q[a, b, t].bitcast(FP8X4),
-                        lhsT_scale=w1_sc[a, b][:, cols],
+                        lhsT=w1_q[a, i].bitcast(FP8X4),
+                        lhsT_scale=w1_scales(a, i, i + 1),
                         rhs=v[a][:, sites].bitcast(FP8X4),
                         rhs_scale=v_sc[:, a, sites],
                         start=(a == 0),
                         stop=(a == PASSES - 1),
                     )
-                nc.scalar.activation(out=h[b, t][:, sites], in_=acc[:], func=TANH)
+                nc.scalar.activation(out=h[i][:, sites], in_=acc[:], func=TANH)
+
+        second = {}
+
+        def gather_second(i, on=""):
+            both = sb("second%d%d" % (i, i + 1), [P, 2, PAIRS], F32, on)
+            for e in range(2):
+                second[i + e] = both[:, e, :]
+                nc.vector.tensor_copy(second[i + e], h[i + e][:].indirect(pos2_sb[:]))
+
+        def gather_second_one(i):
+            second[i] = sb("second%d" % i, [P, PAIRS], F32)[:]
+            nc.vector.tensor_copy(second[i], h[i][:].indirect(pos2_sb[:]))
+
+        def subtract(i, target, c0=0, c1=PAIRS):
+            nc.vector.tensor_tensor(
+                target, h[i][:].indirect(pos1_sb[:, c0 // GROUP : c1 // GROUP]), second[i][:, c0:c1], SUB
+            )
+
+        def scale_on_gpsimd(target, diff, factor):
+            nc.gpsimd.tensor_scalar(target, diff, factor, 0.0, MULT, ADD)
+
+        def scale_on_scalar(target, diff, factor):
+            nc.scalar.activation(out=target, in_=diff, func=COPY, scale=factor)
+
+        z_moved = sb("z_moved", [P, 2, PAIRS, 2], BF16)
+
+        def scale_and_move(u, diffs, on=""):
+            pairs = sb("z_piece%d" % u, [P, PAIRS, 2], BF16, on)
+            for e in range(2):
+                scale_on_gpsimd(pairs[:, :, e], diffs[e], gain_a[:, u, e : e + 1])
+            nc.sync.dma_start(
+                out=z_moved[P // 2 * u : P // 2 * (u + 1)].rearrange("p h c e -> p h (c e)"),
+                in_=pairs[:].rearrange("p c e -> p (c e)"),
+            )
 
         z_sc = [sb("z_sc%d" % b, [P, PAIRS], U8) for b in range(PASSES)]
-        whole = sb("z_q0", [P, PAIRS], U32)
-        z_q = {(0, half): whole[:, HALF * half : HALF * (half + 1)] for half in range(2)}
-        for half in range(2):
-            z_q[1, half] = sb("z_q1%d" % half, [P, HALF], U32)[:]
-        diff0 = {}
-        diff1 = sb("diff1", [P, PACK, PAIRS], F32, "w1_sc11")
-        z_bf = {}
+        z_bf, z_q = {}, {}
 
-
-        late = {}
-
-        def diff_row(b, t, run):
-            if b == 0:
-                return diff0[t][:, run[0] : run[1]]
-            if t >= 2 and run == FIRST:
-                if not late:
-                    late[0] = sb("diff1_first", [P, 2, HALF], F32)
-                return late[0][:, t - 2, :]
-            return diff1[:, t, run[0] : run[1]]
-
-        def differences(b, parts, stage, between=None):
-            for i, (t, (c0, c1)) in enumerate(parts):
-                nc.vector.tensor_copy(
-                    stage[i][:, :], h[b, t][:].indirect(pos_sb[1][:, c0 // GROUP : c1 // GROUP])
-                )
-            if between:
-                between()
-            for i, (t, (c0, c1)) in enumerate(parts):
-                nc.vector.tensor_tensor(
-                    diff_row(b, t, (c0, c1)),
-                    h[b, t][:].indirect(pos_sb[0][:, c0 // GROUP : c1 // GROUP]),
-                    stage[i][:, :],
-                    SUB,
-                )
-
-        shared = sb("z_rows1", [P, PACK + 2, HALF], BF16)
-        z_rows = {(0, ALL): sb("z_rows0", [P, PACK, PAIRS], BF16), (1, FIRST): shared[:, 2:, :], (1, LAST): shared[:, :PACK, :]}
-
-        def scale_on_scalar(b, run, t):
-            source = diff_row(b, t, run)
-            nc.scalar.activation(out=z_rows[b, run][:, t, :], in_=source, func=COPY, scale=gain_b[:, t : t + 1])
-
-        z_pair = {}
-
-        def scale_and_move(i):
-            if i % 2 == 0:
-                z_pair[i // 2] = sb("z_pair%d" % i, [P, 2 * PAIRS], BF16, "w1_q1001" if i == 0 else "")
-            z_tile = z_pair[i // 2][:, PAIRS * (i % 2) : PAIRS * (i % 2 + 1)]
-            nc.gpsimd.tensor_scalar(z_tile, diff0[i][:], gain_a[:, i : i + 1], 0.0, MULT, ADD)
-            nc.sync.dma_start(out=z_rows[0, ALL][QUADRANT * i : QUADRANT * (i + 1)], in_=z_tile)
-
-        def interleave_on_scalar(b, held, run):
-            z_bf[b, run] = sb("z_bf%d_%d" % (b, run[0]), [P, run[1] - run[0], PACK], BF16)
+        def weave(key, pairs, count, on=""):
+            z_bf[key] = sb("z_bf%s" % key, [P, count * PACK], BF16, on)
             nc.scalar.copy(
-                out=z_bf[b, run][:].rearrange("p (c i) t -> p c t i", i=4),
-                in_=z_rows[b, held][:, :, run[0] : run[1]].rearrange("p t (c i) -> p c t i", i=4),
+                out=z_bf[key][:].bitcast(U32).rearrange("p (c h) -> p c h", h=2),
+                in_=words(pairs).rearrange("p h c -> p c h"),
             )
 
-        def interleave_on_vector(b, run):
-            z_bf[b, run] = sb("z_bf%d_%d" % (b, run[0]), [P, run[1] - run[0], PACK], BF16)
-            nc.vector.tensor_copy(
-                out=z_bf[b, run][:].rearrange("p (c i) t -> p c t i", i=4),
-                in_=z_rows[b, run].rearrange("p t (c i) -> p c t i", i=4),
-            )
+        def quantize_z(key, b, c0, c1):
+            codes = sb("z_q%s" % key, [P, c1 - c0], U32)
+            for half in range(c0 // HALF, c1 // HALF):
+                z_q[b, half] = codes[:, HALF * half - c0 : HALF * (half + 1) - c0]
+            nc.vector.quantize_mx(out=codes[:].bitcast(FP8X4), scales=z_sc[b][:, c0:c1], in_=z_bf[key][:])
 
-        def quantize_z(b, run):
-            cols = slice(run[0], run[1])
-            nc.vector.quantize_mx(
-                out=(whole[:] if b == 0 else z_q[b, run[0] // HALF][:, run[0] % HALF : run[0] % HALF + run[1] - run[0]]).bitcast(FP8X4),
-                scales=z_sc[b][:, cols],
-                in_=z_bf[b, run][:].rearrange("p c t -> p (c t)"),
-            )
-
-        w4_bf = {}
-        w4_q = {}
+        w4_bf, w4_q = {}, {}
         w4_sc = [sb("w4_sc%d" % b, [P, N], U8) for b in range(PASSES)]
 
-        def round_w4(b, n0, n1, tag=""):
-            w4_bf[b, n0] = sb("w4_bf%d_%d" % (b, n0), [P, n1 - n0, PACK], BF16, tag)
+        def round_w4(target, b, n0, n1):
             nc.scalar.copy(
-                out=w4_bf[b, n0][:].rearrange("p (c i) j -> p c j i", i=4),
-                in_=w4_raw[b][:, :, n0:n1].rearrange("p j (c i) -> p c j i", i=4),
+                out=target.rearrange("p (c i) j -> p c j i", i=LINE),
+                in_=w4_raw[b][:, :, n0:n1].rearrange("p j (c i) -> p c j i", i=LINE),
             )
 
-        def quantize_w4(b, n0=0, n1=N):
-            if n0 == 0:
-                w4_q[b] = sb("w4_q%d" % b, [P, N], U32, "z_bf0_0" if b == 1 else "stage_b")
+        def quantize_w4(name, values, b, n0, n1):
+            codes = sb(name, [P, n1 - n0], U32)
+            for u in range(n0 // HALF, n1 // HALF):
+                w4_q[b, u] = codes[:, HALF * u - n0 : HALF * (u + 1) - n0]
             nc.vector.quantize_mx(
-                out=w4_q[b][:, n0:n1].bitcast(FP8X4),
-                scales=w4_sc[b][:, n0:n1],
-                in_=(w4_bf[0, n0][:] if b == 0 else w4_bf[1, 0][:, n0:n1, :]).rearrange("p c j -> p (c j)"),
+                out=codes[:].bitcast(FP8X4), scales=w4_sc[b][:, n0:n1], in_=values.rearrange("p c j -> p (c j)")
             )
+
+        w2_sb = sb("w2_sb", [P, PASSES, 2 * N], U8)
+        w3_sb = sb("w3_sb", [P, PASSES, N], I32)
 
         def weights(which, b, tile):
             cols = slice(P * tile, P * (tile + 1))
@@ -276,62 +247,50 @@ def tile_list_site_pair_couplings_kernel(
                 return w2_sb[:, b, 2 * P * tile : 2 * P * (tile + 1)].bitcast(FP4X4), w23_sc[:, b, cols]
             if which == 3:
                 return w3_sb[:, b, cols].bitcast(FP8X4), w23_sc[SCALE_ROWS:, b, cols]
-            return w4_q[b][:, cols].bitcast(FP8X4), w4_sc[b][:, cols]
+            return w4_q[b, tile // 2][:, P * (tile % 2) : P * (tile % 2 + 1)].bitcast(FP8X4), w4_sc[b][:, cols]
 
         y, y2_sb, y23 = {}, {}, {}
 
         def product(block, which, b, bank=None):
-            half, u = block
+            half, u = divmod(block, 2)
             if b == 0:
-                y[block, which] = psum.tile([P, BANK], F32, name="y%d%d%d" % (half, u, which), tag="bank%d" % bank)
-            acc = y[block, which]
-            width = HALF
-            for at in range(0, BANK, width):
-                codes, scales = weights(which, b, 2 * u + at // HALF)
-                cols = slice(HALF * half + at % HALF, HALF * half + at % HALF + width)
+                y[block, which] = psum.tile([P, BANK], F32, name="y%d%d" % (block, which), tag="bank%d" % bank)
+            for i in range(2):
+                codes, scales = weights(which, b, 2 * u + i)
                 nc.tensor.matmul_mx(
-                    out=acc[:, at : at + width],
+                    out=y[block, which][:, HALF * i : HALF * (i + 1)],
                     lhsT=codes,
                     lhsT_scale=scales,
-                    rhs=z_q[b, half][:, at % HALF : at % HALF + width].bitcast(FP8X4),
-                    rhs_scale=z_sc[b][:, cols],
-                    start=(b == 0 and at == 0),
-                    stop=(b == PASSES - 1 and at + width == BANK),
+                    rhs=z_q[b, half].bitcast(FP8X4),
+                    rhs_scale=z_sc[b][:, HALF * half : HALF * (half + 1)],
+                    start=(b == 0 and i == 0),
+                    stop=(b == PASSES - 1 and i == 1),
                 )
 
         def copy_y2(block):
-            y2_sb[block] = sb("y2_sb%d%d" % block, [P, BANK], F32)
+            y2_sb[block] = sb("y2_sb%d" % block, [P, BANK], F32)
             nc.scalar.copy(out=y2_sb[block][:], in_=y[block, 2][:])
 
         def multiply(block):
-            y23[block] = sb("y23_%d%d" % block, [P, BANK], F32)
+            y23[block] = sb("y23_%d" % block, [P, BANK], F32)
             nc.vector.tensor_tensor(y23[block][:], y[block, 3][:], y2_sb[block][:], MULT)
 
         def add_and_store(block, parts=1):
-            half, u = block
+            half, u = divmod(block, 2)
             width = BANK // parts
             for at in range(0, BANK, width):
-                result = sb("result%d%d_%d" % (half, u, at), [P, width], F32)
+                result = sb("result%d" % block + "_%d" % at * (parts > 1), [P, width], F32)
                 nc.vector.tensor_tensor(result[:], y[block, 4][:, at : at + width], y23[block][:, at : at + width], ADD)
-                store(block, result, at, width)
+                row = HALF * u + at // HALF * P
+                rows = out[row : row + width // HALF * P, HALF * half : HALF * (half + 1)]
+                nc.sync.dma_start(
+                    out=rows.rearrange("(i p) c -> p i c", p=P), in_=result[:].rearrange("p (i c) -> p i c", c=HALF)
+                )
 
-        def add_on_gpsimd(block):
-            result = sb("result%d%d" % block, [P, BANK], F32)
-            nc.gpsimd.tensor_tensor(result[:], y4_sb[:], y23[block][:], ADD)
-            store(block, result, 0, BANK)
-
-        def store(block, result, at, width):
-            half, u = block
-            row = HALF * u + at // HALF * P
-            nc.sync.dma_start(
-                out=out[row : row + width // HALF * P, HALF * half : HALF * (half + 1)].rearrange("(i p) c -> p i c", p=P),
-                in_=result[:].rearrange("p (i c) -> p i c", c=HALF),
-            )
-
-        gather_table_words(0)
-        round_w1(0, 0, 0, nc.scalar.copy)
-        quantize_w1(0, 0, 0, 0, 2)
-        w23_sc = sb("w23_sc", [P, PASSES, N], U8, "w1_raw000")
+        gather_words(0)
+        round_piece(0, 0, nc.scalar.copy)
+        quantize_w1(0, 0, 2)
+        w23_sc = sb("w23_sc", [P, PASSES, N], U8, "w1_raw00")
         for q in range(P // QUADRANT):
             for first_row, scales in ((0, w2_scales), (SCALE_ROWS, w3_scales)):
                 row = QUADRANT * q + first_row
@@ -341,95 +300,106 @@ def tile_list_site_pair_couplings_kernel(
                 )
         nc.sync.dma_start(out=w2_sb[:].bitcast(I32), in_=w2_words.rearrange("b p n -> p b n").bitcast(I32))
         nc.sync.dma_start(out=w3_sb[:], in_=w3_words.rearrange("b p n i -> p b (n i)").bitcast(I32))
+        gather_words(1, "w1_bf00")
+        round_piece(1, 0, nc.scalar.copy)
+        quantize_w1(1, 0, 1)
+        quantize_w1(1, 1, 2)
+        round_piece(0, 1, nc.scalar.copy)
+        round_piece(1, 1, nc.vector.tensor_copy)
+        quantize_w1(0, 2, 4)
+        quantize_w1(1, 2, 4)
 
-        gather_table_words(1, "w1_bf000")
-        round_w1(1, 0, 0, nc.scalar.copy)
-        quantize_w1(1, 0, 0, 0, 1)
-        quantize_w1(1, 0, 0, 1, 2)
-        round_w1(0, 0, 1, nc.scalar.copy)
-        round_w1(1, 0, 1, nc.vector.tensor_copy)
-        quantize_w1(0, 0, 1, 0, 2)
-        quantize_w1(1, 0, 1, 0, 2)
+        embed(0)
+        embed(1)
+        round_second(0, "w1_q11")
+        embed(2)
+        embed(3)
+        round_second(1)
+        w4_bf0 = [sb("w4_bf00", [P, HALF, PACK], BF16)]
+        round_w4(w4_bf0[0][:], 0, 0, HALF)
+        gather_second(0)
+        diff = {0: sb("diff0", [P, PAIRS], F32, "w1_q02"), 1: sb("diff1", [P, PAIRS], F32, "w1_q12")}
+        subtract(0, diff[0][:])
+        subtract(1, diff[1][:])
+        quantize_w1(0, 4, 8)
+        scale_and_move(0, [diff[0][:], diff[1][:]], "w1_q11")
+        gather_second(2)
+        quantize_w1(1, 4, 6)
+        quantize_w1(1, 6, 8)
+        for i in (2, 3):
+            diff[i] = sb("diff%d" % i, [P, PAIRS], F32)
+            subtract(i, diff[i][:])
+        embed(4)
+        embed(5)
+        scale_and_move(1, [diff[2][:], diff[3][:]])
+        embed(6)
+        embed(7)
+        w4_bf0.append(sb("w4_bf01", [P, HALF, PACK], BF16, "w1_q16"))
+        round_w4(w4_bf0[1][:], 0, HALF, N)
+        weave("0", z_moved[:], PAIRS, "w1_q04")
 
-        def stage(name, width, tag=""):
-            both = sb(name, [P, 2, width], F32, tag)
-            return [both[:, i, :] for i in range(2)]
+        gather_second(4)
+        diff45 = sb("diff45", [P, 2, PAIRS], F32, "w1_sc_last")
+        z_pairs = [sb("z_pairs%d" % half, [P, 2, HALF, 2], BF16) for half in range(2)]
+        for e in range(2):
+            subtract(4 + e, diff45[:, e, :])
+        for e in range(2):
+            scale_on_gpsimd(z_pairs[0][:, 0, :, e], diff45[:, e, :HALF], gain_b[:, e : e + 1])
+        for e in range(2):
+            scale_on_scalar(z_pairs[1][:, 0, :, e], diff45[:, e, HALF:], gain_b[:, e : e + 1])
+        w4_bf1 = sb("w4_bf1", [P, N, PACK], BF16)
+        round_w4(w4_bf1[:], 1, 0, N)
+        gather_second_one(6)
+        quantize_z("0", 0, 0, PAIRS)
+        for block in range(3):
+            product(block, 2, 0, 2 * block)
+            product(block, 3, 0, 2 * block + 1)
+        gather_second_one(7)
 
-        embed(0, 0)
-        embed(0, 1)
-        round_w1(0, 1, 0, nc.scalar.copy, "w1_q1001")
-        embed(0, 2)
-        embed(0, 3)
-        round_w1(1, 1, 0, nc.scalar.copy)
-        round_w4(0, 0, N // 2)
-        diff0[0] = sb("diff00", [P, PAIRS], F32, "w1_q0010")
-        diff0[1] = sb("diff01", [P, PAIRS], F32, "w1_q1010")
-        differences(0, [(0, ALL), (1, ALL)], stage("stage1", PAIRS))
-        quantize_w1(0, 1, 0, 0, PACK)
-        scale_and_move(0)
-        scale_and_move(1)
-        diff0[2] = sb("diff02", [P, PAIRS], F32)
-        diff0[3] = sb("diff03", [P, PAIRS], F32)
+        def last_tile(i, half, on=""):
+            part = sb("diff%d_%d" % (i, half), [P, HALF], F32, on)
+            subtract(i, part[:], HALF * half, HALF * (half + 1))
+            scale_on_scalar(z_pairs[half][:, 1, :, i - 6], part[:], gain_b[:, i - PACK : i - PACK + 1])
 
-        def quantize_second_channels():
-            quantize_w1(1, 1, 0, 0, 2)
-            quantize_w1(1, 1, 0, 2, PACK)
-
-        differences(0, [(2, ALL), (3, ALL)], stage("stage_a", PAIRS), quantize_second_channels)
-        embed(1, 0)
-        embed(1, 1)
-        scale_and_move(2)
-        scale_and_move(3)
-        embed(1, 2)
-        embed(1, 3)
-        round_w4(0, N // 2, N, "w1_q1102")
-        interleave_on_scalar(0, ALL, ALL)
-
-        differences(1, [(0, ALL), (1, ALL)], stage("stage_b", PAIRS))
-        differences(1, [(2, FIRST), (3, FIRST)], stage("stage_first", HALF), lambda: quantize_z(0, ALL))
-        quantize_w4(0, 0, N // 2)
-        quantize_w4(0, N // 2, N)
-        blocks = [(half, u) for half in range(2) for u in range(2)]
-        for bank in range(BANKS):
-            product(blocks[bank // 3], 2 + bank % 3, 0, bank)
-        differences(1, [(2, LAST), (3, LAST)], stage("stage_last", HALF, "z_bf0_0"))
-        round_w4(1, 0, N)
-        for run, t in ((FIRST, 0), (FIRST, 1), (LAST, 0), (LAST, 1), (FIRST, 2), (FIRST, 3)):
-            scale_on_scalar(1, run, t)
-        for quarter in ((0, CHUNK), (CHUNK, HALF)):
-            interleave_on_scalar(1, FIRST, quarter)
-        for t in (2, 3):
-            scale_on_scalar(1, LAST, t)
-        for quarter in ((0, CHUNK), (CHUNK, HALF)):
-            quantize_z(1, quarter)
-        for block in blocks[:2]:
+        last_tile(6, 0)
+        last_tile(7, 0)
+        weave("10", z_pairs[0][:], HALF)
+        codes0 = sb("w4_q0", [P, N], U32, "w1_q04")
+        for u in range(2):
+            w4_q[0, u] = codes0[:, HALF * u : HALF * (u + 1)]
+            nc.vector.quantize_mx(
+                out=w4_q[0, u].bitcast(FP8X4),
+                scales=w4_sc[0][:, HALF * u : HALF * (u + 1)],
+                in_=w4_bf0[u][:].rearrange("p c j -> p (c j)"),
+            )
+            product(u, 4, 0, 6 + u)
+        last_tile(6, 1, "diff7_0")
+        quantize_z("10", 1, 0, HALF)
+        quantize_w4("w4_q1", w4_bf1[:], 1, 0, N)
+        for which in (2, 3, 4):
+            product(0, which, 1)
+        for which in (2, 3, 4):
+            product(1, which, 1)
+        copy_y2(0)
+        last_tile(7, 1)
+        weave("11", z_pairs[1][:], HALF)
+        copy_y2(1)
+        product(3, 2, 0, 0)
+        multiply(0)
+        product(3, 3, 0, 1)
+        add_and_store(0)
+        product(2, 4, 0, 6)
+        quantize_z("11", 1, HALF, PAIRS)
+        for block in (2, 3):
             for which in (2, 3):
                 product(block, which, 1)
             copy_y2(block)
-        quantize_w4(1, 0, N // 2)
-        product(blocks[0], 4, 1)
-        interleave_on_vector(1, LAST)
-        quantize_w4(1, N // 2, N)
-        product(blocks[1], 4, 1)
-        product(blocks[3], 2, 0, 0)
-        product(blocks[3], 3, 0, 3)
-        quantize_z(1, LAST)
-        for which in (2, 3):
-            for block in blocks[2:]:
-                product(block, which, 1)
-        y4_sb = sb("y4_sb", [P, BANK], F32)
-        nc.scalar.copy(out=y4_sb[:], in_=y[blocks[0], 4][:])
-        copy_y2(blocks[2])
-        copy_y2(blocks[3])
-        multiply(blocks[0])
-        multiply(blocks[1])
-        product(blocks[2], 4, 0, 1)
-        product(blocks[2], 4, 1)
-        product(blocks[3], 4, 0, 4)
-        product(blocks[3], 4, 1)
-        add_on_gpsimd(blocks[0])
-        add_and_store(blocks[1])
-        multiply(blocks[2])
-        multiply(blocks[3])
-        add_and_store(blocks[2])
-        add_and_store(blocks[3], 2)
+        product(2, 4, 1)
+        product(3, 4, 0, 2)
+        product(3, 4, 1)
+        multiply(1)
+        add_and_store(1)
+        multiply(2)
+        multiply(3)
+        add_and_store(2)
+        add_and_store(3, 2)

@@ -34,16 +34,17 @@ KIB = 1024
 STEP = 64
 PLACE = {
     "tab_sc": 0,
-    "w1_raw10": 0, "w1_bf01": 0, "w1_bf11": 2 * KIB, "second01": 0,
+    "w1_raw10": 0, "w1_bf01": 0, "w1_bf11": 2 * KIB, "second0": KIB, "second1": 3 * KIB, "w1_q04": KIB, "z_bf00": KIB,
     "w1_raw01": 4 * KIB, "w1_raw11": 8 * KIB,
-    "w1_raw0b": 12 * KIB, "h2": 12 * KIB,
-    "w1_raw1b": 22 * KIB, "diff2": 22 * KIB, "diff3": 24 * KIB, "w4_bf00": 26 * KIB,
+    "w1_raw0b": 12 * KIB,
+    "w1_raw1b": 22 * KIB, "diff3": 22 * KIB,
     "w4_raw0": 30 * KIB,
     "w4_raw1": 38 * KIB,
     "w3_sb": 46 * KIB, "w2_sb": 50 * KIB, "gain_a": 52 * KIB, "gain_b": 52 * KIB + STEP,
-    "y2_sb1": 54 * KIB, "z_pairs1": 55 * KIB, "z_moved": 57 * KIB - STEP, "second7": 57 * KIB, "diff6_0": 59 * KIB,
-    "w4_bf1": 60 * KIB,
-    "w4_q1": 64 * KIB, "z_pairs0": 66 * KIB - STEP, "diff7_1": 66 * KIB,
+    "w4_bf10": 56 * KIB, "z_moved": 58 * KIB - STEP, "diff7_0": 58 * KIB, "diff7_1": 58 * KIB, "w4_q01": 58 * KIB,
+    "w4_q00": 59 * KIB, "diff6_0": 60 * KIB, "diff6_1": 60 * KIB, "w4_bf11": 60 * KIB,
+    "z_rows0": 64 * KIB, "w4_q10": 64 * KIB,
+    "w4_bf0": 72 * KIB, "w1_q16": 76 * KIB - 512,
 }
 HELD_BYTES = 53 * KIB
 
@@ -61,9 +62,6 @@ def tile_list_site_pair_couplings_kernel(
             if name in PLACE:
                 return placed.tile(shape, dtype, name=name, tag=name, align_bytes=64, offset=PLACE[name])
             return keep.tile(shape, dtype, name=name, tag=on or name, align_bytes=64)
-
-        def words(pairs):
-            return pairs.rearrange("p h c e -> p h (c e)").bitcast(U32)
 
         offs_sb = sb("offs_sb", [P, S // GROUP], U16)
         pos1_sb = sb("pos1_sb", [P, PAIRS // GROUP], U16)
@@ -106,10 +104,10 @@ def tile_list_site_pair_couplings_kernel(
             w1_raw[a, 1] = load_rows("w1_raw%d1" % a, w1, PASS * a, HALF, HALF)
         for a in range(PASSES):
             w1_raw[a, "b"] = load_rows("w1_raw%db" % a, w1, PASS * a, PASS, PASS)
-        gain_a = sb("gain_a", [P, 2, 2], F32)
+        gain_a = sb("gain_a", [P, PACK], F32)
         gain_b = sb("gain_b", [P, PACK], F32)
-        with nc.allow_non_contiguous_dma(reason="two neighbouring gains for each partition and piece"):
-            nc.sync.dma_start(out=gain_a[:], in_=gain[0:PASS].rearrange("(u q e) -> q u e", u=2, e=2))
+        with nc.allow_non_contiguous_dma(reason="one gain for each partition and tile"):
+            nc.sync.dma_start(out=gain_a[:], in_=gain[0:PASS].rearrange("(i m) -> m i", m=P))
         nc.sync.dma_start(out=gain_b[:], in_=gain[PASS:].rearrange("(p t) -> p t", t=PACK))
         w4_raw = [load_rows("w4_raw%d" % b, w4, PASS * b, 0, N) for b in range(PASSES)]
 
@@ -123,29 +121,34 @@ def tile_list_site_pair_couplings_kernel(
             return w1_sc[a][:, P * first : P * end]
 
         def round_piece(a, u, copy):
-            w1_bf[a, u] = sb("w1_bf%d%d" % (a, u), [P, 2, P, PACK], BF16)
+            w1_bf[a, u] = sb("w1_bf%d%d" % (a, u), [P, HALF, PACK], BF16)
             copy(
-                out=w1_bf[a, u][:].rearrange("p e (m s) j -> p m j s e", s=2),
-                in_=w1_raw[a, u][:].rearrange("p j (m s e) -> p m j s e", s=2, e=2),
+                out=w1_bf[a, u][:].rearrange("p (c i) j -> p c j i", i=LINE),
+                in_=w1_raw[a, u][:].rearrange("p j (c i) -> p c j i", i=LINE),
             )
 
-        def round_second(a, on=""):
-            w1_bf[a, "b"] = sb("w1_bf%db" % a, [P, PACK, P, PACK], BF16, on)
+        def round_planes(a, u, on=""):
+            w1_bf[a, u] = sb("w1_bf%d%d" % (a, u), [P, HALF, PACK], BF16, on)
+            planes = w1_raw[a, "b"][:].rearrange("p j (m t) -> p m j t", t=PACK)
             nc.scalar.copy(
-                out=w1_bf[a, "b"][:].rearrange("p t m j -> p m j t"),
+                out=w1_bf[a, u][:].rearrange("p (e m) j -> p m j e", e=2),
+                in_=planes[:, :, :, 2 * (u - 2) : 2 * (u - 1)],
+            )
+
+        def round_all_planes(a, on):
+            w1_bf[a, 2] = sb("w1_bf%d2" % a, [P, PASS, PACK], BF16, on)
+            nc.scalar.copy(
+                out=w1_bf[a, 2][:].rearrange("p (t m) j -> p m j t", t=PACK),
                 in_=w1_raw[a, "b"][:].rearrange("p j (m t) -> p m j t", t=PACK),
             )
 
         def quantize_w1(a, first, end):
-            piece, base = (first // 2, 2 * (first // 2)) if first < PACK else ("b", PACK)
             codes = sb("w1_q%d%d" % (a, first), [P, P * (end - first)], U32)
             for i in range(first, end):
                 w1_q[a, i] = codes[:, P * (i - first) : P * (i - first + 1)]
-            values = w1_bf[a, piece][:].rearrange("p t m j -> p (t m j)")
+            values = w1_bf[a, first // 2][:, P * (first % 2) : P * (first % 2 + end - first), :]
             nc.vector.quantize_mx(
-                out=codes[:].bitcast(FP8X4),
-                scales=w1_scales(a, first, end),
-                in_=values[:, PASS * (first - base) : PASS * (end - base)],
+                out=codes[:].bitcast(FP8X4), scales=w1_scales(a, first, end), in_=values.rearrange("p c j -> p (c j)")
             )
 
         v, h = {}, {}
@@ -194,25 +197,21 @@ def tile_list_site_pair_couplings_kernel(
         def scale_on_scalar(target, diff, factor):
             nc.scalar.activation(out=target, in_=diff, func=COPY, scale=factor)
 
-        z_moved = sb("z_moved", [P, 2, PAIRS, 2], BF16)
+        z_moved = sb("z_moved", [P, PACK, PAIRS], BF16)
 
-        def scale_and_move(u, diffs, on=""):
-            pairs = sb("z_piece%d" % u, [P, PAIRS, 2], BF16, on)
-            for e in range(2):
-                scale_on_gpsimd(pairs[:, :, e], diffs[e], gain_a[:, u, e : e + 1])
-            nc.sync.dma_start(
-                out=z_moved[P // 2 * u : P // 2 * (u + 1)].rearrange("p h c e -> p h (c e)"),
-                in_=pairs[:].rearrange("p c e -> p (c e)"),
-            )
+        def scale_and_move(i, on=""):
+            rows = sb("z_tile%d" % i, [P, PAIRS], BF16, on)
+            scale_on_gpsimd(rows[:], diff[i], gain_a[:, i : i + 1])
+            nc.sync.dma_start(out=z_moved[QUADRANT * i : QUADRANT * (i + 1)], in_=rows[:])
 
         z_sc = [sb("z_sc%d" % b, [P, PAIRS], U8) for b in range(PASSES)]
         z_bf, z_q = {}, {}
 
-        def weave(key, pairs, count, on=""):
+        def weave(key, rows, count, copy, on=""):
             z_bf[key] = sb("z_bf%s" % key, [P, count * PACK], BF16, on)
-            nc.scalar.copy(
-                out=z_bf[key][:].bitcast(U32).rearrange("p (c h) -> p c h", h=2),
-                in_=words(pairs).rearrange("p h c -> p c h"),
+            copy(
+                out=z_bf[key][:].rearrange("p (c i t) -> p c t i", i=LINE, t=PACK),
+                in_=rows.rearrange("p t (c i) -> p c t i", i=LINE),
             )
 
         def quantize_z(key, b, c0, c1):
@@ -230,8 +229,8 @@ def tile_list_site_pair_couplings_kernel(
                 in_=w4_raw[b][:, :, n0:n1].rearrange("p j (c i) -> p c j i", i=LINE),
             )
 
-        def quantize_w4(name, values, b, n0, n1):
-            codes = sb(name, [P, n1 - n0], U32)
+        def quantize_w4(name, values, b, n0, n1, on=""):
+            codes = sb(name, [P, n1 - n0], U32, on)
             for u in range(n0 // HALF, n1 // HALF):
                 w4_q[b, u] = codes[:, HALF * u - n0 : HALF * (u + 1) - n0]
             nc.vector.quantize_mx(
@@ -275,17 +274,20 @@ def tile_list_site_pair_couplings_kernel(
             y23[block] = sb("y23_%d" % block, [P, BANK], F32)
             nc.vector.tensor_tensor(y23[block][:], y[block, 3][:], y2_sb[block][:], MULT)
 
-        def add_and_store(block, parts=1):
+        def store(block, result, at, width):
             half, u = divmod(block, 2)
+            row = HALF * u + at // HALF * P
+            rows = out[row : row + width // HALF * P, HALF * half : HALF * (half + 1)]
+            nc.sync.dma_start(
+                out=rows.rearrange("(i p) c -> p i c", p=P), in_=result[:].rearrange("p (i c) -> p i c", c=HALF)
+            )
+
+        def add_and_store(block, parts=1):
             width = BANK // parts
             for at in range(0, BANK, width):
-                result = sb("result%d" % block + "_%d" % at * (parts > 1), [P, width], F32)
+                result = sb("result%d_%d" % (block, at), [P, width], F32)
                 nc.vector.tensor_tensor(result[:], y[block, 4][:, at : at + width], y23[block][:, at : at + width], ADD)
-                row = HALF * u + at // HALF * P
-                rows = out[row : row + width // HALF * P, HALF * half : HALF * (half + 1)]
-                nc.sync.dma_start(
-                    out=rows.rearrange("(i p) c -> p i c", p=P), in_=result[:].rearrange("p (i c) -> p i c", c=HALF)
-                )
+                store(block, result, at, width)
 
         gather_words(0)
         round_piece(0, 0, nc.scalar.copy)
@@ -307,97 +309,108 @@ def tile_list_site_pair_couplings_kernel(
         round_piece(0, 1, nc.scalar.copy)
         round_piece(1, 1, nc.vector.tensor_copy)
         quantize_w1(0, 2, 4)
-        quantize_w1(1, 2, 4)
+        quantize_w1(1, 2, 3)
+        quantize_w1(1, 3, 4)
 
         embed(0)
         embed(1)
-        round_second(0, "w1_q11")
+        round_all_planes(0, "w1_q11")
         embed(2)
+        round_planes(1, 2)
         embed(3)
-        round_second(1)
-        w4_bf0 = [sb("w4_bf00", [P, HALF, PACK], BF16)]
-        round_w4(w4_bf0[0][:], 0, 0, HALF)
-        gather_second(0)
-        diff = {0: sb("diff0", [P, PAIRS], F32, "w1_q02"), 1: sb("diff1", [P, PAIRS], F32, "w1_q12")}
-        subtract(0, diff[0][:])
-        subtract(1, diff[1][:])
+        round_planes(1, 3)
+        gather_second_one(0)
+        gather_second_one(1)
+        diff01 = sb("diff01", [P, 2, PAIRS], F32, "w1_q12")
+        diff = {i: diff01[:, i, :] for i in range(2)}
+        subtract(0, diff[0])
+        subtract(1, diff[1])
         quantize_w1(0, 4, 8)
-        scale_and_move(0, [diff[0][:], diff[1][:]], "w1_q11")
-        gather_second(2)
+        scale_and_move(0, "w1_q11")
+        scale_and_move(1)
+        gather_second_one(2)
         quantize_w1(1, 4, 6)
+        diff[2] = sb("diff2", [P, PAIRS], F32, "w1_bf12")[:]
+        subtract(2, diff[2])
+        scale_and_move(2)
+        gather_second_one(3)
         quantize_w1(1, 6, 8)
-        for i in (2, 3):
-            diff[i] = sb("diff%d" % i, [P, PAIRS], F32)
-            subtract(i, diff[i][:])
+        diff[3] = sb("diff3", [P, PAIRS], F32)[:]
+        subtract(3, diff[3])
         embed(4)
         embed(5)
-        scale_and_move(1, [diff[2][:], diff[3][:]])
+        scale_and_move(3)
         embed(6)
         embed(7)
-        w4_bf0.append(sb("w4_bf01", [P, HALF, PACK], BF16, "w1_q16"))
-        round_w4(w4_bf0[1][:], 0, HALF, N)
-        weave("0", z_moved[:], PAIRS, "w1_q04")
+        w4_bf0 = sb("w4_bf0", [P, N, PACK], BF16)
+        round_w4(w4_bf0[:], 0, 0, N)
+        weave("00", z_moved[:, :, :HALF], HALF, nc.scalar.copy)
+        weave("01", z_moved[:, :, HALF:], HALF, nc.scalar.copy)
+        w4_bf1 = [sb("w4_bf10", [P, HALF, PACK], BF16)]
+        round_w4(w4_bf1[0][:], 1, 0, HALF)
 
         gather_second(4)
         diff45 = sb("diff45", [P, 2, PAIRS], F32, "w1_sc_last")
-        z_pairs = [sb("z_pairs%d" % half, [P, 2, HALF, 2], BF16) for half in range(2)]
+        z_rows = [sb("z_rows%d" % half, [P, PACK, HALF], BF16) for half in range(2)]
         for e in range(2):
             subtract(4 + e, diff45[:, e, :])
-        for e in range(2):
-            scale_on_gpsimd(z_pairs[0][:, 0, :, e], diff45[:, e, :HALF], gain_b[:, e : e + 1])
-        for e in range(2):
-            scale_on_scalar(z_pairs[1][:, 0, :, e], diff45[:, e, HALF:], gain_b[:, e : e + 1])
-        w4_bf1 = sb("w4_bf1", [P, N, PACK], BF16)
-        round_w4(w4_bf1[:], 1, 0, N)
-        gather_second_one(6)
-        quantize_z("0", 0, 0, PAIRS)
-        for block in range(3):
+        for half in range(2):
+            for e in range(2):
+                cols = slice(HALF * half, HALF * (half + 1))
+                scale_on_gpsimd(z_rows[half][:, e, :], diff45[:, e, cols], gain_b[:, e : e + 1])
+        gather_second(6)
+        quantize_z("00", 0, 0, HALF)
+        for block in range(2):
             product(block, 2, 0, 2 * block)
             product(block, 3, 0, 2 * block + 1)
-        gather_second_one(7)
 
-        def last_tile(i, half, on=""):
-            part = sb("diff%d_%d" % (i, half), [P, HALF], F32, on)
+        def last_tile(i, half):
+            part = sb("diff%d_%d" % (i, half), [P, HALF], F32)
             subtract(i, part[:], HALF * half, HALF * (half + 1))
-            scale_on_scalar(z_pairs[half][:, 1, :, i - 6], part[:], gain_b[:, i - PACK : i - PACK + 1])
+            scale_on_scalar(z_rows[half][:, i - PACK, :], part[:], gain_b[:, i - PACK : i - PACK + 1])
 
         last_tile(6, 0)
         last_tile(7, 0)
-        weave("10", z_pairs[0][:], HALF)
-        codes0 = sb("w4_q0", [P, N], U32, "w1_q04")
-        for u in range(2):
-            w4_q[0, u] = codes0[:, HALF * u : HALF * (u + 1)]
-            nc.vector.quantize_mx(
-                out=w4_q[0, u].bitcast(FP8X4),
-                scales=w4_sc[0][:, HALF * u : HALF * (u + 1)],
-                in_=w4_bf0[u][:].rearrange("p c j -> p (c j)"),
-            )
-            product(u, 4, 0, 6 + u)
-        last_tile(6, 1, "diff7_0")
-        quantize_z("10", 1, 0, HALF)
-        quantize_w4("w4_q1", w4_bf1[:], 1, 0, N)
-        for which in (2, 3, 4):
-            product(0, which, 1)
-        for which in (2, 3, 4):
-            product(1, which, 1)
-        copy_y2(0)
+        weave("10", z_rows[0][:], HALF, nc.scalar.copy)
+        quantize_z("01", 0, HALF, PAIRS)
+        product(2, 2, 0, 4)
+        product(2, 3, 0, 5)
+        quantize_w4("w4_q00", w4_bf0[:, :HALF, :], 0, 0, HALF)
+        product(0, 4, 0, 6)
+        last_tile(6, 1)
         last_tile(7, 1)
-        weave("11", z_pairs[1][:], HALF)
-        copy_y2(1)
-        product(3, 2, 0, 0)
-        multiply(0)
-        product(3, 3, 0, 1)
-        add_and_store(0)
-        product(2, 4, 0, 6)
-        quantize_z("11", 1, HALF, PAIRS)
-        for block in (2, 3):
+        w4_bf1.append(sb("w4_bf11", [P, HALF, PACK], BF16))
+        round_w4(w4_bf1[1][:], 1, HALF, N)
+        quantize_z("10", 1, 0, HALF)
+        quantize_w4("w4_q10", w4_bf1[0][:], 1, 0, HALF)
+        weave("11", z_rows[1][:], HALF, nc.vector.tensor_copy)
+        quantize_w4("w4_q01", w4_bf0[:, HALF:, :], 0, HALF, N)
+        for block in range(2):
             for which in (2, 3):
                 product(block, which, 1)
             copy_y2(block)
-        product(2, 4, 1)
-        product(3, 4, 0, 2)
-        product(3, 4, 1)
+        product(0, 4, 1)
+        product(1, 4, 0, 7)
+        product(3, 2, 0, 0)
+        product(3, 3, 0, 2)
+        quantize_z("11", 1, HALF, PAIRS)
+        quantize_w4("w4_q11", w4_bf1[1][:], 1, HALF, N)
+        for block in (2, 3):
+            for which in (2, 3):
+                product(block, which, 1)
+        product(1, 4, 1)
+        y4_sb = sb("y4_sb", [P, BANK], F32)
+        nc.scalar.copy(out=y4_sb[:], in_=y[0, 4][:])
+        copy_y2(2)
+        copy_y2(3)
+        multiply(0)
         multiply(1)
+        for block in (2, 3):
+            product(block, 4, 0, 2 * block - 3)
+            product(block, 4, 1)
+        result0 = sb("result0", [P, BANK], F32)
+        nc.gpsimd.tensor_tensor(result0[:], y4_sb[:], y23[0][:], ADD)
+        store(0, result0, 0, BANK)
         add_and_store(1)
         multiply(2)
         multiply(3)

@@ -36,15 +36,15 @@ PLACE = {
     "tab_sc": 0,
     "w1_raw10": 0, "w1_bf01": 0, "w1_bf11": 2 * KIB, "second0": KIB, "second1": 3 * KIB, "w1_q04": KIB, "z_bf00": KIB,
     "w1_raw01": 4 * KIB, "w1_raw11": 8 * KIB,
-    "w1_raw0b": 12 * KIB,
-    "w1_raw1b": 22 * KIB, "diff3": 22 * KIB,
+    "w1_raw0b": 12 * KIB, "h2": 12 * KIB,
+    "w1_raw1b": 22 * KIB, "diff2": 22 * KIB, "diff3": 24 * KIB, "w4_bf00": 26 * KIB,
     "w4_raw0": 30 * KIB,
     "w4_raw1": 38 * KIB,
     "w3_sb": 46 * KIB, "w2_sb": 50 * KIB, "gain_a": 52 * KIB, "gain_b": 52 * KIB + STEP,
     "w4_bf10": 56 * KIB, "z_moved": 58 * KIB - STEP, "diff7_0": 58 * KIB, "diff7_1": 58 * KIB, "w4_q01": 58 * KIB,
     "w4_q00": 59 * KIB, "diff6_0": 60 * KIB, "diff6_1": 60 * KIB, "w4_bf11": 60 * KIB,
     "z_rows0": 64 * KIB, "w4_q10": 64 * KIB,
-    "w4_bf0": 72 * KIB, "w1_q16": 76 * KIB - 512,
+    "w4_bf01": 74 * KIB, "w1_q16": 76 * KIB - 512,
 }
 HELD_BYTES = 53 * KIB
 
@@ -127,15 +127,7 @@ def tile_list_site_pair_couplings_kernel(
                 in_=w1_raw[a, u][:].rearrange("p j (c i) -> p c j i", i=LINE),
             )
 
-        def round_planes(a, u, on=""):
-            w1_bf[a, u] = sb("w1_bf%d%d" % (a, u), [P, HALF, PACK], BF16, on)
-            planes = w1_raw[a, "b"][:].rearrange("p j (m t) -> p m j t", t=PACK)
-            nc.scalar.copy(
-                out=w1_bf[a, u][:].rearrange("p (e m) j -> p m j e", e=2),
-                in_=planes[:, :, :, 2 * (u - 2) : 2 * (u - 1)],
-            )
-
-        def round_all_planes(a, on):
+        def round_all_planes(a, on=""):
             w1_bf[a, 2] = sb("w1_bf%d2" % a, [P, PASS, PACK], BF16, on)
             nc.scalar.copy(
                 out=w1_bf[a, 2][:].rearrange("p (t m) j -> p m j t", t=PACK),
@@ -146,7 +138,8 @@ def tile_list_site_pair_couplings_kernel(
             codes = sb("w1_q%d%d" % (a, first), [P, P * (end - first)], U32)
             for i in range(first, end):
                 w1_q[a, i] = codes[:, P * (i - first) : P * (i - first + 1)]
-            values = w1_bf[a, first // 2][:, P * (first % 2) : P * (first % 2 + end - first), :]
+            piece = min(first // 2, 2)
+            values = w1_bf[a, piece][:, P * (first - 2 * piece) : P * (end - 2 * piece), :]
             nc.vector.quantize_mx(
                 out=codes[:].bitcast(FP8X4), scales=w1_scales(a, first, end), in_=values.rearrange("p c j -> p (c j)")
             )
@@ -316,9 +309,10 @@ def tile_list_site_pair_couplings_kernel(
         embed(1)
         round_all_planes(0, "w1_q11")
         embed(2)
-        round_planes(1, 2)
         embed(3)
-        round_planes(1, 3)
+        round_all_planes(1)
+        w4_bf0 = [sb("w4_bf00", [P, HALF, PACK], BF16)]
+        round_w4(w4_bf0[0][:], 0, 0, HALF)
         gather_second_one(0)
         gather_second_one(1)
         diff01 = sb("diff01", [P, 2, PAIRS], F32, "w1_q12")
@@ -328,22 +322,20 @@ def tile_list_site_pair_couplings_kernel(
         quantize_w1(0, 4, 8)
         scale_and_move(0, "w1_q11")
         scale_and_move(1)
-        gather_second_one(2)
+        gather_second(2)
         quantize_w1(1, 4, 6)
-        diff[2] = sb("diff2", [P, PAIRS], F32, "w1_bf12")[:]
-        subtract(2, diff[2])
-        scale_and_move(2)
-        gather_second_one(3)
         quantize_w1(1, 6, 8)
-        diff[3] = sb("diff3", [P, PAIRS], F32)[:]
-        subtract(3, diff[3])
+        for i in (2, 3):
+            diff[i] = sb("diff%d" % i, [P, PAIRS], F32)[:]
+            subtract(i, diff[i])
         embed(4)
         embed(5)
+        scale_and_move(2)
         scale_and_move(3)
         embed(6)
         embed(7)
-        w4_bf0 = sb("w4_bf0", [P, N, PACK], BF16)
-        round_w4(w4_bf0[:], 0, 0, N)
+        w4_bf0.append(sb("w4_bf01", [P, HALF, PACK], BF16))
+        round_w4(w4_bf0[1][:], 0, HALF, N)
         weave("00", z_moved[:, :, :HALF], HALF, nc.scalar.copy)
         weave("01", z_moved[:, :, HALF:], HALF, nc.scalar.copy)
         w4_bf1 = [sb("w4_bf10", [P, HALF, PACK], BF16)]
@@ -375,7 +367,7 @@ def tile_list_site_pair_couplings_kernel(
         quantize_z("01", 0, HALF, PAIRS)
         product(2, 2, 0, 4)
         product(2, 3, 0, 5)
-        quantize_w4("w4_q00", w4_bf0[:, :HALF, :], 0, 0, HALF)
+        quantize_w4("w4_q00", w4_bf0[0][:], 0, 0, HALF)
         product(0, 4, 0, 6)
         last_tile(6, 1)
         last_tile(7, 1)
@@ -384,7 +376,7 @@ def tile_list_site_pair_couplings_kernel(
         quantize_z("10", 1, 0, HALF)
         quantize_w4("w4_q10", w4_bf1[0][:], 1, 0, HALF)
         weave("11", z_rows[1][:], HALF, nc.vector.tensor_copy)
-        quantize_w4("w4_q01", w4_bf0[:, HALF:, :], 0, HALF, N)
+        quantize_w4("w4_q01", w4_bf0[1][:], 0, HALF, N)
         for block in range(2):
             for which in (2, 3):
                 product(block, which, 1)

@@ -34,16 +34,15 @@ KIB = 1024
 STEP = 64
 PLACE = {
     "tab_sc": 0,
-    "w1_raw10": 0, "w1_bf01": 0, "w1_bf11": 2 * KIB, "second0": KIB, "second1": 3 * KIB, "w1_q04": KIB, "z_bf00": KIB,
+    "w1_raw10": 0, "w1_bf01": 0, "w1_bf11": 2 * KIB, "second0": KIB, "second1": 3 * KIB, "w1_q04": KIB, "z_bf0": KIB, "w4_q0": KIB,
     "w1_raw01": 4 * KIB, "w1_raw11": 8 * KIB,
     "w1_raw0b": 12 * KIB, "h2": 12 * KIB,
     "w1_raw1b": 22 * KIB, "diff2": 22 * KIB, "diff3": 24 * KIB, "w4_bf00": 26 * KIB,
     "w4_raw0": 30 * KIB,
     "w4_raw1": 38 * KIB,
     "w3_sb": 46 * KIB, "w2_sb": 50 * KIB, "gain_a": 52 * KIB, "gain_b": 52 * KIB + STEP,
-    "w4_bf10": 56 * KIB, "z_moved": 58 * KIB - STEP, "diff7_0": 58 * KIB, "diff7_1": 58 * KIB, "w4_q01": 58 * KIB,
-    "w4_q00": 59 * KIB, "diff6_0": 60 * KIB, "diff6_1": 60 * KIB, "w4_bf11": 60 * KIB,
-    "z_rows0": 64 * KIB, "w4_q10": 64 * KIB,
+    "w4_bf1": 54 * KIB, "z_moved": 58 * KIB - STEP, "diff67_0": 58 * KIB,
+    "w4_q10": 58 * KIB, "diff67_1": 59 * KIB, "w4_q11": 60 * KIB,
     "w4_bf01": 74 * KIB, "w1_q16": 76 * KIB - 512,
 }
 HELD_BYTES = 53 * KIB
@@ -336,61 +335,59 @@ def tile_list_site_pair_couplings_kernel(
         embed(7)
         w4_bf0.append(sb("w4_bf01", [P, HALF, PACK], BF16))
         round_w4(w4_bf0[1][:], 0, HALF, N)
-        weave("00", z_moved[:, :, :HALF], HALF, nc.scalar.copy)
-        weave("01", z_moved[:, :, HALF:], HALF, nc.scalar.copy)
-        w4_bf1 = [sb("w4_bf10", [P, HALF, PACK], BF16)]
-        round_w4(w4_bf1[0][:], 1, 0, HALF)
+        weave("0", z_moved[:], PAIRS, nc.scalar.copy)
+        w4_bf1 = sb("w4_bf1", [P, N, PACK], BF16)
+        round_w4(w4_bf1[:], 1, 0, N)
 
         gather_second(4)
         diff45 = sb("diff45", [P, 2, PAIRS], F32, "w1_sc_last")
-        z_rows = [sb("z_rows%d" % half, [P, PACK, HALF], BF16) for half in range(2)]
         for e in range(2):
             subtract(4 + e, diff45[:, e, :])
-        for half in range(2):
-            for e in range(2):
-                cols = slice(HALF * half, HALF * (half + 1))
-                scale_on_gpsimd(z_rows[half][:, e, :], diff45[:, e, cols], gain_b[:, e : e + 1])
+        z_rows = sb("z_rows", [P, PACK, PAIRS], BF16, "second45")
+        for e in range(2):
+            scale_on_gpsimd(z_rows[:, e, :], diff45[:, e, :], gain_b[:, e : e + 1])
         gather_second(6)
-        quantize_z("00", 0, 0, HALF)
-        for block in range(2):
+        quantize_z("0", 0, 0, PAIRS)
+        for block in range(3):
             product(block, 2, 0, 2 * block)
             product(block, 3, 0, 2 * block + 1)
 
-        def last_tile(i, half):
-            part = sb("diff%d_%d" % (i, half), [P, HALF], F32)
-            subtract(i, part[:], HALF * half, HALF * (half + 1))
-            scale_on_scalar(z_rows[half][:, i - PACK, :], part[:], gain_b[:, i - PACK : i - PACK + 1])
+        def last_tiles(half):
+            cols = slice(HALF * half, HALF * (half + 1))
+            part = sb("diff67_%d" % half, [P, 2, HALF], F32)
+            for e in range(2):
+                subtract(6 + e, part[:, e, :], cols.start, cols.stop)
+            for e in range(2):
+                scale_on_scalar(z_rows[:, 2 + e, cols], part[:, e, :], gain_b[:, 2 + e : 3 + e])
 
-        last_tile(6, 0)
-        last_tile(7, 0)
-        weave("10", z_rows[0][:], HALF, nc.scalar.copy)
-        quantize_z("01", 0, HALF, PAIRS)
-        product(2, 2, 0, 4)
-        product(2, 3, 0, 5)
-        quantize_w4("w4_q00", w4_bf0[0][:], 0, 0, HALF)
-        product(0, 4, 0, 6)
-        last_tile(6, 1)
-        last_tile(7, 1)
-        w4_bf1.append(sb("w4_bf11", [P, HALF, PACK], BF16))
-        round_w4(w4_bf1[1][:], 1, HALF, N)
+        last_tiles(0)
+        weave("10", z_rows[:, :, :HALF], HALF, nc.scalar.copy)
+        codes0 = sb("w4_q0", [P, N], U32)
+        for u in range(2):
+            w4_q[0, u] = codes0[:, HALF * u : HALF * (u + 1)]
+            nc.vector.quantize_mx(
+                out=w4_q[0, u].bitcast(FP8X4),
+                scales=w4_sc[0][:, HALF * u : HALF * (u + 1)],
+                in_=w4_bf0[u][:].rearrange("p c j -> p (c j)"),
+            )
+            product(u, 4, 0, 6 + u)
+        last_tiles(1)
+        quantize_w4("w4_q10", w4_bf1[:, :HALF, :], 1, 0, HALF)
         quantize_z("10", 1, 0, HALF)
-        quantize_w4("w4_q10", w4_bf1[0][:], 1, 0, HALF)
-        weave("11", z_rows[1][:], HALF, nc.vector.tensor_copy)
-        quantize_w4("w4_q01", w4_bf0[1][:], 0, HALF, N)
+        weave("11", z_rows[:, :, HALF:], HALF, nc.vector.tensor_copy)
+        quantize_w4("w4_q11", w4_bf1[:, HALF:, :], 1, HALF, N)
         for block in range(2):
             for which in (2, 3):
                 product(block, which, 1)
             copy_y2(block)
-        product(0, 4, 1)
-        product(1, 4, 0, 7)
+        for block in range(2):
+            product(block, 4, 1)
         product(3, 2, 0, 0)
         product(3, 3, 0, 2)
         quantize_z("11", 1, HALF, PAIRS)
-        quantize_w4("w4_q11", w4_bf1[1][:], 1, HALF, N)
         for block in (2, 3):
             for which in (2, 3):
                 product(block, which, 1)
-        product(1, 4, 1)
         y4_sb = sb("y4_sb", [P, BANK], F32)
         nc.scalar.copy(out=y4_sb[:], in_=y[0, 4][:])
         copy_y2(2)

@@ -34,7 +34,8 @@ KIB = 1024
 STEP = 64
 PLACE = {
     "tab_sc": 0,
-    "w1_raw10": 0, "w1_bf01": 0, "w1_bf11": 2 * KIB, "second0": KIB, "second1": 3 * KIB, "w1_q04": KIB, "z_bf0": KIB, "w4_q0": KIB,
+    "w1_raw10": 0, "w1_bf01": 0, "w1_bf11": 2 * KIB, "second0": KIB, "second1": 3 * KIB,
+    "w1_q04": KIB, "z_bf0": KIB, "w4_q0": KIB,
     "w1_raw01": 4 * KIB, "w1_raw11": 8 * KIB,
     "w1_raw0b": 12 * KIB, "h2": 12 * KIB,
     "w1_raw1b": 22 * KIB, "diff2": 22 * KIB, "diff3": 24 * KIB, "w4_bf00": 26 * KIB,
@@ -43,6 +44,7 @@ PLACE = {
     "w3_sb": 46 * KIB, "w2_sb": 50 * KIB, "gain_a": 52 * KIB, "gain_b": 52 * KIB + STEP,
     "w4_bf1": 54 * KIB, "z_moved": 58 * KIB - STEP, "diff67_0": 58 * KIB,
     "w4_q10": 58 * KIB, "diff67_1": 59 * KIB, "w4_q11": 60 * KIB,
+    "w1_raw00": 80 * KIB, "w23_sc": 80 * KIB, "v1": 81 * KIB,
     "w4_bf01": 74 * KIB, "w1_q16": 76 * KIB - 512,
 }
 HELD_BYTES = 53 * KIB
@@ -284,7 +286,7 @@ def tile_list_site_pair_couplings_kernel(
         gather_words(0)
         round_piece(0, 0, nc.scalar.copy)
         quantize_w1(0, 0, 2)
-        w23_sc = sb("w23_sc", [P, PASSES, N], U8, "w1_raw00")
+        w23_sc = sb("w23_sc", [P, PASSES, N], U8)
         for q in range(P // QUADRANT):
             for first_row, scales in ((0, w2_scales), (SCALE_ROWS, w3_scales)):
                 row = QUADRANT * q + first_row
@@ -294,7 +296,7 @@ def tile_list_site_pair_couplings_kernel(
                 )
         nc.sync.dma_start(out=w2_sb[:].bitcast(I32), in_=w2_words.rearrange("b p n -> p b n").bitcast(I32))
         nc.sync.dma_start(out=w3_sb[:], in_=w3_words.rearrange("b p n i -> p b (n i)").bitcast(I32))
-        gather_words(1, "w1_bf00")
+        gather_words(1)
         round_piece(1, 0, nc.scalar.copy)
         quantize_w1(1, 0, 1)
         quantize_w1(1, 1, 2)
@@ -389,7 +391,7 @@ def tile_list_site_pair_couplings_kernel(
             for which in (2, 3):
                 product(block, which, 1)
         y4_sb = sb("y4_sb", [P, BANK], F32)
-        nc.scalar.copy(out=y4_sb[:], in_=y[0, 4][:])
+        nc.scalar.copy(out=y4_sb[:], in_=y[1, 4][:])
         copy_y2(2)
         copy_y2(3)
         multiply(0)
@@ -397,10 +399,10 @@ def tile_list_site_pair_couplings_kernel(
         for block in (2, 3):
             product(block, 4, 0, 2 * block - 3)
             product(block, 4, 1)
-        result0 = sb("result0", [P, BANK], F32)
-        nc.gpsimd.tensor_tensor(result0[:], y4_sb[:], y23[0][:], ADD)
-        store(0, result0, 0, BANK)
-        add_and_store(1)
+        add_and_store(0)
+        result1 = sb("result1", [P, BANK], F32)
+        nc.gpsimd.tensor_tensor(result1[:], y4_sb[:], y23[1][:], ADD)
+        store(1, result1, 0, BANK)
         multiply(2)
         multiply(3)
         add_and_store(2)

@@ -43,7 +43,7 @@ PLACE = {
     "w4_raw1": 38 * KIB,
     "w3_sb": 46 * KIB, "w2_sb": 50 * KIB, "gain_a": 52 * KIB, "gain_b": 52 * KIB + STEP,
     "w4_bf1": 54 * KIB, "z_moved": 58 * KIB - STEP, "diff67_0": 58 * KIB,
-    "w4_q10": 58 * KIB, "diff67_1": 59 * KIB, "w4_q11": 60 * KIB,
+    "diff67_1": 59 * KIB, "w4_q10": 59 * KIB, "w4_q11": 60 * KIB,
     "w1_raw00": 80 * KIB, "w23_sc": 80 * KIB, "v1": 81 * KIB,
     "w4_bf01": 74 * KIB, "w1_q16": 76 * KIB - 512,
 }
@@ -264,9 +264,10 @@ def tile_list_site_pair_couplings_kernel(
             y2_sb[block] = sb("y2_sb%d" % block, [P, BANK], F32)
             nc.scalar.copy(out=y2_sb[block][:], in_=y[block, 2][:])
 
-        def multiply(block):
-            y23[block] = sb("y23_%d" % block, [P, BANK], F32)
-            nc.vector.tensor_tensor(y23[block][:], y[block, 3][:], y2_sb[block][:], MULT)
+        def multiply(block, cols=slice(0, BANK)):
+            if cols.start == 0:
+                y23[block] = sb("y23_%d" % block, [P, BANK], F32)
+            nc.vector.tensor_tensor(y23[block][:, cols], y[block, 3][:, cols], y2_sb[block][:, cols], MULT)
 
         def store(block, result, at, width):
             half, u = divmod(block, 2)
@@ -374,8 +375,8 @@ def tile_list_site_pair_couplings_kernel(
             )
             product(u, 4, 0, 6 + u)
         last_tiles(1)
-        quantize_w4("w4_q10", w4_bf1[:, :HALF, :], 1, 0, HALF)
         quantize_z("10", 1, 0, HALF)
+        quantize_w4("w4_q10", w4_bf1[:, :HALF, :], 1, 0, HALF)
         weave("11", z_rows[:, :, HALF:], HALF, nc.vector.tensor_copy)
         quantize_w4("w4_q11", w4_bf1[:, HALF:, :], 1, HALF, N)
         for block in range(2):
@@ -404,6 +405,7 @@ def tile_list_site_pair_couplings_kernel(
         nc.gpsimd.tensor_tensor(result1[:], y4_sb[:], y23[1][:], ADD)
         store(1, result1, 0, BANK)
         multiply(2)
-        multiply(3)
+        multiply(3, slice(0, HALF))
         add_and_store(2)
+        multiply(3, slice(HALF, BANK))
         add_and_store(3, 2)

from contextlib import ExitStack

import concourse.mybir as mybir

K, T, S, PAIRS, H, N = 1024, 2048, 1024, 512, 1024, 512
FLOPS = 2 * K * H * S + 3 * 2 * H * N * PAIRS

F32 = mybir.dt.float32
BF16 = mybir.dt.bfloat16
I32 = mybir.dt.int32
U32 = mybir.dt.uint32
U16 = mybir.dt.uint16
U8 = mybir.dt.uint8
FP8X4 = mybir.dt.float8_e4m3fn_x4
FP4X4 = mybir.dt.float4_e2m1fn_x4
MULT = mybir.AluOpType.mult
ADD = mybir.AluOpType.add
SUB = mybir.AluOpType.subtract
TANH = mybir.ActivationFunctionType.Tanh
COPY = mybir.ActivationFunctionType.Copy

P = 128
PACK = 4
PASS = P * PACK
PASSES = 2
BANK = 512
GROUP = 16
QUADRANT = 32
SCALE_ROWS = 4
HALF = PAIRS // 2
LINE = 4

KIB = 1024
STEP = 64
PLACE = {
    "tab_sc": 0,
    "w1_raw10": 0, "w1_bf01": 0, "w1_bf11": 2 * KIB, "second0": KIB, "second1": 3 * KIB,
    "w1_q04": KIB, "z_bf0": KIB, "w4_q0": KIB,
    "w1_raw01": 4 * KIB, "w1_raw11": 8 * KIB,
    "w1_raw0b": 12 * KIB, "h2": 12 * KIB,
    "w1_raw1b": 22 * KIB, "diff2": 22 * KIB, "diff3": 24 * KIB, "w4_bf00": 26 * KIB,
    "w4_raw0": 30 * KIB,
    "w4_raw1": 38 * KIB,
    "w3_sb": 46 * KIB, "w2_sb": 50 * KIB, "gain_a": 52 * KIB, "gain_b": 52 * KIB + STEP,
    "w4_bf1": 54 * KIB, "z_moved": 58 * KIB - STEP, "diff67_0": 58 * KIB,
    "diff67_1": 59 * KIB, "w4_q10": 59 * KIB, "w4_q11": 60 * KIB,
    "w1_raw00": 80 * KIB, "w23_sc": 80 * KIB, "v1": 81 * KIB,
    "w4_bf01": 74 * KIB, "w1_q16": 76 * KIB - 512,
}
HELD_BYTES = 53 * KIB


def tile_list_site_pair_couplings_kernel(
    tc, tab_words, tab_scales, offs, w1, gain, pos1, pos2, w2_words, w2_scales, w3_words, w3_scales, w4, out
):
    nc = tc.nc
    with ExitStack() as ctx:
        keep = ctx.enter_context(tc.tile_pool(name="keep", bufs=1))
        placed = ctx.enter_context(tc.tile_pool(name="placed", bufs=1))
        psum = ctx.enter_context(tc.psum_pool(name="psum", bufs=1))

        def sb(name, shape, dtype, on=""):
            if name in PLACE:
                return placed.tile(shape, dtype, name=name, tag=name, align_bytes=64, offset=PLACE[name])
            return keep.tile(shape, dtype, name=name, tag=on or name, align_bytes=64)

        offs_sb = sb("offs_sb", [P, S // GROUP], U16)
        pos1_sb = sb("pos1_sb", [P, PAIRS // GROUP], U16)
        pos2_sb = sb("pos2_sb", [P, PAIRS // GROUP], U16)
        tab = [sb("tab%d" % a, [P, T], I32) for a in range(PASSES)]
        tab_sc = sb("tab_sc", [P, HELD_BYTES], U8)[:, 0:T]
        picked_sc = sb("picked_sc", [P, S], U8)
        v_sc = sb("v_sc", [P, PASSES, S], U8)
        nc.vector.memset(tab_sc[QUADRANT : 2 * QUADRANT].bitcast(I32), 0)
        nc.vector.memset(tab_sc[2 * QUADRANT :].bitcast(I32), 0)
        nc.gpsimd.memset(v_sc[:].bitcast(I32), 0)

        def load_rows(name, source, first_row, first_col, width):
            raw = sb(name, [P, PACK, width], F32)
            rows = source[first_row : first_row + PASS, first_col : first_col + width]
            nc.sync.dma_start(out=raw[:], in_=rows.rearrange("(p j) c -> p j c", j=PACK))
            return raw

        def load_table_words(a):
            nc.sync.dma_start(out=tab[a][:], in_=tab_words[a].rearrange("p c i -> p (c i)").bitcast(I32))

        w1_raw = {}
        nc.sync.dma_start(offs_sb[:], offs)
        nc.scalar.dma_start(
            out=tab_sc[0:QUADRANT, :].bitcast(I32), in_=tab_scales.bitcast(I32).rearrange("a row c -> row a c")
        )
        load_table_words(0)
        nc.sync.dma_start(pos2_sb[:], pos2)
        nc.sync.dma_start(pos1_sb[:], pos1)
        w1_raw[0, 0] = load_rows("w1_raw00", w1, 0, 0, HALF)
        load_table_words(1)
        nc.vector.tensor_copy(picked_sc[:], tab_sc.indirect(offs_sb[:]))
        for q in range(P // QUADRANT):
            nc.sync.dma_start(
                out=v_sc[QUADRANT * q : QUADRANT * q + SCALE_ROWS].bitcast(I32),
                in_=picked_sc[PASSES * SCALE_ROWS * q : PASSES * SCALE_ROWS * (q + 1), :].bitcast(I32),
            )
        w1_raw[1, 0] = load_rows("w1_raw10", w1, PASS, 0, HALF)
        for a in range(PASSES):
            w1_raw[a, 1] = load_rows("w1_raw%d1" % a, w1, PASS * a, HALF, HALF)
        for a in range(PASSES):
            w1_raw[a, "b"] = load_rows("w1_raw%db" % a, w1, PASS * a, PASS, PASS)
        gain_a = sb("gain_a", [P, PACK], F32)
        gain_b = sb("gain_b", [P, PACK], F32)
        with nc.allow_non_contiguous_dma(reason="one gain for each partition and tile"):
            nc.sync.dma_start(out=gain_a[:], in_=gain[0:PASS].rearrange("(i m) -> m i", m=P))
        nc.sync.dma_start(out=gain_b[:], in_=gain[PASS:].rearrange("(p t) -> p t", t=PACK))
        w4_raw = [load_rows("w4_raw%d" % b, w4, PASS * b, 0, N) for b in range(PASSES)]

        w1_bf, w1_q = {}, {}
        w1_sc = [sb("w1_sc%d" % a, [P, H], U8) for a in range(PASSES)]
        w1_sc_last = sb("w1_sc_last", [P, PASS], U8)

        def w1_scales(a, first, end):
            if a == 1 and first >= PACK:
                return w1_sc_last[:, P * (first - PACK) : P * (end - PACK)]
            return w1_sc[a][:, P * first : P * end]

        def round_piece(a, u, copy):
            w1_bf[a, u] = sb("w1_bf%d%d" % (a, u), [P, HALF, PACK], BF16)
            copy(
                out=w1_bf[a, u][:].rearrange("p (c i) j -> p c j i", i=LINE),
                in_=w1_raw[a, u][:].rearrange("p j (c i) -> p c j i", i=LINE),
            )

        def round_all_planes(a, on=""):
            w1_bf[a, 2] = sb("w1_bf%d2" % a, [P, PASS, PACK], BF16, on)
            nc.scalar.copy(
                out=w1_bf[a, 2][:].rearrange("p (t m) j -> p m j t", t=PACK),
                in_=w1_raw[a, "b"][:].rearrange("p j (m t) -> p m j t", t=PACK),
            )

        def quantize_w1(a, first, end):
            codes = sb("w1_q%d%d" % (a, first), [P, P * (end - first)], U32)
            for i in range(first, end):
                w1_q[a, i] = codes[:, P * (i - first) : P * (i - first + 1)]
            piece = min(first // 2, 2)
            values = w1_bf[a, piece][:, P * (first - 2 * piece) : P * (end - 2 * piece), :]
            nc.vector.quantize_mx(
                out=codes[:].bitcast(FP8X4), scales=w1_scales(a, first, end), in_=values.rearrange("p c j -> p (c j)")
            )

        v, h = {}, {}

        def gather_words(a, on=""):
            v[a] = sb("v%d" % a, [P, S], U32, on)
            nc.vector.tensor_copy(v[a][:], tab[a][:].bitcast(U32).indirect(offs_sb[:]))

        def embed(i):
            h[i] = sb("h%d" % i, [P, S], F32)
            for site in range(0, S, BANK):
                sites = slice(site, site + BANK)
                acc = psum.tile([P, BANK], F32, name="acc%d_%d" % (i, site), tag="bank%d" % (4 + 2 * (i % 2) + site // BANK))
                for a in range(PASSES):
                    nc.tensor.matmul_mx(
                        out=acc[:],
                        lhsT=w1_q[a, i].bitcast(FP8X4),
                        lhsT_scale=w1_scales(a, i, i + 1),
                        rhs=v[a][:, sites].bitcast(FP8X4),
                        rhs_scale=v_sc[:, a, sites],
                        start=(a == 0),
                        stop=(a == PASSES - 1),
                    )
                nc.scalar.activation(out=h[i][:, sites], in_=acc[:], func=TANH)

        second = {}

        def gather_second(i, on=""):
            both = sb("second%d%d" % (i, i + 1), [P, 2, PAIRS], F32, on)
            for e in range(2):
                second[i + e] = both[:, e, :]
                nc.vector.tensor_copy(second[i + e], h[i + e][:].indirect(pos2_sb[:]))

        def gather_second_one(i):
            second[i] = sb("second%d" % i, [P, PAIRS], F32)[:]
            nc.vector.tensor_copy(second[i], h[i][:].indirect(pos2_sb[:]))

        def subtract(i, target, c0=0, c1=PAIRS):
            nc.vector.tensor_tensor(
                target, h[i][:].indirect(pos1_sb[:, c0 // GROUP : c1 // GROUP]), second[i][:, c0:c1], SUB
            )

        def scale_on_gpsimd(target, diff, factor):
            nc.gpsimd.tensor_scalar(target, diff, factor, 0.0, MULT, ADD)

        def scale_on_scalar(target, diff, factor):
            nc.scalar.activation(out=target, in_=diff, func=COPY, scale=factor)

        z_moved = sb("z_moved", [P, PACK, PAIRS], BF16)

        def scale_and_move(i, on=""):
            rows = sb("z_tile%d" % i, [P, PAIRS], BF16, on)
            scale_on_gpsimd(rows[:], diff[i], gain_a[:, i : i + 1])
            nc.sync.dma_start(out=z_moved[QUADRANT * i : QUADRANT * (i + 1)], in_=rows[:])

        z_sc = [sb("z_sc%d" % b, [P, PAIRS], U8) for b in range(PASSES)]
        z_bf, z_q = {}, {}

        def weave(key, rows, count, copy, on=""):
            z_bf[key] = sb("z_bf%s" % key, [P, count * PACK], BF16, on)
            copy(
                out=z_bf[key][:].rearrange("p (c i t) -> p c t i", i=LINE, t=PACK),
                in_=rows.rearrange("p t (c i) -> p c t i", i=LINE),
            )

        def quantize_z(key, b, c0, c1):
            codes = sb("z_q%s" % key, [P, c1 - c0], U32)
            for half in range(c0 // HALF, c1 // HALF):
                z_q[b, half] = codes[:, HALF * half - c0 : HALF * (half + 1) - c0]
            nc.vector.quantize_mx(out=codes[:].bitcast(FP8X4), scales=z_sc[b][:, c0:c1], in_=z_bf[key][:])

        w4_bf, w4_q = {}, {}
        w4_sc = [sb("w4_sc%d" % b, [P, N], U8) for b in range(PASSES)]

        def round_w4(target, b, n0, n1):
            nc.scalar.copy(
                out=target.rearrange("p (c i) j -> p c j i", i=LINE),
                in_=w4_raw[b][:, :, n0:n1].rearrange("p j (c i) -> p c j i", i=LINE),
            )

        def quantize_w4(name, values, b, n0, n1, on=""):
            codes = sb(name, [P, n1 - n0], U32, on)
            for u in range(n0 // HALF, n1 // HALF):
                w4_q[b, u] = codes[:, HALF * u - n0 : HALF * (u + 1) - n0]
            nc.vector.quantize_mx(
                out=codes[:].bitcast(FP8X4), scales=w4_sc[b][:, n0:n1], in_=values.rearrange("p c j -> p (c j)")
            )

        w2_sb = sb("w2_sb", [P, PASSES, 2 * N], U8)
        w3_sb = sb("w3_sb", [P, PASSES, N], I32)

        def weights(which, b, tile):
            cols = slice(P * tile, P * (tile + 1))
            if which == 2:
                return w2_sb[:, b, 2 * P * tile : 2 * P * (tile + 1)].bitcast(FP4X4), w23_sc[:, b, cols]
            if which == 3:
                return w3_sb[:, b, cols].bitcast(FP8X4), w23_sc[SCALE_ROWS:, b, cols]
            return w4_q[b, tile // 2][:, P * (tile % 2) : P * (tile % 2 + 1)].bitcast(FP8X4), w4_sc[b][:, cols]

        y, y2_sb, y23 = {}, {}, {}

        def product(block, which, b, bank=None):
            half, u = divmod(block, 2)
            if b == 0:
                y[block, which] = psum.tile([P, BANK], F32, name="y%d%d" % (block, which), tag="bank%d" % bank)
            for i in range(2):
                codes, scales = weights(which, b, 2 * u + i)
                nc.tensor.matmul_mx(
                    out=y[block, which][:, HALF * i : HALF * (i + 1)],
                    lhsT=codes,
                    lhsT_scale=scales,
                    rhs=z_q[b, half].bitcast(FP8X4),
                    rhs_scale=z_sc[b][:, HALF * half : HALF * (half + 1)],
                    start=(b == 0 and i == 0),
                    stop=(b == PASSES - 1 and i == 1),
                )

        def copy_y2(block):
            y2_sb[block] = sb("y2_sb%d" % block, [P, BANK], F32)
            nc.scalar.copy(out=y2_sb[block][:], in_=y[block, 2][:])

        def multiply(block, cols=slice(0, BANK)):
            if cols.start == 0:
                y23[block] = sb("y23_%d" % block, [P, BANK], F32)
            nc.vector.tensor_tensor(y23[block][:, cols], y[block, 3][:, cols], y2_sb[block][:, cols], MULT)

        def store(block, result, at, width):
            half, u = divmod(block, 2)
            row = HALF * u + at // HALF * P
            rows = out[row : row + width // HALF * P, HALF * half : HALF * (half + 1)]
            nc.sync.dma_start(
                out=rows.rearrange("(i p) c -> p i c", p=P), in_=result[:].rearrange("p (i c) -> p i c", c=HALF)
            )

        def add_and_store(block, parts=1):
            width = BANK // parts
            for at in range(0, BANK, width):
                result = sb("result%d_%d" % (block, at), [P, width], F32)
                nc.vector.tensor_tensor(result[:], y[block, 4][:, at : at + width], y23[block][:, at : at + width], ADD)
                store(block, result, at, width)

        gather_words(0)
        round_piece(0, 0, nc.scalar.copy)
        quantize_w1(0, 0, 2)
        w23_sc = sb("w23_sc", [P, PASSES, N], U8)
        for q in range(P // QUADRANT):
            for first_row, scales in ((0, w2_scales), (SCALE_ROWS, w3_scales)):
                row = QUADRANT * q + first_row
                nc.sync.dma_start(
                    out=w23_sc[row : row + SCALE_ROWS].bitcast(I32),
                    in_=scales[:, SCALE_ROWS * q : SCALE_ROWS * (q + 1), :].rearrange("b r n -> r b n").bitcast(I32),
                )
        nc.sync.dma_start(out=w2_sb[:].bitcast(I32), in_=w2_words.rearrange("b p n -> p b n").bitcast(I32))
        nc.sync.dma_start(out=w3_sb[:], in_=w3_words.rearrange("b p n i -> p b (n i)").bitcast(I32))
        gather_words(1)
        round_piece(1, 0, nc.scalar.copy)
        quantize_w1(1, 0, 1)
        quantize_w1(1, 1, 2)
        round_piece(0, 1, nc.scalar.copy)
        round_piece(1, 1, nc.vector.tensor_copy)
        quantize_w1(0, 2, 4)
        quantize_w1(1, 2, 3)
        quantize_w1(1, 3, 4)

        embed(0)
        embed(1)
        round_all_planes(0, "w1_q11")
        embed(2)
        embed(3)
        round_all_planes(1)
        w4_bf0 = [sb("w4_bf00", [P, HALF, PACK], BF16)]
        round_w4(w4_bf0[0][:], 0, 0, HALF)
        gather_second_one(0)
        gather_second_one(1)
        diff01 = sb("diff01", [P, 2, PAIRS], F32, "w1_q12")
        diff = {i: diff01[:, i, :] for i in range(2)}
        subtract(0, diff[0])
        subtract(1, diff[1])
        quantize_w1(0, 4, 8)
        scale_and_move(0, "w1_q11")
        scale_and_move(1)
        gather_second(2)
        quantize_w1(1, 4, 6)
        quantize_w1(1, 6, 8)
        for i in (2, 3):
            diff[i] = sb("diff%d" % i, [P, PAIRS], F32)[:]
            subtract(i, diff[i])
        embed(4)
        embed(5)
        scale_and_move(2)
        scale_and_move(3)
        embed(6)
        embed(7)
        w4_bf0.append(sb("w4_bf01", [P, HALF, PACK], BF16))
        round_w4(w4_bf0[1][:], 0, HALF, N)
        weave("0", z_moved[:], PAIRS, nc.scalar.copy)
        w4_bf1 = sb("w4_bf1", [P, N, PACK], BF16)
        round_w4(w4_bf1[:], 1, 0, N)

        gather_second(4)
        diff45 = sb("diff45", [P, 2, PAIRS], F32, "w1_sc_last")
        for e in range(2):
            subtract(4 + e, diff45[:, e, :])
        z_rows = sb("z_rows", [P, PACK, PAIRS], BF16, "second45")
        for e in range(2):
            scale_on_gpsimd(z_rows[:, e, :], diff45[:, e, :], gain_b[:, e : e + 1])
        gather_second(6)
        quantize_z("0", 0, 0, PAIRS)
        for block in range(3):
            product(block, 2, 0, 2 * block)
            product(block, 3, 0, 2 * block + 1)

        def last_tiles(half):
            cols = slice(HALF * half, HALF * (half + 1))
            part = sb("diff67_%d" % half, [P, 2, HALF], F32)
            for e in range(2):
                subtract(6 + e, part[:, e, :], cols.start, cols.stop)
            for e in range(2):
                scale_on_scalar(z_rows[:, 2 + e, cols], part[:, e, :], gain_b[:, 2 + e : 3 + e])

        last_tiles(0)
        weave("10", z_rows[:, :, :HALF], HALF, nc.scalar.copy)
        codes0 = sb("w4_q0", [P, N], U32)
        for u in range(2):
            w4_q[0, u] = codes0[:, HALF * u : HALF * (u + 1)]
            nc.vector.quantize_mx(
                out=w4_q[0, u].bitcast(FP8X4),
                scales=w4_sc[0][:, HALF * u : HALF * (u + 1)],
                in_=w4_bf0[u][:].rearrange("p c j -> p (c j)"),
            )
            product(u, 4, 0, 6 + u)
        last_tiles(1)
        quantize_z("10", 1, 0, HALF)
        quantize_w4("w4_q10", w4_bf1[:, :HALF, :], 1, 0, HALF)
        weave("11", z_rows[:, :, HALF:], HALF, nc.vector.tensor_copy)
        quantize_w4("w4_q11", w4_bf1[:, HALF:, :], 1, HALF, N)
        for block in range(2):
            for which in (2, 3):
                product(block, which, 1)
            copy_y2(block)
        for block in range(2):
            product(block, 4, 1)
        product(3, 2, 0, 0)
        product(3, 3, 0, 2)
        quantize_z("11", 1, HALF, PAIRS)
        for block in (2, 3):
            for which in (2, 3):
                product(block, which, 1)
        y4_sb = sb("y4_sb", [P, BANK], F32)
        nc.scalar.copy(out=y4_sb[:], in_=y[1, 4][:])
        copy_y2(2)
        copy_y2(3)
        multiply(0)
        multiply(1)
        for block in (2, 3):
            product(block, 4, 0, 2 * block - 3)
            product(block, 4, 1)
        add_and_store(0)
        result1 = sb("result1", [P, BANK], F32)
        nc.gpsimd.tensor_tensor(result1[:], y4_sb[:], y23[1][:], ADD)
        store(1, result1, 0, BANK)
        multiply(2)
        multiply(3, slice(0, HALF))
        add_and_store(2)
        multiply(3, slice(HALF, BANK))
        add_and_store(3, 2)
